import numpy as np, ml_dtypes
CORES = [13,21,141,149]
N = 4
BF = ml_dtypes.bfloat16
T, NB, C, RO = 1, 12, 4096, 3
V, W, CN = 8 * N * T, 2 ** NB, C // N
def scores(rng):
    w = rng.choice(np.array([0.0, 0.25, 0.5, 0.75], np.float32), (N, 8, T, 1, 1))
    a = rng.integers(0, 256, (N, 8, T, 1, W)).astype(np.float32); b = rng.integers(0, 256, (N, 8, T, 16, W)).astype(np.float32)
    return np.floor(w * a + (1 - w) * b)
def parents(rng):
    return np.argsort(rng.random((V, V)) + 2 * np.eye(V), axis=1)[:, :NB]
def orders(rng):
    return np.argsort(rng.random((V, C)), axis=0)
def full(rng, cd):
    v = int(rng.integers(0, V)); m = rng.permutation(C) & (W - 1)
    key = 2 * rng.random((V, C)); bit = (m[None, :] >> np.arange(NB)[:, None]) & 1
    key[v] = 1.0; key[cd[v]] = 0.9 * rng.random((NB, C)) + 1.1 * (1 - bit)
    return np.argsort(np.argsort(key, axis=0), axis=0)
def moves(rng):
    return 2 * rng.integers(0, V // 2, (RO, C)) + 1, rng.integers(0, V, (RO, C)), rng.integers(0, 18, (RO, C))
def pack(rng, v, cd, p, fa, ic, t):
    t = np.array(t)
    for k in range(N):
        i = k * CN + rng.permutation(CN)[:2]; t[:, i[0]] = 0; t[:, i[1]] = 17
    same = lambda a: np.repeat(np.asarray(a)[None], N, axis=0).astype(np.int32)
    return {"tab": np.ascontiguousarray(v.transpose(0, 1, 3, 2, 4)).reshape(N, 128, T * W).astype(np.float32).astype(BF),
            "cand": np.ascontiguousarray(np.reshape(cd, (N, 8, T * NB))).astype(np.int32),
            "pos0": same(p), "fac": same(fa), "inc": same(ic), "th": same(t)}
def setup_inputs(rng):
    fa, ic, t = moves(rng)
    t = np.where(rng.random((RO, C)) < 0.7, rng.integers(5, 12, (RO, C)), t)
    return pack(rng, scores(rng), parents(rng), orders(rng), fa, ic, t)
def setup_inputs_ties(rng):
    v = rng.integers(0, 2 + rng.integers(0, 2, (N, 8, T, 1, 1)), (N, 8, T, 16, W))
    fa, ic, t = moves(rng); u = rng.integers(0, 3, (RO, C))
    fa = np.where(u < 2, 1, fa); ic = np.where(u == 0, 0, ic)
    t = np.where(rng.random((RO, C)) < 0.6, rng.choice(np.array([1, 8, 15, 16, 17]), (RO, C)), t)
    o = rng.permutation(V); b = V // 16; cd = np.empty((V, NB), np.int64); p = np.empty((V, C), np.int64)
    j = np.argsort(rng.random((V, 16)) + 2 * np.tile(np.eye(16), (b, 1)), axis=1)[:, :NB]
    cd[o] = o[16 * (np.arange(V) >> 4)[:, None] + j]
    p[o] = (16 * np.argsort(rng.random((b, C)), axis=0)[:, None, :] + np.argsort(rng.random((b, 16, C)), axis=1)).reshape(V, C)
    al = rng.random(C) < 0.5; p = np.where(al[None, :], p, orders(rng))
    fa[0] = np.where(al, 1, fa[0]); ic[0] = np.where(al, 16 * rng.integers(1, b, C), ic[0])
    return pack(rng, v, cd, p, fa, ic, t)
def setup_inputs_ends(rng):
    v = scores(rng); cd = parents(rng); p = orders(rng); fa, ic, t = moves(rng)
    v[..., 0] = 255 * rng.integers(0, 2, v.shape[:-1]); v[..., W - 1] = 255 * rng.integers(0, 2, v.shape[:-1])
    v[:, :, :, 0] = 0; v[:, :, :, 15] = 255
    o = rng.permutation(V); n = V // 8; me = np.arange(V)[:, None]
    cd[o[:n]] = me[o[:n]]; cd[o[n:2 * n]] = cd[o[n:2 * n], :1]; cd[o[2 * n:3 * n]] = rng.choice(np.array([0, V - 1]), (n, NB)); cd[o[3 * n:4 * n], NB - 1] = o[3 * n:4 * n]
    cd[o[3 * n:], 0] = int(rng.integers(0, V))
    u = rng.integers(0, 4, C)[None, :]
    p = np.where(u == 0, me, np.where(u == 1, V - 1 - me, np.where(u == 2, (me + rng.integers(0, V, C)[None, :]) & (V - 1), p)))
    fa = np.where(rng.random((RO, C)) < 0.5, rng.choice(np.array([1, V - 1]), (RO, C)), fa); ic = np.where(rng.random((RO, C)) < 0.5, rng.choice(np.array([0, 1, V - 1]), (RO, C)), ic)
    return pack(rng, v, cd, p, fa, ic, t)
def setup_inputs_lone(rng):
    v = scores(rng); k = int(rng.integers(0, N)); c = 255 * rng.integers(0, 2, N)
    for r in range(N):
        if r != k: v[r] = c[r]
    p = orders(rng)[:, :3][:, rng.integers(0, 3, C)]; fa, ic, t = moves(rng)
    u = rng.integers(0, 2, (RO, C)); fa = np.take_along_axis(fa[:, :2], u, 1); ic = np.take_along_axis(ic[:, :2], u, 1)
    d = pack(rng, v, parents(rng), p, fa, ic, t); h = d["th"]; o = [int(a) * CN for a in rng.permutation(N)]
    for a, i, x in ((o[0], 1, 17), (o[1], 0, 17), (o[1], 1, 0), (o[3], RO - 1, 17)): h[:, i, a:a + CN] = x
    h[:, :, o[2]:o[2] + CN] = np.minimum(h[:, :, o[2]:o[2] + CN], 16)
    return d
def setup_inputs_votes(rng):
    base = rng.permutation(V); cd = np.empty((V, NB), np.int64); pb = np.empty((V, 1), np.int64); pb[base, 0] = np.arange(V)
    for j in range(V): cd[base[j]] = base[np.resize(rng.permutation(max(j, 1)), NB)]
    pop = np.add.reduce((np.arange(W)[None, :] >> np.arange(NB)[:, None]) & 1, axis=0)
    opp = np.concatenate([rng.permutation(12) < 6, rng.permutation(4) < 2])
    a = rng.integers(52, 73, (N, 8, T, 16, 1)); a[:, :, :, ~opp] = 255; a[N - 1] = 255
    up = (np.arange(16) < 12)[:, None] ^ (opp[:, None] & (np.arange(N) < N - 1)[:, None, None, None, None])
    w = (a * pop) // NB; v = (rng.random(a.shape) * (256 - a)).astype(np.int64) + np.where(up, w, a - w)
    u = rng.integers(0, 6, C)[None, :]
    p = np.where(u < 2, pb, np.where(u == 2, V - 1 - pb, np.where(u == 3, (pb + rng.integers(0, V, C)[None, :]) & (V - 1), orders(rng))))
    fa, ic, t = moves(rng); back = rng.random((RO, C)) < 0.6
    fa = np.where(back, V - 1, fa); ic = np.where(back, V - 1, ic)
    t = np.where(rng.random((RO, C)) < 0.7, rng.choice(np.array([4, 5, 12, 13]), (RO, C)), t)
    return pack(rng, v, cd, p, fa, ic, t)
def setup_inputs_spread(rng):
    s = np.exp2(8 * rng.random((N, 8, T, 1, W), dtype=np.float32)) * (rng.random((N, 8, T, 1, W)) > 0.0625)
    v = np.minimum(np.floor(s * rng.random((N, 8, T, 16, W), dtype=np.float32)), 255)
    fa, ic, t = moves(rng); cd = parents(rng)
    return pack(rng, v, cd, full(rng, cd), fa, ic, t)
def check_inputs(d):
    bad = []
    x = np.asarray(d["tab"]).astype(np.float32)
    if not np.all((x >= 0) & (x <= 255) & (x == np.floor(x))): bad.append("whole numbers of tab")
    for k, lo, hi in (("cand", 0, V - 1), ("pos0", 0, V - 1), ("fac", 1, V - 1), ("inc", 0, V - 1), ("th", 0, 17)):
        if np.min(d[k]) < lo or np.max(d[k]) > hi: bad.append("range of " + k)
    if not np.all(np.sort(d["pos0"], axis=1) == np.arange(V)[None, :, None]): bad.append("orders of pos0")
    if not np.all((np.asarray(d["fac"]) & 1) == 1): bad.append("odd numbers of fac")
    for k in ("pos0", "fac", "inc", "th"):
        if np.any(d[k] != d[k][:1]): bad.append("one " + k + " on all ranks")
    return bad
def reference(tab, cand, pos0, fac, inc, th):
    tb = np.ascontiguousarray(tab.astype(np.float32).astype(np.int32).reshape(N, 8, 16, T, W).transpose(0, 1, 3, 2, 4)).reshape(V, 16, W)
    cd = cand.astype(np.int64).reshape(V, NB)
    def score(p):
        before = (p[cd] < p[:, None, :]).astype(np.int64)
        m = np.add.reduce(before << np.arange(NB)[None, :, None], axis=1)
        return np.add.reduce(np.take_along_axis(tb, m[:, None, :], 2).astype(np.int64), axis=0)
    p = pos0[0].astype(np.int64); F = score(p); flags = []
    for k in range(RO):
        q = (fac[0, k].astype(np.int64) * p + inc[0, k]) & (V - 1)
        G = score(q)
        ok = np.add.reduce((G >= F).astype(np.int64), axis=0) >= th[0, k]
        p = np.where(ok, q, p); F = np.where(ok, G, F); flags.append(ok)
    A = np.stack(flags).astype(np.float32)
    return {"yf": np.ascontiguousarray(F.reshape(16, N, CN).transpose(1, 0, 2)).astype(np.float32), "ya": np.ascontiguousarray(A.reshape(RO, N, CN).transpose(1, 0, 2))}

@@ -1,0 +1,620 @@
+from concourse.bass import DstId, RemoteDMATransfer
+from concourse.mybir import AluOpType as Op, ActivationFunctionType as Fn
+
+CHUNKS = [2, 2, 2, 2]
+MODES = ["t2", "t2", "t2", "t2"]
+STAGES = {"t2": [3], "s4": [1, 1]}
+NCH = len(CHUNKS)
+H0 = [sum(CHUNKS[:i]) for i in range(NCH)]
+PAR = {"cyc": 0.00104, "pe": 0.00052, "fix": 0.02, "afix": 0.1, "lat": 0.1, "gat": 1.56, "hop": 3.0, "iss": 0.5, "pos": 4.7,
+       "tab": 9.5, "small": 2.3, "first": 2.0, "look": 0.4, "dg0": 3.0, "dg1": 1.0, "ab": -0.5, "skew": 1.5, "e8": 1}
+BASE = {}
+NU = 0
+for _c in range(NCH):
+    for _s, _e in enumerate(STAGES[MODES[_c]]):
+        BASE[(_c, _s)] = NU
+        NU += CHUNKS[_c] * _e
+
+SCRATCH = {}
+for _t, _l in (
+        ("bfloat16", {"tb": [4096], "fa": [768], "ones": [512], "zz": [608], "qq": [96], "ns": [64], "eq": [128], "ss": [1536],
+                      "ww": [408], "sel": [512], "s16": [16], "pm": [128], "npm": [128], "rm": [96], "x0": [1024],
+                      "y1": [1024], "b0": [6144], "g0": [8192], "b1": [384 * NU], "g1": [512 * NU], "wb": [32 * NU],
+                      "xt": [32 * NU], "pc": [256], "ge": [512], "cn": [512], "wv": [384], "zv": [384]}),
+        ("float16", {"x1": [1024], "s0": [1024], "l0": [768], "s1": [64 * NU], "l1": [48 * NU]}),
+        ("uint16", {"o0": [512], "om": [32 * NU], "ol": [24 * NU]}),
+        ("int32", {"p32": [4, 256], "cs": [4], "cl": [4], "fi": [512], "y32": [96], "pi": [4], "wi": [32 * NU], "wa": [32 * NU]}),
+        ("float32", {"cf": [4], "yfl": [96], "yt": [3, 8, 4], "col": [136], "pf": [8], "onesf": [128], "idf": [128], "nidf": [128],
+                     "cb": [8, 6], "cd": [8, 6], "ct": [8, 6], "cc": [8, 6], "dm": [3, 8, 2], "tmp": [16], "tm": [3, 128],
+                     "ff": [2, 128], "th3": [NCH, 6], "t3": [384], "t2": [2, 128], "ft": [8, 19], "yy": [4, 256]})):
+    for _n in _l:
+        SCRATCH[_n] = ("sbuf", [128] + _l[_n], _t)
+for _i in range(8):
+    SCRATCH["ps%d" % _i] = ("psum", [128, 512], "float32")
+
+SEMAPHORES = ["pe", "dve", "act", "gp", "sent", "ac", "lc", "lp", "lt", "lf", "ly", "st"]
+for _c in range(NCH):
+    SEMAPHORES.append("a0_%d" % _c)
+    for _s in range(len(STAGES[MODES[_c]])):
+        SEMAPHORES += ["m%d_%d_%d" % (_j, _c, _s) for _j in range(3)] + ["a_%d_%d" % (_c, _s)]
+
+POOLS = {"w": [0, 1, 2, 3], "s": [4, 5], "o": [6, 7]}
+FAR = {}
+
+
+def wiring(T, topo):
+    cores = list(T.cores)
+    n = len(cores)
+    slots, relay = [], {}
+    for r in range(n):
+        far = [d for d in range(n) if d != r and not topo.may_write(cores[r], cores[d])]
+        near = [d for d in range(n) if d != r and d not in far]
+        slots.append(far + near + [r])
+        used = []
+        for d in far:
+            c = [k for k in topo.cores_of(cores[r]) if k not in cores and k not in used and topo.may_write(k, cores[d])]
+            c.sort(key=lambda k: topo.die(k) != topo.die(cores[r]))
+            used.append(c[0])
+            relay[(r, d)] = c[0]
+    return cores, slots, relay
+
+
+def messages(T, j):
+    m = {"c": ("ac", T.cl[:, j:j + 1])}
+    for c in range(NCH):
+        n, h = CHUNKS[c], H0[c]
+        m["a0_%d" % c] = ("a0_%d" % c, T.l0[:, 96 * h + 32 * n * j:96 * h + 32 * n * (j + 1)])
+        for s, e in enumerate(STAGES[MODES[c]]):
+            b, q = BASE[(c, s)], n * e
+            m["m_%d_%d" % (c, s)] = ("m%d_%d_%d" % (j, c, s), T.ol[:, 24 * b + 8 * q * j:24 * b + 8 * q * (j + 1)])
+            m["a_%d_%d" % (c, s)] = ("a_%d_%d" % (c, s), T.l1[:, 48 * b + 16 * q * j:48 * b + 16 * q * (j + 1)])
+    return m
+
+
+def bits_of(lst):
+    m = 0
+    for e in lst:
+        m |= 1 << e
+    return m
+
+
+def build(g, T, topo, r, P):
+    cores, slots, relay = wiring(T, topo)
+    me = cores[r]
+    sl = slots[r]
+    ops = []
+    cur = [0]
+    Q = {"pe": g.tensor, "dve": g.vector, "act": g.scalar, "gp": g, "sp": g.sync}
+    V = g.vector
+    R = None
+
+    def add(name, eng, cost, deps, prio, emit, unit=None, kind="c", sem=None, lat=0.0, at=None):
+        if not isinstance(eng, list):
+            eng, cost = [eng], {eng: cost}
+        o = {"name": name, "eng": eng, "cost": cost, "deps": list(deps), "p": prio, "emit": emit, "unit": unit, "kind": kind,
+             "sem": sem, "lat": lat, "at": at, "n": len(ops), "c": cur[0]}
+        if unit is not None:
+            unit["ops"].append(o)
+        ops.append(o)
+        return o
+
+    def unit(pool):
+        return {"pool": pool, "ops": [], "bank": None}
+
+    def ps(u):
+        return T["ps%d" % u["bank"]]
+
+    def vc(n):
+        return P["fix"] + max(64, n) * P["cyc"]
+
+    def dv(name, n, deps, fn, u=None, prio=R):
+        return add(name, "dve", vc(n), deps, prio, lambda e: fn(), unit=u)
+
+    def act(n, deps, out, in_, scale=1.0, u=None, prio=R):
+        return add("ac", "act", P["afix"] + n * P["cyc"], deps, prio,
+                   lambda e: g.scalar.activation(out, in_(), Fn.Identity, scale=scale), unit=u)
+
+    def pe(name, cyc, deps, fn, u, prio=R):
+        return add(name, "pe", 0.05 + cyc * P["pe"], deps, prio, lambda e: mms(fn()), unit=u)
+
+    def gp(n, deps, prio, fn):
+        return add("gp", "gp", 0.17 + 2 * n * P["cyc"], deps, prio, lambda e: fn())
+
+    def dma(eng, deps, prio, out, in_, sem, tot, at=None):
+        return add(sem, eng, 0.05, deps, prio, lambda e: Q[e].dma_start(out, in_).then_inc(T.sem[sem], 16), kind="d",
+                   sem=(sem, tot), lat=2.0, at=at)
+
+    def ts(out, a, s1, s2, o0, o1=None):
+        if o1 is None:
+            return V.tensor_scalar(out, a, s1, None, o0)
+        return V.tensor_scalar(out, a, s1, s2, o0, o1)
+
+    def tt(out, a, b, op):
+        return V.tensor_tensor(out, a, b, op)
+
+    def mms(lst):
+        last = None
+        for (o, l, rr, a, b) in lst:
+            last = g.tensor.matmul(o, l, rr, a, b)
+        return last
+
+    sent = [0]
+
+    def send(key, src, dfar, dnear, prio):
+        def far(e):
+            tr = []
+            for j in (0, 1):
+                k = relay[(r, sl[j])]
+                sem, dst = messages(T, slots[sl[j]].index(r))[key]
+                en = topo.engines(me, k)
+                h = len(en) // 2
+                rid, pid = topo.addr(k, me)
+                tr.append(RemoteDMATransfer(dst_ids=[DstId(rid=rid, pnc=pid)], dma_engine_mask=bits_of(en[j * h:(j + 1) * h]),
+                                            remote_sem=T.sem[sem], src=src(j), dst=dst))
+                sent[0] += h
+            return g.remote_dma_fused(tr, local_sem=T.sem.sent)
+
+        def near(e):
+            k = cores[sl[2]]
+            sem, dst = messages(T, slots[sl[2]].index(r))[key]
+            rid, pid = topo.addr(k, me)
+            sent[0] += len(topo.engines(me, k))
+            return g.remote_dma(dst, src(2), T.sem[sem], T.sem.sent, pid, rid, topo.mask(me, k))
+        a = add("F", "gp", P["iss"], dfar, prio, far, kind="r")
+        a["key"] = key
+        return a, add("N", "gp", P["iss"], dnear, prio + 0.01, near, kind="r")
+
+    def incs(j):
+        return len(topo.engines(cores[sl[j]] if j == 2 else relay[(sl[j], r)], me))
+
+    def arrive(snd, js, sem, extra=0.0):
+        lat = (2 * P["hop"] if min(js) < 2 else P["hop"]) + extra
+        return add("x", "x", 0.0, [snd[0] if min(js) < 2 else snd[1]] + ([snd[1]] if len(js) > 1 else []), 0, None, kind="x",
+                   sem=(sem, sum(incs(j) for j in js)), lat=lat)
+
+    def sel(out, in_, pat, op, base, cm):
+        return lambda: g.affine_select(out, in_, pat, op, 0.0, base, cm)
+
+    lc = dma("sp", [], 0, T.cs[0:96, 0:1], T.cand[:], "lc", 16, at=P["small"])
+    lf = [dma("act", [], 0.5, T.fi[0:16, 0:256], T.fac[0, :], "lf", 32, at=P["small"]),
+          dma("act", [], 0.5, T.fi[0:16, 256:512], T.inc[0, :], "lf", 32, at=P["small"])]
+    lp = []
+    for i in range(16):
+        a, j = i // 4, i % 4
+        c0 = 1024 * sl[j] + 256 * a
+        lp.append(dma("act" if i % 2 and i > 2 else "sp", [], 1, T.p32[32 * a:32 * a + 32, j, :], T.pos0[:, c0:c0 + 256],
+                      "lp", 256, at=P["pos"]))
+    lt = dma("sp", [], 2, T.tb[:], T.tab[:], "lt", 16, at=P["tab"])
+    my = dv("my", 96, [], lambda: V.memset(T.y32[:], 0), prio=0.5)
+    ly = []
+    for tn, src in enumerate((T.fac, T.inc, T.th)):
+        for k in range(3):
+            ly.append(dma("sp", [my], 3, T.y32[k:128:4, 32 * tn:32 * tn + 32], src[k, 1024 * r:1024 * r + 1024], "ly", 144,
+                          at=P["tab"] + 0.5))
+
+    def c_(n, deps, prio, fn):
+        return dv("c", n, deps, fn, prio=prio)
+    mc = c_(1, [], 0, lambda: V.memset(T.cs[96:128, :], 0))
+    m1 = c_(256, [], 0.1, lambda: V.memset(T.ones[:], 1.0))
+    mz = c_(304, [], 1, lambda: V.memset(T.zz[:], 0.0))
+    icol = gp(136, [], 0, lambda: g.iota(T.col[:], [[1, 136]], 0, 0, allow_small_or_imprecise_dtypes=True))
+    ip = gp(1, [], 0.1, lambda: g.iota(T.pi[:, 0:1], [[0, 1]], 0, 1))
+    gq = gp(96, [m1], 1, sel(T.qq[0:96, :], T.ones[0:96, 0:96], [[-4, 3], [-1, 4], [-12, 8]], Op.is_equal, 0, 1))
+    gn1 = gp(56, [m1], 1.2, sel(T.ns[0:96, 0:56], T.ones[0:96, 0:56], [[-12, 56]], Op.is_ge, 288, 1))
+    gns = gp(56, [gn1], 1.2, sel(T.ns[0:96, 0:56], T.ns[0:96, 0:56], [[12, 56]], Op.is_ge, -277, -1))
+    gs1 = gp(512, [m1], 2.5, sel(T.sel[0:32, :], T.ones[0:32, :], [[-1, 16], [0, 32]], Op.is_equal, 0, 1))
+    gpm = gp(128, [m1], 6, sel(T.pm[:], T.ones[:, 0:128], [[-4, 4], [-16, 8], [-1, 4]], Op.is_equal, 0, 1))
+    gnp = act(128, [gpm], T.npm[:], lambda: T.pm[:], -1.0, prio=7)
+    m1f = c_(128, [], 7, lambda: V.memset(T.onesf[:], 1.0))
+    gid = gp(128, [m1f], 7, sel(T.idf[:], T.onesf[:], [[-1, 128]], Op.is_equal, 0, 1))
+    gni = act(128, [gid], T.nidf[:], lambda: T.idf[:], -1.0, prio=7)
+    a31 = c_(1, [ip], 2, lambda: ts(T.pi[:, 1:2], T.pi[:, 0:1], 31, None, Op.bitwise_and))
+    a15 = c_(1, [ip], 2, lambda: ts(T.pi[:, 2:3], T.pi[:, 0:1], 15, None, Op.bitwise_and))
+    c31 = c_(1, [a31], 2, lambda: ts(T.pf[:, 0:1], T.pi[:, 1:2], 4.0, 3.0, Op.mult, Op.add))
+    c15 = c_(1, [a15], 2, lambda: V.tensor_copy(T.pf[:, 1:2], T.pi[:, 2:3]))
+    wq = [c_(1, [], 2, lambda q=q: V.memset(T.pf[32 * q:32 * q + 32, 2:3], 0.5 * 2 ** q)) for q in range(4)]
+    w0 = c_(136, [icol, c31] + wq, 3, lambda: ts(T.ww[:, 0:136], T.col[:], T.pf[:, 0:1], T.pf[:, 2:3], Op.is_equal, Op.mult))
+    wts = [w0] + [act(136, [w0], T.ww[:, 136 * t:136 * t + 136], lambda: T.ww[:, 0:136], 16.0 ** t, prio=3) for t in (1, 2)]
+    ks = c_(16, [icol, c15], 4, lambda: ts(T.s16[:], T.col[:, 0:16], T.pf[:, 1:2], None, Op.is_equal))
+    mfa = c_(128, [], 1, lambda: V.memset(T.fa[0:32, 512:768], -6144.0))
+    r1 = c_(48, [], 5, lambda: V.memset(T.rm[:], 1.0))
+    r16 = c_(6, [r1], 5, lambda: V.memset(T.rm[:, 0:96:16], 0.0))
+    mzv = c_(192, [], 6, lambda: V.memset(T.zv[:], 0.0))
+
+    sc = send("c", lambda j: T.cs[:, 0:1], [lc, mc], [lc, mc], 3)
+    ac = arrive(sc, [0, 1, 2], "ac", P["first"])
+    cfo = c_(1, [lc], 1.5, lambda: V.tensor_copy(T.cf[0:96, 3:4], T.cs[0:96, 0:1]))
+    cfr = c_(3, [ac], R, lambda: V.tensor_copy(T.cf[0:96, 0:3], T.cl[0:96, 0:3]))
+    S = []
+    for j in range(4):
+        pr = 1.6 if j == 3 else R
+        b = 96 + 128 * j
+        e = c_(32, [cfo if j == 3 else cfr, icol], pr,
+               lambda j=j: ts(T.eq[0:96, 32 * j:32 * j + 32], T.col[0:96, 0:32], T.cf[0:96, j:j + 1], None, Op.is_equal))
+        e = c_(64, [e, gns, mz], pr, lambda j=j, b=b: tt(T.zz[0:96, b:b + 32], T.eq[0:96, 32 * j:32 * j + 32],
+                                                        T.ns[0:96, 24 - 8 * sl[j]:56 - 8 * sl[j]], Op.subtract))
+        u = unit("w")
+        m = pe("sm", 400, [e, gq], lambda u=u, b=b: [
+            (ps(u)[:, a:384:4], T.zz[0:96, b - 32 * a:b - 32 * a + 128], T.qq[0:96, :], True, True) for a in range(4)], u, pr)
+        S.append(act(384, [m], T.ss[:, 384 * j:384 * j + 384], lambda u=u: ps(u)[:, 0:384], u=u, prio=pr))
+
+    def st(j, t):
+        return T.ss[:, 384 * j + 128 * t:384 * j + 128 * t + 128]
+
+    ca = c_(256, lf, 4.5, lambda: V.tensor_copy(T.fa[0:16, 0:256], T.fi[0:16, 0:256]))
+    cbb = c_(256, lf, 4.5, lambda: ts(T.fa[0:16, 256:512], T.fi[0:16, 256:512], -1.0, 15.5, Op.mult, Op.add))
+    yc = dv("yc", 96, ly, lambda: V.tensor_copy(T.yfl[:], T.y32[:]))
+    yt = dv("yt", 96, [yc], lambda: V.transpose(T.yt[:], T.yfl[:]))
+    k0 = dv("k", 16, [yt], lambda: V.tensor_copy(T.cb[:, :, 0:2], T.yt[:, 0, :, 1:3]))
+    k3 = dv("k", 16, [yt], lambda: V.tensor_copy(T.cb[:, :, 3:5], T.yt[:, 1, :, 1:3]))
+    k2 = dv("k", 8, [yt], lambda: tt(T.cb[:, :, 2], T.yt[:, 0, :, 1], T.yt[:, 0, :, 2], Op.mult))
+    k5a = dv("k", 8, [yt], lambda: tt(T.tmp[:, 0:8], T.yt[:, 0, :, 2], T.yt[:, 1, :, 1], Op.mult))
+    kf = dv("k", 8, [yt], lambda: ts(T.tmp[:, 8:16], T.yt[:, 0, :, 0], -1.0, None, Op.add))
+    k5 = dv("k", 8, [k5a], lambda: tt(T.cb[:, :, 5], T.tmp[:, 0:8], T.yt[:, 1, :, 2], Op.add))
+    kd = []
+    for j, kj in enumerate((k0, k0, k2)):
+        kd.append(dv("k", 8, [kj, kf], lambda j=j: tt(T.cd[:, :, j], T.cb[:, :, j], T.tmp[:, 8:16], Op.mult)))
+        kd.append(dv("k", 8, [kj], lambda j=j: tt(T.cd[:, :, 3 + j], T.cb[:, :, j], T.yt[:, 1, :, 0], Op.mult)))
+    kb = [k0, k2, k3, k5]
+    if len(set(CHUNKS)) == 1:
+        kt = [dv("kt", 8, [yt], lambda j=j, n=CHUNKS[0]: V.tensor_copy(T.th3[:, :, j * n:(j + 1) * n], T.yt[:, 2, :, min(j + 1, 2)]))
+              for j in range(3)]
+    else:
+        kt = [dv("kt", 8, [yt], lambda j=j, c=c, n=CHUNKS[c], h=H0[c]: V.tensor_copy(
+            T.th3[:, c, j * n:(j + 1) * n], T.yt[:, 2, h:h + n, min(j + 1, 2)])) for j in range(3) for c in range(NCH)]
+
+    def masks(w, diff, dcyc, ddeps, bits, ba, out):
+        cm = []
+        for t in range(3):
+            u = unit("w")
+            d = pe("md", dcyc, ddeps, lambda u=u, t=t: diff(ps(u), t), u)
+
+            def em(e, u=u, t=t):
+                o = bits[:, ba + w * t:ba + w * (t + 1)]
+                if e == "act":
+                    return g.scalar.activation(o, ps(u)[:, 0:w], Fn.Sign, bias=-0.5, scale=-1.0)
+                return ts(o, ps(u)[:, 0:w], 0.0, 2.0, Op.is_lt, Op.mult)
+            cm.append(add("mb", ["dve", "act"], {"dve": vc(w), "act": P["afix"] + w * P["cyc"]}, [d], R, em, unit=u))
+        u = unit("w")
+        m = pe("mm", 12 * max(64, w // 4), cm + wts, lambda: [
+            (ps(u)[:, 0:w // 4], T.ww[:, 136 * t + 3 - s:136 * t + 131 - s], bits[:, ba + w * t + s:ba + w * (t + 1):4],
+             t == 0 and s == 0, t == 2 and s == 3) for t in range(3) for s in range(4)], u)
+        return dv("mc", w // 4, [m], lambda: ts(
+            out, ps(u)[:, 0:w // 4], sum(7.5 * 16 ** t for t in range(3) if cm[t]["on"] == "act") + 0.0, None, Op.add), u)
+
+    def gather(name, off, k, out, deps):
+        def em(e):
+            src = T.tb[:, 0:4096].indirect(off)
+            if e == "act":
+                return g.scalar.activation(out, src, Fn.Copy)
+            return V.tensor_copy(out, src)
+        c = 16 * k * P["gat"] * P["cyc"]
+        return add(name, ["act", "dve"], {"act": 0.08 + c, "dve": 0.06 + c}, deps + [lt], R, em)
+
+    def owner_stage(c, s, coef, deps):
+        n, h, ne = CHUNKS[c], H0[c], STAGES[MODES[c]][s]
+        b, q = BASE[(c, s)], n * ne
+        af = [dv("af", 32, deps, lambda k=k, ev=ev: ts(
+            T.wi[:, 32 * (b + k * ne + ev):32 * (b + k * ne + ev + 1)], T.pc[:, 32 * (h + k):32 * (h + k + 1)],
+            coef(h + k, ev)[0], coef(h + k, ev)[1], Op.mult, Op.add)) for k in range(n) for ev in range(ne)]
+        xa, xb = 32 * b, 32 * (b + q)
+        e7 = dv("d7", 32 * q, af, lambda: ts(T.wa[:, xa:xb], T.wi[:, xa:xb], 31, None, Op.bitwise_and))
+        e8 = dv("d8", 32 * q, [e7], lambda: V.tensor_copy(T.wb[:, xa:xb], T.wa[:, xa:xb]))
+        e9 = dv("d9", 16 * q, [e8], lambda: V.transpose(T.xt[:, xa:xb], T.wb[:, xa:xb]))
+        mo = {}
+        for js in ([[0, 1, 2, 3]] if q <= 4 else [[0, 1], [2, 3]]):
+            o = masks(32 * q * len(js), lambda p, t, js=js: [
+                (p[:, 32 * q * i:32 * q * (i + 1)], st(j, t), T.xt[:, xa:xb], True, True) for i, j in enumerate(js)],
+                len(js) * max(64, 32 * q), [e9] + [S[j] for j in js], T.b1, 384 * b + 96 * q * js[0],
+                T.om[:, 32 * b + 8 * q * js[0]:32 * b + 8 * q * (js[-1] + 1)])
+            for j in js:
+                mo[j] = o
+        sm_ = send("m_%d_%d" % (c, s), lambda j: T.om[:, 32 * b + 8 * q * j:32 * b + 8 * q * (j + 1)], [mo[0]], [mo[2]], 19)
+        cvs = {}
+        for js in ([[0, 1, 2, 3]] if q <= 2 else [[0, 1], [2, 3]]):
+            u = unit("s")
+            sm = []
+            for gs in ([[0, 1], [2], [3]] if q <= 2 else [[j] for j in js]):
+                j, nj = gs[0], len(gs)
+                if j == 3:
+                    off, dep = T.om[:, 32 * b + 24 * q:32 * b + 32 * q], [mo[3]]
+                else:
+                    off = T.ol[:, 24 * b + 8 * q * j:24 * b + 8 * q * (j + nj)]
+                    dep = [arrive(sm_, [i], "m%d_%d_%d" % (i, c, s)) for i in gs]
+                g1 = 512 * b + 128 * q * j
+                ga = gather("g1", off, 8 * q * nj, T.g1[:, g1:g1 + 128 * q * nj], dep)
+
+                def su(u=u, gs=gs, j0=js[0]):
+                    lst = []
+                    for j in gs:
+                        for k in range(n):
+                            for ev in range(ne):
+                                o = 16 * (q * (j - j0) + ev * n + k)
+                                i = 512 * b + 128 * (q * j + k * ne + ev)
+                                lst.append((ps(u)[:, o:o + 16], T.g1[:, i:i + 128], T.s16[:], True, True))
+                    return lst
+                sm.append(pe("su", 64 * q * nj, [ga, ks], su, u))
+            s1, w = 64 * b + 16 * q * js[0], 16 * q * len(js)
+            o = dv("sc", w, sm, lambda u=u, s1=s1, w=w: V.tensor_copy(T.s1[:, s1:s1 + w], ps(u)[:, 0:w]), u)
+            for j in js:
+                cvs[j] = o
+        sn = send("a_%d_%d" % (c, s), lambda j: T.s1[:, 64 * b + 16 * q * j:64 * b + 16 * q * (j + 1)], [cvs[0]], [cvs[2]], 20)
+        a1 = arrive(sn, [0, 1, 2], "a_%d_%d" % (c, s))
+
+        def src(j, a, e):
+            x, o = (T.s1, 64 * b + 48 * q) if j == 3 else (T.l1, 48 * b + 16 * q * j)
+            return x[:, o + 16 * n * a:o + 16 * n * e]
+        return src, [a1, cvs[3]]
+
+    J = (3, 0, 1, 2)
+
+    def count(u, o, a, w, out, th, deps):
+        e1 = dv("ge", w, deps[:1], lambda: ts(T.ge[:, a:a + w], ps(u)[:, o:o + w], 0.0, None, Op.is_ge), u)
+        e2 = dv("cn", w // 2, [e1, r16], lambda: V.tensor_tensor_scan(T.cn[:, a:a + w], T.rm[:, 0:w], T.ge[:, a:a + w], 0.0,
+                                                                     Op.mult, Op.add))
+        return dv("wv", w // 8, [e2] + deps[1:], lambda: tt(out, T.cn[:, a + 15:a + w:16], th, Op.is_ge))
+
+    def flag(k, rnd):
+        return T.ft[:, k, 16 + rnd:17 + rnd]
+
+    def decide1(c, rnd, src, deps, fprev, fout):
+        n, h = CHUNKS[c], H0[c]
+        w = 16 * n
+        u = unit("o")
+        if fprev is None:
+            to = pe("to", 768, deps + [gpm, gnp], lambda: (
+                [(ps(u)[:, w:2 * w], T.pm[:], src(j, 1, 2), j == 3, False) for j in J] +
+                [(ps(u)[:, w:2 * w], T.npm[:], src(j, 0, 1), False, j == 2) for j in J] +
+                [(ps(u)[:, 0:w], T.pm[:], src(j, 0, 1), j == 3, j == 2) for j in J]), u)
+        else:
+            to = pe("to", 512, deps + [gpm, gni], lambda: (
+                [(ps(u)[:, w:2 * w], T.nidf[:], fprev, True, False)] +
+                [(ps(u)[:, w:2 * w], T.pm[:], src(j, 0, 1), False, j == 2) for j in J]), u)
+        a = count(u, w, 64 * h + w * rnd, w, T.ft[:, h:h + n, 16 + rnd], T.yt[:, 2, h:h + n, rnd], [to, yt])
+        f1 = [dv("f1", 16, [a], lambda k=k: ts(T.tm[:, rnd, 16 * (h + k):16 * (h + k + 1)], ps(u)[:, w + 16 * k:w + 16 * k + 16],
+                                               flag(h + k, rnd), None, Op.mult), u) for k in range(n)]
+        tm = T.tm[:, rnd, 16 * h:16 * (h + n)]
+        if fprev is None:
+            return a, [dv("f2", w, f1, lambda: tt(fout, ps(u)[:, 0:w], tm, Op.add), u)]
+        if fout is not None:
+            return a, [dv("f2", 2 * w, f1, lambda: tt(fout, fprev, tm, Op.add))]
+        return a, [dv("f2", 32, [f1[k]], lambda k=k: tt(T.ft[:, h + k, 0:16], T.ff[:, 1, 16 * (h + k):16 * (h + k + 1)],
+                                                       T.tm[:, rnd, 16 * (h + k):16 * (h + k + 1)], Op.add)) for k in range(n)]
+
+    def decide2(c, src, deps, fprev):
+        n, h = CHUNKS[c], H0[c]
+        w = 16 * n
+        o = 48 * h
+        u = unit("o")
+        to = pe("to", 1150, deps + [gpm, gnp, gni], lambda: (
+            [(ps(u)[:, 0:3 * w], T.pm[:], src(j, 0, 3), j == 3, False) for j in J] +
+            [(ps(u)[:, i * w:(i + 1) * w], T.nidf[:], fprev, False, False) for i in range(2)] +
+            [(ps(u)[:, 2 * w:3 * w], T.npm[:], src(j, 0, 1), False, j == 2) for j in J]), u)
+        a = count(u, 0, 64 * h + w, 3 * w, T.zv[:, o:o + 3 * w:16], T.th3[:, c, 0:3 * n], [to, mzv] + kt)
+
+        def z(k):
+            return T.zv[:, o + k * w:o + (k + 1) * w:16]
+        zu = dv("u", n, [a], lambda: tt(z(1), z(1), z(0), Op.is_gt))
+        zv = dv("v", n, [a], lambda: tt(z(2), z(2), z(0), Op.mult))
+        z4 = dv("bw", 3 * w // 2, [zu, zv], lambda: V.tensor_tensor_scan(T.wv[:, o:o + 3 * w], T.rm[:, 0:3 * w], T.zv[:, o:o + 3 * w],
+                                                                        0.0, Op.mult, Op.add))
+        z5 = dv("t3", 3 * w, [z4], lambda: tt(T.t3[:, o:o + 3 * w], ps(u)[:, 0:3 * w], T.wv[:, o:o + 3 * w], Op.mult), u)
+        z6 = dv("ta", 2 * w, [z5], lambda: tt(T.t2[:, 0, 16 * h:16 * (h + n)], T.t3[:, o:o + w], T.t3[:, o + w:o + 2 * w], Op.add))
+        z7 = dv("tb", 2 * w, [z5], lambda: tt(T.t2[:, 1, 16 * h:16 * (h + n)], T.t3[:, o + 2 * w:o + 3 * w], fprev, Op.add))
+        return [dv("tc", 32, [z6, z7], lambda k=k: tt(T.ft[:, k, 0:16], T.t2[:, 0, 16 * k:16 * k + 16], T.t2[:, 1, 16 * k:16 * k + 16],
+                                                     Op.add)) for k in range(h, h + n)] + [
+            dv("fl", n, [a], lambda: V.tensor_copy(T.ft[:, h:h + n, 17], z(0))),
+            dv("fl", n, [zu, zv], lambda: tt(T.ft[:, h:h + n, 18], z(1), z(2), Op.add))]
+
+    fin = []
+    prev = []
+
+    def chunk(c):
+        n, h, mode = CHUNKS[c], H0[c], MODES[c]
+        w, xa = 128 * n, 128 * h
+        cv = dv("cv", w, lp, lambda: V.tensor_copy(T.x0[:, xa:xa + w], T.p32[:, :, 32 * h:32 * (h + n)]))
+        ub = unit("o")
+        bc = pe("bc", 8 * max(64, 32 * n) + w, [ca, cbb, gs1, mfa, m1] + prev[-1:], lambda: [
+            (ps(ub)[:, 32 * n * j:32 * n * (j + 1)], T.sel[0:16, 128 * sl[j]:128 * sl[j] + 128],
+             T.fa[0:16, 32 * h:32 * (h + n)], True, True) for j in range(4)] +
+            [(ps(ub)[:, 256:256 + w], T.ones[0:1, 0:128], T.fa[0:1, 512:512 + w], True, False)] + [
+            (ps(ub)[:, 256 + 32 * n * j:256 + 32 * n * (j + 1)], T.sel[0:16, 128 * sl[j]:128 * sl[j] + 128],
+             T.fa[0:16, 256 + 32 * h:256 + 32 * (h + n)], False, j == 3) for j in range(4)], ub)
+        xx = dv("x", w, [bc, cv], lambda: tt(T.x1[:, xa:xa + w], ps(ub)[:, 0:w], T.x0[:, xa:xa + w], Op.mult), ub)
+        yy = dv("y", w, [xx], lambda: tt(T.y1[:, xa:xa + w], ps(ub)[:, 256:256 + w], T.x1[:, xa:xa + w], Op.subtract), ub)
+        prev.append(xx)
+        oa, sa = 64 * h, 128 * h
+        mk = masks(2 * w, lambda p, t: [(p[:, 0:w], st(3, t), T.x0[:, xa:xa + w], True, True),
+                                        (p[:, w:2 * w], st(3, t), T.x1[:, xa:xa + w], True, False),
+                                        (p[:, w:2 * w], st(3, t), T.y1[:, xa:xa + w], False, True)],
+                   3 * w, [yy, S[3]], T.b0, 768 * h, T.o0[:, oa:oa + 64 * n])
+        cvs = []
+        for hf in range(2):
+            u = unit("s")
+            sm = []
+            for ev in range(2):
+                o1 = oa + 32 * n * ev + 16 * n * hf
+                ga = gather("g0", T.o0[:, o1:o1 + 16 * n], 16 * n, T.g0[:, 16 * o1:16 * o1 + 256 * n], [mk])
+                sm.append(pe("su", 128 * n, [ga, ks], lambda u=u, o1=o1, ev=ev: [
+                    (ps(u)[:, 32 * n * jj + 16 * n * ev + 16 * k:32 * n * jj + 16 * n * ev + 16 * k + 16],
+                     T.g0[:, 16 * o1 + 128 * (n * jj + k):16 * o1 + 128 * (n * jj + k + 1)], T.s16[:], True, True)
+                    for jj in range(2) for k in range(n)], u))
+            s1 = sa + 64 * n * hf
+            cvs.append(dv("sc", 64 * n, sm, lambda u=u, s1=s1: V.tensor_copy(T.s0[:, s1:s1 + 64 * n], ps(u)[:, 0:64 * n]), u))
+        sn = send("a0_%d" % c, lambda j: T.s0[:, sa + 32 * n * j:sa + 32 * n * (j + 1)], [cvs[0]], [cvs[1]], 20)
+        d0 = [arrive(sn, [0, 1, 2], "a0_%d" % c), cvs[1]]
+
+        def src0(j, a, e):
+            x, o = (T.s0, sa + 96 * n) if j == 3 else (T.l0, 96 * h + 32 * n * j)
+            return x[:, o + 16 * n * a:o + 16 * n * e]
+        pt = dv("pt", 16 * n, [cv], lambda: V.transpose(T.pc[:, 32 * h:32 * (h + n)], T.x0[:, xa + 96 * n:xa + 128 * n]))
+
+        def ff(i):
+            return T.ff[:, i, 16 * h:16 * (h + n)]
+        hs = slice(h, h + n)
+        a, f = decide1(c, 0, src0, d0, None, ff(0))
+        e4 = [dv("d4", 6, [a] + kd, lambda k=k: ts(T.ct[:, k, :], T.cd[:, k, :], flag(k, 0), None, Op.mult)) for k in range(h, h + n)]
+        e5 = dv("d5", 12 * n, e4 + kb, lambda: tt(T.cc[:, hs, :], T.ct[:, hs, :], T.cb[:, hs, :], Op.add))
+        src, d1 = owner_stage(c, 0, lambda k, ev: (T.cc[:, k, ev:ev + 1], T.cc[:, k, 3 + ev:4 + ev]), [e5, pt])
+        if mode == "t2":
+            done = decide2(c, src, d1 + f, ff(0))
+        else:
+            dl = dv("dl", 4 * n, [e5], lambda: tt(T.dm[:, 0, hs, :], T.cc[:, hs, 2:6:3], T.cc[:, hs, 1:6:3], Op.subtract))
+            a, f = decide1(c, 1, src, d1 + f, ff(0), ff(1))
+            e4 = [dv("d4", 2, [a, dl], lambda k=k: ts(T.dm[:, 1, k, :], T.dm[:, 0, k, :], flag(k, 1), None, Op.mult))
+                  for k in range(h, h + n)]
+            e6 = dv("d5", 4 * n, e4, lambda: tt(T.dm[:, 2, hs, :], T.dm[:, 1, hs, :], T.cc[:, hs, 1:6:3], Op.add))
+            sr2, d2 = owner_stage(c, 1, lambda k, ev: (T.dm[:, 2, k, 0:1], T.dm[:, 2, k, 1:2]), [e6])
+            a, done = decide1(c, 2, sr2, d2 + f, ff(1), None)
+        u = unit("o")
+        z7 = pe("tr", 512 * n, done + [gid], lambda: [
+            (ps(u)[0:19, 128 * k:128 * k + 128], T.ft[:, h + k, :], T.idf[:], True, True) for k in range(n)], u)
+        for k in range(n):
+            o, i = T.yy[0:19, :, 32 * (h + k):32 * (h + k + 1)], slice(128 * k, 128 * k + 128)
+            if P["e8"] and c < NCH - 1:
+                fin.append(act(128, [z7], o, lambda i=i: ps(u)[0:19, i], u=u))
+            else:
+                fin.append(dv("e8", 128, [z7], lambda o=o, i=i: V.tensor_copy(o, ps(u)[0:19, i]), u))
+
+    for c in range(NCH):
+        cur[0] = c
+        chunk(c)
+    dma("sp", fin, 90, T.yf[:], T.yy[0:16, :, :], "st", 32)
+    dma("act", fin, 9000, T.ya[:], T.yy[16:19, :, :], "st", 32)
+    return ops, Q, sent
+
+
+def lay_out(ops, P):
+    free = {e: 0.0 for e in ("pe", "dve", "act", "gp", "sp")}
+    order = {e: [] for e in free}
+    holder = [None] * 8
+    left = list(ops)
+    for o in ops:
+        o["end"], o["bdeps"], o["up"] = None, [], 0.0
+    for o in reversed(ops):
+        o["up"] += min(o["cost"].values()) + o["lat"] + P["lat"]
+        for d in o["deps"]:
+            d["up"] = max(d["up"], o["up"])
+        if o["p"] is None:
+            v = 1000.0 - o["up"] + P["skew"] * o["c"]
+            ga = o["name"] in ("g0", "g1")
+            o["prio"] = {e: v + (P["d" + o["name"]] if ga and e == "dve" else P["ab"] if e == "act" and not ga else 0.0)
+                         for e in o["eng"]}
+        else:
+            o["prio"] = {e: o["p"] for e in o["eng"]}
+    t = 0.0
+    marks = []
+    while left:
+        did = False
+        for o in [o for o in left if o["kind"] == "x" and all(d["end"] is not None for d in o["deps"])]:
+            o["end"] = max(d["end"] for d in o["deps"]) + o["lat"]
+            o["on"] = "x"
+            marks.append(o["end"] + P["lat"])
+            left.remove(o)
+        ready, soon = [], []
+        for o in left:
+            if o["kind"] != "x" and all(d["end"] is not None for d in o["deps"]):
+                y = max([d["end"] + P["lat"] for d in o["deps"]] + [0.0])
+                if y <= t + 1e-9:
+                    ready.append(o)
+                elif o["kind"] == "c":
+                    soon.append((o, y))
+                    if o["eng"] == ["pe"]:
+                        soon += [(x, y + o["cost"]["pe"] + P["lat"]) for x in o["unit"]["ops"] if len(x["deps"]) == 1 and x["deps"][0] is o]
+        for e in ("gp", "sp", "pe", "dve", "act"):
+            if free[e] > t + 1e-9:
+                continue
+            best, bank = None, None
+            for o in ready:
+                if o["end"] is not None or e not in o["eng"] or (best is not None and o["prio"][e] >= best["prio"][e]):
+                    continue
+                b = None
+                u = o["unit"]
+                if u is not None and u["bank"] is None:
+                    for k in POOLS[u["pool"]]:
+                        hu = holder[k]
+                        if hu is None or all(x["end"] is not None and x["end"] + P["lat"] <= t + 1e-9 for x in hu["ops"]):
+                            b = k
+                            break
+                    if b is None:
+                        continue
+                best, bank = o, b
+            if best is None:
+                continue
+            o = best
+            if e in ("dve", "act") and any(e in x["eng"] and x["prio"][e] < o["prio"][e] and y < t + P["look"] * o["cost"][e]
+                                           and (len(x["eng"]) == 1 or e == "act") for x, y in soon):
+                continue
+            if bank is not None:
+                if holder[bank] is not None:
+                    o["bdeps"] = list(holder[bank]["ops"])
+                holder[bank] = o["unit"]
+                o["unit"]["bank"] = bank
+            o["on"] = e
+            o["start"] = t
+            free[e] = t + o["cost"][e]
+            o["end"] = free[e] + o["lat"]
+            if o["at"] is not None:
+                o["end"] = max(o["at"], free[e] + 1.5)
+            order[e].append(o)
+            marks.extend([free[e], o["end"] + P["lat"]])
+            left.remove(o)
+            did = True
+        if not did:
+            t = min([y for y in marks if y > t + 1e-9] + [t + 1.0])
+    FAR["order"] = [o["key"] for o in order["gp"] if "key" in o]
+    return order
+
+
+def emit_all(g, T, Q, order, sent):
+    for e in order:
+        k = 0
+        for o in order[e]:
+            if o["kind"] == "c":
+                k += 1
+                o["sem"] = (e, k)
+    allo = sorted([o for e in order for o in order[e]], key=lambda o: (o["start"], o["n"]))
+    seen = {e: {} for e in order}
+    top = {}
+    for o in allo:
+        e = o["on"]
+        need = {}
+        for d in o["deps"] + [d for d in o["bdeps"] if d["on"] != e]:
+            s, v = d["sem"]
+            need[s] = max(need.get(s, 0), v)
+        for s in need:
+            if seen[e].get(s, 0) < need[s]:
+                Q[e].wait_ge(T.sem[s], need[s])
+                seen[e][s] = need[s]
+        ins = o["emit"](e)
+        if o["kind"] == "c":
+            ins.then_inc(T.sem[e], 1)
+        if o["sem"] is not None:
+            top[o["sem"][0]] = max(top.get(o["sem"][0], 0), o["sem"][1])
+    top["sent"] = sent[0]
+    for s in top:
+        g.wait_ge(T.sem[s], top[s])
+
+
+def rank_program(g, core, T, topo):
+    r = T.rank_of(core)
+    if r is not None:
+        ops, Q, sent = build(g, T, topo, r, PAR)
+        emit_all(g, T, Q, lay_out(ops, PAR), sent)
+        return
+    cores, slots, relay = wiring(T, topo)
+    for (s, d), k in relay.items():
+        if k != core:
+            continue
+        if "order" not in FAR:
+            lay_out(build(g, T, topo, s, PAR)[0], PAR)
+        msg = messages(T, slots[d].index(s))
+        got = len(topo.engines(cores[s], core)) // 2
+        rid, pid = topo.addr(cores[d], core)
+        tot = 0
+        for key in FAR["order"]:
+            sem, ap = msg[key]
+            g.wait_ge(T.sem[sem], got)
+            g.remote_dma(ap, ap, T.sem[sem], T.sem.sent, pid, rid, topo.mask(core, cores[d]))
+            tot += len(topo.engines(core, cores[d]))
+        g.wait_ge(T.sem.sent, tot)

@@ -1,32 +1,26 @@
 from concourse.bass import DstId, RemoteDMATransfer
 from concourse.mybir import AluOpType as Op, ActivationFunctionType as Fn
 
-CHUNKS = [2, 2, 2, 2]
-MODES = ["t2", "t2", "t2", "t2"]
-STAGES = {"t2": [3], "s4": [1, 1]}
-NCH = len(CHUNKS)
-H0 = [sum(CHUNKS[:i]) for i in range(NCH)]
-PAR = {"cyc": 0.00104, "pe": 0.00052, "fix": 0.02, "afix": 0.1, "lat": 0.1, "gat": 1.56, "hop": 3.0, "iss": 0.5, "pos": 4.7,
-       "tab": 9.5, "small": 2.3, "first": 2.0, "look": 0.4, "dg0": 3.0, "dg1": 1.0, "ab": -0.5, "skew": 1.5, "e8": 1}
-BASE = {}
-NU = 0
-for _c in range(NCH):
-    for _s, _e in enumerate(STAGES[MODES[_c]]):
-        BASE[(_c, _s)] = NU
-        NU += CHUNKS[_c] * _e
+NCH = 4
+PAR = {"cyc": 0.00095, "pe": 0.00048, "afix": 0.07, "lat": 0.15, "gat": 1.56, "hop": 2.0, "iss": 0.5, "pos": 4.0,
+       "tab": 8.5, "small": 2.0, "first": 3.0, "look": 0.2, "dg0": 0.0, "dg1": 0.0, "ab": -0.5, "skew": 2.0}
+BIG = 1.5 * 2 ** 23
+LEFT = 3.0 * 2 ** 22 - 54
 
 SCRATCH = {}
 for _t, _l in (
-        ("bfloat16", {"tb": [4096], "fa": [768], "ones": [512], "zz": [608], "qq": [96], "ns": [64], "eq": [128], "ss": [1536],
-                      "ww": [408], "sel": [512], "s16": [16], "pm": [128], "npm": [128], "rm": [96], "x0": [1024],
-                      "y1": [1024], "b0": [6144], "g0": [8192], "b1": [384 * NU], "g1": [512 * NU], "wb": [32 * NU],
-                      "xt": [32 * NU], "pc": [256], "ge": [512], "cn": [512], "wv": [384], "zv": [384]}),
-        ("float16", {"x1": [1024], "s0": [1024], "l0": [768], "s1": [64 * NU], "l1": [48 * NU]}),
-        ("uint16", {"o0": [512], "om": [32 * NU], "ol": [24 * NU]}),
-        ("int32", {"p32": [4, 256], "cs": [4], "cl": [4], "fi": [512], "y32": [96], "pi": [4], "wi": [32 * NU], "wa": [32 * NU]}),
-        ("float32", {"cf": [4], "yfl": [96], "yt": [3, 8, 4], "col": [136], "pf": [8], "onesf": [128], "idf": [128], "nidf": [128],
-                     "cb": [8, 6], "cd": [8, 6], "ct": [8, 6], "cc": [8, 6], "dm": [3, 8, 2], "tmp": [16], "tm": [3, 128],
-                     "ff": [2, 128], "th3": [NCH, 6], "t3": [384], "t2": [2, 128], "ft": [8, 19], "yy": [4, 256]})):
+        ("bfloat16", {"tb": [4096], "fa": [8, 64], "ones": [768], "zz": [528], "wk": [96], "qq": [96], "ns": [64], "eq": [128],
+                      "ss": [1536], "ww": [144], "sel": [768], "fb": [4, 64], "s8": [384], "s16": [16], "pm": [128], "npm": [128],
+                      "cm": [512], "kc": [512],
+                      "al": [384], "tf0": [128], "tf1": [4, 192], "xq": [4, 512], "b0": [4, 512], "g0": [4, 2048],
+                      "b1": [4, 768], "g1": [4, 3072], "xt": [4, 192], "dl": [4, 64], "cu": [4, 128], "ge0": [4, 32],
+                      "ge1": [4, 96], "ze": [4, 192]}),
+        ("float16", {"s0": [4, 256], "l0": [4, 192], "s1": [4, 384], "l1": [4, 288], "m0": [4, 256]}),
+        ("uint16", {"o0": [4, 128], "om": [4, 192], "ol": [4, 144]}),
+        ("int32", {"p32": [8, 128], "cs": [4], "cl": [4], "fi": [512], "fj": [640], "pi": [8], "xi": [4, 256], "xa": [4, 256],
+                   "mi": [4, 192], "yi": [4, 192], "yb": [4, 192]}),
+        ("float32", {"cf": [8], "col": [144], "pf": [8], "mk": [4], "r0": [4, 96], "xx": [4, 128], "zm": [4, 192],
+                     "om1": [4, 192], "oe1": [4, 192], "yy": [128], "ye": [128]})):
     for _n in _l:
         SCRATCH[_n] = ("sbuf", [128] + _l[_n], _t)
 for _i in range(8):
@@ -34,11 +28,9 @@ for _i in range(8):
 
 SEMAPHORES = ["pe", "dve", "act", "gp", "sent", "ac", "lc", "lp", "lt", "lf", "ly", "st"]
 for _c in range(NCH):
-    SEMAPHORES.append("a0_%d" % _c)
-    for _s in range(len(STAGES[MODES[_c]])):
-        SEMAPHORES += ["m%d_%d_%d" % (_j, _c, _s) for _j in range(3)] + ["a_%d_%d" % (_c, _s)]
+    SEMAPHORES += ["a0_%d" % _c, "a1_%d" % _c] + ["m%d_%d" % (_j, _c) for _j in range(3)]
 
-POOLS = {"w": [0, 1, 2, 3], "s": [4, 5], "o": [6, 7]}
+POOLS = {"w": [0, 1, 2], "s": [3, 4], "o": [5, 6, 7]}
 FAR = {}
 
 
@@ -62,12 +54,9 @@ def wiring(T, topo):
 def messages(T, j):
     m = {"c": ("ac", T.cl[:, j:j + 1])}
     for c in range(NCH):
-        n, h = CHUNKS[c], H0[c]
-        m["a0_%d" % c] = ("a0_%d" % c, T.l0[:, 96 * h + 32 * n * j:96 * h + 32 * n * (j + 1)])
-        for s, e in enumerate(STAGES[MODES[c]]):
-            b, q = BASE[(c, s)], n * e
-            m["m_%d_%d" % (c, s)] = ("m%d_%d_%d" % (j, c, s), T.ol[:, 24 * b + 8 * q * j:24 * b + 8 * q * (j + 1)])
-            m["a_%d_%d" % (c, s)] = ("a_%d_%d" % (c, s), T.l1[:, 48 * b + 16 * q * j:48 * b + 16 * q * (j + 1)])
+        m["a0_%d" % c] = ("a0_%d" % c, T.l0[:, c, 64 * j:64 * j + 64])
+        m["m_%d" % c] = ("m%d_%d" % (j, c), T.ol[:, c, 48 * j:48 * j + 48])
+        m["a1_%d" % c] = ("a1_%d" % c, T.l1[:, c, 96 * j:96 * j + 96])
     return m
 
 
@@ -104,18 +93,18 @@ def build(g, T, topo, r, P):
     def ps(u):
         return T["ps%d" % u["bank"]]
 
-    def vc(n):
-        return P["fix"] + max(64, n) * P["cyc"]
-
     def dv(name, n, deps, fn, u=None, prio=R):
-        return add(name, "dve", vc(n), deps, prio, lambda e: fn(), unit=u)
+        return add(name, "dve", max(64, n) * P["cyc"], deps, prio, lambda e: fn(), unit=u)
 
-    def act(n, deps, out, in_, scale=1.0, u=None, prio=R):
-        return add("ac", "act", P["afix"] + n * P["cyc"], deps, prio,
-                   lambda e: g.scalar.activation(out, in_(), Fn.Identity, scale=scale), unit=u)
+    def shift(name, n, deps, out, in_, scale=1.0, bias=0.0, u=None, prio=R):
+        def em(e):
+            if e == "act":
+                return g.scalar.activation(out, in_(), Fn.Identity, bias=bias, scale=scale)
+            return V.tensor_scalar(out, in_(), scale, bias, Op.mult, Op.add)
+        return add(name, ["dve", "act"], {"dve": max(64, n) * P["cyc"], "act": P["afix"] + n * P["cyc"]}, deps, prio, em, unit=u)
 
     def pe(name, cyc, deps, fn, u, prio=R):
-        return add(name, "pe", 0.05 + cyc * P["pe"], deps, prio, lambda e: mms(fn()), unit=u)
+        return add(name, "pe", 0.02 + cyc * P["pe"], deps, prio, lambda e: mms(fn()), unit=u)
 
     def gp(n, deps, prio, fn):
         return add("gp", "gp", 0.17 + 2 * n * P["cyc"], deps, prio, lambda e: fn())
@@ -132,10 +121,11 @@ def build(g, T, topo, r, P):
     def tt(out, a, b, op):
         return V.tensor_tensor(out, a, b, op)
 
-    def mms(lst):
+    def mms(groups):
         last = None
-        for (o, l, rr, a, b) in lst:
-            last = g.tensor.matmul(o, l, rr, a, b)
+        for grp in groups:
+            for i, (o, l, rr) in enumerate(grp):
+                last = g.tensor.matmul(o, l, rr, i == 0, i == len(grp) - 1)
         return last
 
     sent = [0]
@@ -160,7 +150,7 @@ def build(g, T, topo, r, P):
             rid, pid = topo.addr(k, me)
             sent[0] += len(topo.engines(me, k))
             return g.remote_dma(dst, src(2), T.sem[sem], T.sem.sent, pid, rid, topo.mask(me, k))
-        a = add("F", "gp", P["iss"], dfar, prio, far, kind="r")
+        a = add("F", "gp", P["iss"] + (P["first"] if key == "c" else 0), dfar, prio, far, kind="r")
         a["key"] = key
         return a, add("N", "gp", P["iss"], dnear, prio + 0.01, near, kind="r")
 
@@ -175,112 +165,112 @@ def build(g, T, topo, r, P):
     def sel(out, in_, pat, op, base, cm):
         return lambda: g.affine_select(out, in_, pat, op, 0.0, base, cm)
 
+    own = slice(1024 * r, 1024 * r + 1024)
     lc = dma("sp", [], 0, T.cs[0:96, 0:1], T.cand[:], "lc", 16, at=P["small"])
-    lf = [dma("act", [], 0.5, T.fi[0:16, 0:256], T.fac[0, :], "lf", 32, at=P["small"]),
-          dma("act", [], 0.5, T.fi[0:16, 256:512], T.inc[0, :], "lf", 32, at=P["small"])]
-    lp = []
-    for i in range(16):
-        a, j = i // 4, i % 4
-        c0 = 1024 * sl[j] + 256 * a
-        lp.append(dma("act" if i % 2 and i > 2 else "sp", [], 1, T.p32[32 * a:32 * a + 32, j, :], T.pos0[:, c0:c0 + 256],
-                      "lp", 256, at=P["pos"]))
+    lp = [dma("sp", [], 1, T.p32[:, 2 * j:2 * j + 2, :], T.pos0[:, 1024 * sl[j]:1024 * sl[j] + 1024], "lp", 64, at=P["pos"])
+          for j in range(4)]
     lt = dma("sp", [], 2, T.tb[:], T.tab[:], "lt", 16, at=P["tab"])
-    my = dv("my", 96, [], lambda: V.memset(T.y32[:], 0), prio=0.5)
-    ly = []
-    for tn, src in enumerate((T.fac, T.inc, T.th)):
-        for k in range(3):
-            ly.append(dma("sp", [my], 3, T.y32[k:128:4, 32 * tn:32 * tn + 32], src[k, 1024 * r:1024 * r + 1024], "ly", 144,
-                          at=P["tab"] + 0.5))
+    lf = [dma("act", [], 0.5, o, i, "lf", 64, at=P["small"] + 0.3) for o, i in (
+        (T.fi[0:16, 0:256], T.fac[0, :]), (T.fi[0:16, 256:512], T.inc[0, :]),
+        (T.fi[16:24, 0:256], T.fac[1:3, own]), (T.fi[16:24, 256:512], T.inc[1:3, own]))]
+    ly = [dma("act", [], 0.6, o, i, "ly", 64, at=P["tab"]) for o, i in
+          [(T.fj[0:4, 384:640], T.th[0, own])] + [(T.fj[0:8, 128 * k:128 * k + 128], T.th[k, own]) for k in range(3)]]
 
     def c_(n, deps, prio, fn):
         return dv("c", n, deps, fn, prio=prio)
-    mc = c_(1, [], 0, lambda: V.memset(T.cs[96:128, :], 0))
-    m1 = c_(256, [], 0.1, lambda: V.memset(T.ones[:], 1.0))
-    mz = c_(304, [], 1, lambda: V.memset(T.zz[:], 0.0))
-    icol = gp(136, [], 0, lambda: g.iota(T.col[:], [[1, 136]], 0, 0, allow_small_or_imprecise_dtypes=True))
+
+    def fill(ap, n, val, prio, deps=()):
+        return c_(n, deps, prio, lambda: V.memset(ap, val))
+    mc = fill(T.cs[96:128, :], 1, 0, 0)
+    m1 = fill(T.ones[:], 384, 1.0, 0.1)
+    wk = [fill(T.wk[0:96, 32 * k:32 * k + 32], 1, 2.0 ** k / 32, 0.2) for k in range(3)]
+    mz = fill(T.zz[:], 264, 0.0, 1)
+    al = [fill(T.al[0:1, 128 * k:128 * k + 128], 64, 2.0 ** k / 32 * (1 / 128 - (0.5 if k == 1 else 0.0)), 1) for k in range(3)]
+    k0 = fill(T.kc[0:2, 0:128], 64, 8.0, 1.5)
+    kc = [fill(T.kc[0:1, 0:128], 64, 2.0 ** 25, 1.5, [k0])] + [
+        fill(T.kc[0:1, 128 * i:128 * i + 128], 64, v, 1.5) for i, v in ((1, -5.0 * 2 ** 22), (2, BIG), (3, -BIG))] + [m1]
+    icol = gp(144, [], 0, lambda: g.iota(T.col[:], [[1, 144]], 0, 0, allow_small_or_imprecise_dtypes=True))
     ip = gp(1, [], 0.1, lambda: g.iota(T.pi[:, 0:1], [[0, 1]], 0, 1))
-    gq = gp(96, [m1], 1, sel(T.qq[0:96, :], T.ones[0:96, 0:96], [[-4, 3], [-1, 4], [-12, 8]], Op.is_equal, 0, 1))
-    gn1 = gp(56, [m1], 1.2, sel(T.ns[0:96, 0:56], T.ones[0:96, 0:56], [[-12, 56]], Op.is_ge, 288, 1))
+    gn1 = gp(56, [m1], 1, sel(T.ns[0:96, 0:56], T.ones[0:96, 0:56], [[-12, 56]], Op.is_ge, 288, 1))
+    gq = gp(96, wk, 1.1, sel(T.qq[0:96, :], T.wk[0:96, :], [[-1, 3], [-3, 4], [-12, 8]], Op.is_equal, 0, 1))
     gns = gp(56, [gn1], 1.2, sel(T.ns[0:96, 0:56], T.ns[0:96, 0:56], [[12, 56]], Op.is_ge, -277, -1))
-    gs1 = gp(512, [m1], 2.5, sel(T.sel[0:32, :], T.ones[0:32, :], [[-1, 16], [0, 32]], Op.is_equal, 0, 1))
-    gpm = gp(128, [m1], 6, sel(T.pm[:], T.ones[:, 0:128], [[-4, 4], [-16, 8], [-1, 4]], Op.is_equal, 0, 1))
-    gnp = act(128, [gpm], T.npm[:], lambda: T.pm[:], -1.0, prio=7)
-    m1f = c_(128, [], 7, lambda: V.memset(T.onesf[:], 1.0))
-    gid = gp(128, [m1f], 7, sel(T.idf[:], T.onesf[:], [[-1, 128]], Op.is_equal, 0, 1))
-    gni = act(128, [gid], T.nidf[:], lambda: T.idf[:], -1.0, prio=7)
-    a31 = c_(1, [ip], 2, lambda: ts(T.pi[:, 1:2], T.pi[:, 0:1], 31, None, Op.bitwise_and))
-    a15 = c_(1, [ip], 2, lambda: ts(T.pi[:, 2:3], T.pi[:, 0:1], 15, None, Op.bitwise_and))
-    c31 = c_(1, [a31], 2, lambda: ts(T.pf[:, 0:1], T.pi[:, 1:2], 4.0, 3.0, Op.mult, Op.add))
-    c15 = c_(1, [a15], 2, lambda: V.tensor_copy(T.pf[:, 1:2], T.pi[:, 2:3]))
-    wq = [c_(1, [], 2, lambda q=q: V.memset(T.pf[32 * q:32 * q + 32, 2:3], 0.5 * 2 ** q)) for q in range(4)]
-    w0 = c_(136, [icol, c31] + wq, 3, lambda: ts(T.ww[:, 0:136], T.col[:], T.pf[:, 0:1], T.pf[:, 2:3], Op.is_equal, Op.mult))
-    wts = [w0] + [act(136, [w0], T.ww[:, 136 * t:136 * t + 136], lambda: T.ww[:, 0:136], 16.0 ** t, prio=3) for t in (1, 2)]
-    ks = c_(16, [icol, c15], 4, lambda: ts(T.s16[:], T.col[:, 0:16], T.pf[:, 1:2], None, Op.is_equal))
-    mfa = c_(128, [], 1, lambda: V.memset(T.fa[0:32, 512:768], -6144.0))
-    r1 = c_(48, [], 5, lambda: V.memset(T.rm[:], 1.0))
-    r16 = c_(6, [r1], 5, lambda: V.memset(T.rm[:, 0:96:16], 0.0))
-    mzv = c_(192, [], 6, lambda: V.memset(T.zv[:], 0.0))
+    gs1 = gp(512, [m1], 1.3, sel(T.sel[0:24, 0:512], T.ones[0:24, 0:512], [[-4, 4], [0, 32], [-1, 4]], Op.is_equal, 0, 1))
+    gs2 = gp(256, [m1], 6, sel(T.sel[0:24, 512:768], T.ones[0:24, 0:256], [[-4, 2], [0, 32], [-1, 4]], Op.is_equal, -16, 1))
+    gs8 = gp(128, [m1], 6, sel(T.s8[0:8, 0:128], T.ones[0:8, 0:128], [[-2, 4], [0, 16], [-1, 2]], Op.is_equal, 0, 1))
+    gsk = gp(256, [m1], 6, sel(T.s8[0:8, 128:384], T.ones[0:8, 0:256], [[-1, 2], [0, 32], [-2, 4]], Op.is_equal, 0, 1))
+    gpm = gp(128, [m1], 6, sel(T.pm[:], T.ones[:, 0:128], [[-1, 4], [-4, 32]], Op.is_equal, 0, 1))
+    gnp = shift("c", 128, [gpm], T.npm[:], lambda: T.pm[:], -1.0)
+    an = [c_(1, [ip], 2, lambda i=i, v=v: ts(T.pi[:, i:i + 1], T.pi[:, 0:1], v, None, Op.bitwise_and))
+          for i, v in ((1, 28), (2, 3), (3, 15), (4, 30))]
+    t0 = c_(1, an[0:1], 2, lambda: ts(T.pf[:, 0:1], T.pi[:, 1:2], 4.0, 12.0, Op.mult, Op.add))
+    t1 = c_(1, [t0, an[1]], 2, lambda: tt(T.pf[:, 1:2], T.pf[:, 0:1], T.pi[:, 2:3], Op.add))
+    t2 = c_(2, an[2:4], 2, lambda: V.tensor_copy(T.pf[:, 2:4], T.pi[:, 3:5]))
+    wq = [fill(T.pf[32 * q:32 * q + 32, 4:5], 1, 8.0 ** q, 2) for q in range(4)]
+    ww = c_(144, [icol, t1] + wq, 3, lambda: ts(T.ww[:], T.col[:], T.pf[:, 1:2], T.pf[:, 4:5], Op.is_equal, Op.mult))
+    ks = c_(16, [icol, t2], 4, lambda: ts(T.s16[:], T.col[:, 0:16], T.pf[:, 2:3], None, Op.is_equal))
+    mk = c_(3, [icol, t2], 4, lambda: ts(T.mk[:, 0:3], T.col[:, 0:6:2], T.pf[:, 3:4], None, Op.is_equal))
+    z0 = fill(T.ze[:], 384, 0.0, 4.5)
+    ze = [c_(128, [z0, mk, m1], 4.6, lambda: ts(T.ze[:, :, 0:192:3], T.ones[:, 0:256], T.mk[:, 2:3], None, Op.mult)),
+          c_(64, [z0, mk, m1], 4.6, lambda: ts(T.ze[:, :, 97:192:3], T.ones[:, 0:128], T.mk[:, 1:2], None, Op.mult))]
+    zm = [fill(T.zm[:, :, 1:96:3], 128, 0.0, 4.6), fill(T.zm[:, :, 98:192:3], 128, 0.0, 4.6)]
+    z1 = fill(T.tf1[0:8, :, :], 384, 0.0, 4.6)
+    u = unit("w")
+    m = pe("cm", 384, [gs8, gsk], lambda u=u: [[(ps(u)[:, 0:384], T.s8[0:8, 0:128], T.s8[0:8, 0:384])]], u)
+    cm = shift("c", 384, [m], T.cm[:, 0:384], lambda u=u: ps(u)[:, 0:384], 1 / 32, u=u)
+    ncm = shift("c", 128, [cm], T.cm[:, 384:512], lambda: T.cm[:, 0:128], -1.0)
 
     sc = send("c", lambda j: T.cs[:, 0:1], [lc, mc], [lc, mc], 3)
     ac = arrive(sc, [0, 1, 2], "ac", P["first"])
-    cfo = c_(1, [lc], 1.5, lambda: V.tensor_copy(T.cf[0:96, 3:4], T.cs[0:96, 0:1]))
+    cfo = c_(1, [lc], 1.5, lambda: V.tensor_copy(T.cf[0:96, 4:5], T.cs[0:96, 0:1]))
     cfr = c_(3, [ac], R, lambda: V.tensor_copy(T.cf[0:96, 0:3], T.cl[0:96, 0:3]))
     S = []
     for j in range(4):
         pr = 1.6 if j == 3 else R
-        b = 96 + 128 * j
+        b, i = 132 * j, j + j // 3
         e = c_(32, [cfo if j == 3 else cfr, icol], pr,
-               lambda j=j: ts(T.eq[0:96, 32 * j:32 * j + 32], T.col[0:96, 0:32], T.cf[0:96, j:j + 1], None, Op.is_equal))
-        e = c_(64, [e, gns, mz], pr, lambda j=j, b=b: tt(T.zz[0:96, b:b + 32], T.eq[0:96, 32 * j:32 * j + 32],
-                                                        T.ns[0:96, 24 - 8 * sl[j]:56 - 8 * sl[j]], Op.subtract))
+               lambda j=j, i=i: ts(T.eq[0:96, 32 * j:32 * j + 32], T.col[0:96, 0:32], T.cf[0:96, i:i + 1], None, Op.is_equal))
+        e = c_(64, [e, gns, mz], pr, lambda j=j, b=b: tt(T.zz[0:96, b + 3:b + 131:4], T.ns[0:96, 24 - 8 * sl[j]:56 - 8 * sl[j]],
+                                                        T.eq[0:96, 32 * j:32 * j + 32], Op.subtract))
         u = unit("w")
-        m = pe("sm", 400, [e, gq], lambda u=u, b=b: [
-            (ps(u)[:, a:384:4], T.zz[0:96, b - 32 * a:b - 32 * a + 128], T.qq[0:96, :], True, True) for a in range(4)], u, pr)
-        S.append(act(384, [m], T.ss[:, 384 * j:384 * j + 384], lambda u=u: ps(u)[:, 0:384], u=u, prio=pr))
+        m = pe("sm", 768, [e, gq, m1] + al, lambda u=u, b=b: [[(ps(u)[:, 0:384], T.ones[0:1, 0:128], T.al[0:1, :])] + [
+            (ps(u)[:, a:384:4], T.zz[0:96, b + 3 - a:b + 131 - a], T.qq[0:96, :]) for a in range(4)]], u, pr)
+        S.append(shift("sc", 384, [m], T.ss[:, 384 * j:384 * j + 384], lambda u=u: ps(u)[:, 0:384], u=u, prio=pr))
 
-    def st(j, t):
-        return T.ss[:, 384 * j + 128 * t:384 * j + 128 * t + 128]
+    def st(j, k):
+        return T.ss[:, 384 * j + 128 * k:384 * j + 128 * k + 128]
 
-    ca = c_(256, lf, 4.5, lambda: V.tensor_copy(T.fa[0:16, 0:256], T.fi[0:16, 0:256]))
-    cbb = c_(256, lf, 4.5, lambda: ts(T.fa[0:16, 256:512], T.fi[0:16, 256:512], -1.0, 15.5, Op.mult, Op.add))
-    yc = dv("yc", 96, ly, lambda: V.tensor_copy(T.yfl[:], T.y32[:]))
-    yt = dv("yt", 96, [yc], lambda: V.transpose(T.yt[:], T.yfl[:]))
-    k0 = dv("k", 16, [yt], lambda: V.tensor_copy(T.cb[:, :, 0:2], T.yt[:, 0, :, 1:3]))
-    k3 = dv("k", 16, [yt], lambda: V.tensor_copy(T.cb[:, :, 3:5], T.yt[:, 1, :, 1:3]))
-    k2 = dv("k", 8, [yt], lambda: tt(T.cb[:, :, 2], T.yt[:, 0, :, 1], T.yt[:, 0, :, 2], Op.mult))
-    k5a = dv("k", 8, [yt], lambda: tt(T.tmp[:, 0:8], T.yt[:, 0, :, 2], T.yt[:, 1, :, 1], Op.mult))
-    kf = dv("k", 8, [yt], lambda: ts(T.tmp[:, 8:16], T.yt[:, 0, :, 0], -1.0, None, Op.add))
-    k5 = dv("k", 8, [k5a], lambda: tt(T.cb[:, :, 5], T.tmp[:, 0:8], T.yt[:, 1, :, 2], Op.add))
-    kd = []
-    for j, kj in enumerate((k0, k0, k2)):
-        kd.append(dv("k", 8, [kj, kf], lambda j=j: tt(T.cd[:, :, j], T.cb[:, :, j], T.tmp[:, 8:16], Op.mult)))
-        kd.append(dv("k", 8, [kj], lambda j=j: tt(T.cd[:, :, 3 + j], T.cb[:, :, j], T.yt[:, 1, :, 0], Op.mult)))
-    kb = [k0, k2, k3, k5]
-    if len(set(CHUNKS)) == 1:
-        kt = [dv("kt", 8, [yt], lambda j=j, n=CHUNKS[0]: V.tensor_copy(T.th3[:, :, j * n:(j + 1) * n], T.yt[:, 2, :, min(j + 1, 2)]))
-              for j in range(3)]
-    else:
-        kt = [dv("kt", 8, [yt], lambda j=j, c=c, n=CHUNKS[c], h=H0[c]: V.tensor_copy(
-            T.th3[:, c, j * n:(j + 1) * n], T.yt[:, 2, h:h + n, min(j + 1, 2)])) for j in range(3) for c in range(NCH)]
+    fa = [c_(128, lf, 4, lambda f=f, k=k: V.tensor_copy(T.fa[0:24, 4 * f:4 * f + 4, 32 * k:32 * k + 32],
+                                                        T.fi[0:24, 256 * f + 128 * k:256 * f + 128 * k + 128]))
+          for f in range(2) for k in range(2)]
 
-    def masks(w, diff, dcyc, ddeps, bits, ba, out):
-        cm = []
-        for t in range(3):
-            u = unit("w")
-            d = pe("md", dcyc, ddeps, lambda u=u, t=t: diff(ps(u), t), u)
+    def thr(deps, out, in_, sgn):
+        return dv("th", 128, ly + deps, lambda: ts(out, in_, -sgn / 32, 0.5 + sgn / 64, Op.mult, Op.add))
+    tp = [thr([], T.fb[0:4, :, 32 * k:32 * k + 32], T.fj[0:4, 384 + 128 * k:512 + 128 * k], 1) for k in range(2)]
+    tf0 = thr([], T.tf0[0:8, :], T.fj[0:8, 0:128], 1)
+    tf1 = [thr([z1], T.tf1[0:8, :, a:b:3], T.fj[0:8, 128 * k:128 * k + 128], s)
+           for a, b, k, s in ((1, 96, 2, 1), (97, 192, 2, 1), (2, 96, 1, -1), (98, 192, 1, 1))]
 
-            def em(e, u=u, t=t):
-                o = bits[:, ba + w * t:ba + w * (t + 1)]
-                if e == "act":
-                    return g.scalar.activation(o, ps(u)[:, 0:w], Fn.Sign, bias=-0.5, scale=-1.0)
-                return ts(o, ps(u)[:, 0:w], 0.0, 2.0, Op.is_lt, Op.mult)
-            cm.append(add("mb", ["dve", "act"], {"dve": vc(w), "act": P["afix"] + w * P["cyc"]}, [d], R, em, unit=u))
+    def rnd(o, w):
+        return [(o, T.kc[0:1, 256:384], T.ones[0:1, 0:w]), (o, T.kc[0:1, 384:512], T.ones[0:1, 0:w])]
+
+    def masks(parts, deps, bits, out):
+        w = sum(p[2] for p in parts)
         u = unit("w")
-        m = pe("mm", 12 * max(64, w // 4), cm + wts, lambda: [
-            (ps(u)[:, 0:w // 4], T.ww[:, 136 * t + 3 - s:136 * t + 131 - s], bits[:, ba + w * t + s:ba + w * (t + 1):4],
-             t == 0 and s == 0, t == 2 and s == 3) for t in range(3) for s in range(4)], u)
-        return dv("mc", w // 4, [m], lambda: ts(
-            out, ps(u)[:, 0:w // 4], sum(7.5 * 16 ** t for t in range(3) if cm[t]["on"] == "act") + 0.0, None, Op.add), u)
+
+        def diff():
+            def x(k):
+                l, a = [], 0
+                for j, pos, n in parts:
+                    l.append((ps(u)[:, a:a + n], st(j, k), pos))
+                    a += n
+                return l
+            return [[(ps(u)[:, 0:w], T.kc[0:2, 0:128], T.ones[0:2, 0:w])] + x(2) + x(1) +
+                    [(ps(u)[:, 0:w], T.kc[0:1, 128:256], T.ones[0:1, 0:w])] + x(0)]
+        d = pe("md", 5 * w, deps + kc, diff, u)
+        b = shift("mb", w, [d], bits(0, 1), lambda: ps(u)[:, 0:w], 1.0, -LEFT, u)
+        m = pe("mm", 4 * max(64, w // 4), [b, ww], lambda: [[
+            (ps(u)[:, 0:w // 4], T.ww[:, 12 - 4 * s:140 - 4 * s], bits(s, 4)) for s in range(4)]], u)
+        return dv("mc", w // 4, [m], lambda: V.tensor_copy(out, ps(u)[:, 0:w // 4]), u)
 
     def gather(name, off, k, out, deps):
         def em(e):
@@ -289,198 +279,111 @@ def build(g, T, topo, r, P):
                 return g.scalar.activation(out, src, Fn.Copy)
             return V.tensor_copy(out, src)
         c = 16 * k * P["gat"] * P["cyc"]
-        return add(name, ["act", "dve"], {"act": 0.08 + c, "dve": 0.06 + c}, deps + [lt], R, em)
-
-    def owner_stage(c, s, coef, deps):
-        n, h, ne = CHUNKS[c], H0[c], STAGES[MODES[c]][s]
-        b, q = BASE[(c, s)], n * ne
-        af = [dv("af", 32, deps, lambda k=k, ev=ev: ts(
-            T.wi[:, 32 * (b + k * ne + ev):32 * (b + k * ne + ev + 1)], T.pc[:, 32 * (h + k):32 * (h + k + 1)],
-            coef(h + k, ev)[0], coef(h + k, ev)[1], Op.mult, Op.add)) for k in range(n) for ev in range(ne)]
-        xa, xb = 32 * b, 32 * (b + q)
-        e7 = dv("d7", 32 * q, af, lambda: ts(T.wa[:, xa:xb], T.wi[:, xa:xb], 31, None, Op.bitwise_and))
-        e8 = dv("d8", 32 * q, [e7], lambda: V.tensor_copy(T.wb[:, xa:xb], T.wa[:, xa:xb]))
-        e9 = dv("d9", 16 * q, [e8], lambda: V.transpose(T.xt[:, xa:xb], T.wb[:, xa:xb]))
-        mo = {}
-        for js in ([[0, 1, 2, 3]] if q <= 4 else [[0, 1], [2, 3]]):
-            o = masks(32 * q * len(js), lambda p, t, js=js: [
-                (p[:, 32 * q * i:32 * q * (i + 1)], st(j, t), T.xt[:, xa:xb], True, True) for i, j in enumerate(js)],
-                len(js) * max(64, 32 * q), [e9] + [S[j] for j in js], T.b1, 384 * b + 96 * q * js[0],
-                T.om[:, 32 * b + 8 * q * js[0]:32 * b + 8 * q * (js[-1] + 1)])
-            for j in js:
-                mo[j] = o
-        sm_ = send("m_%d_%d" % (c, s), lambda j: T.om[:, 32 * b + 8 * q * j:32 * b + 8 * q * (j + 1)], [mo[0]], [mo[2]], 19)
-        cvs = {}
-        for js in ([[0, 1, 2, 3]] if q <= 2 else [[0, 1], [2, 3]]):
-            u = unit("s")
-            sm = []
-            for gs in ([[0, 1], [2], [3]] if q <= 2 else [[j] for j in js]):
-                j, nj = gs[0], len(gs)
-                if j == 3:
-                    off, dep = T.om[:, 32 * b + 24 * q:32 * b + 32 * q], [mo[3]]
-                else:
-                    off = T.ol[:, 24 * b + 8 * q * j:24 * b + 8 * q * (j + nj)]
-                    dep = [arrive(sm_, [i], "m%d_%d_%d" % (i, c, s)) for i in gs]
-                g1 = 512 * b + 128 * q * j
-                ga = gather("g1", off, 8 * q * nj, T.g1[:, g1:g1 + 128 * q * nj], dep)
-
-                def su(u=u, gs=gs, j0=js[0]):
-                    lst = []
-                    for j in gs:
-                        for k in range(n):
-                            for ev in range(ne):
-                                o = 16 * (q * (j - j0) + ev * n + k)
-                                i = 512 * b + 128 * (q * j + k * ne + ev)
-                                lst.append((ps(u)[:, o:o + 16], T.g1[:, i:i + 128], T.s16[:], True, True))
-                    return lst
-                sm.append(pe("su", 64 * q * nj, [ga, ks], su, u))
-            s1, w = 64 * b + 16 * q * js[0], 16 * q * len(js)
-            o = dv("sc", w, sm, lambda u=u, s1=s1, w=w: V.tensor_copy(T.s1[:, s1:s1 + w], ps(u)[:, 0:w]), u)
-            for j in js:
-                cvs[j] = o
-        sn = send("a_%d_%d" % (c, s), lambda j: T.s1[:, 64 * b + 16 * q * j:64 * b + 16 * q * (j + 1)], [cvs[0]], [cvs[2]], 20)
-        a1 = arrive(sn, [0, 1, 2], "a_%d_%d" % (c, s))
-
-        def src(j, a, e):
-            x, o = (T.s1, 64 * b + 48 * q) if j == 3 else (T.l1, 48 * b + 16 * q * j)
-            return x[:, o + 16 * n * a:o + 16 * n * e]
-        return src, [a1, cvs[3]]
+        return add(name, ["act", "dve"], {"act": 0.07 + c, "dve": 0.05 + c}, deps + [lt], R, em)
 
     J = (3, 0, 1, 2)
-
-    def count(u, o, a, w, out, th, deps):
-        e1 = dv("ge", w, deps[:1], lambda: ts(T.ge[:, a:a + w], ps(u)[:, o:o + w], 0.0, None, Op.is_ge), u)
-        e2 = dv("cn", w // 2, [e1, r16], lambda: V.tensor_tensor_scan(T.cn[:, a:a + w], T.rm[:, 0:w], T.ge[:, a:a + w], 0.0,
-                                                                     Op.mult, Op.add))
-        return dv("wv", w // 8, [e2] + deps[1:], lambda: tt(out, T.cn[:, a + 15:a + w:16], th, Op.is_ge))
-
-    def flag(k, rnd):
-        return T.ft[:, k, 16 + rnd:17 + rnd]
-
-    def decide1(c, rnd, src, deps, fprev, fout):
-        n, h = CHUNKS[c], H0[c]
-        w = 16 * n
-        u = unit("o")
-        if fprev is None:
-            to = pe("to", 768, deps + [gpm, gnp], lambda: (
-                [(ps(u)[:, w:2 * w], T.pm[:], src(j, 1, 2), j == 3, False) for j in J] +
-                [(ps(u)[:, w:2 * w], T.npm[:], src(j, 0, 1), False, j == 2) for j in J] +
-                [(ps(u)[:, 0:w], T.pm[:], src(j, 0, 1), j == 3, j == 2) for j in J]), u)
-        else:
-            to = pe("to", 512, deps + [gpm, gni], lambda: (
-                [(ps(u)[:, w:2 * w], T.nidf[:], fprev, True, False)] +
-                [(ps(u)[:, w:2 * w], T.pm[:], src(j, 0, 1), False, j == 2) for j in J]), u)
-        a = count(u, w, 64 * h + w * rnd, w, T.ft[:, h:h + n, 16 + rnd], T.yt[:, 2, h:h + n, rnd], [to, yt])
-        f1 = [dv("f1", 16, [a], lambda k=k: ts(T.tm[:, rnd, 16 * (h + k):16 * (h + k + 1)], ps(u)[:, w + 16 * k:w + 16 * k + 16],
-                                               flag(h + k, rnd), None, Op.mult), u) for k in range(n)]
-        tm = T.tm[:, rnd, 16 * h:16 * (h + n)]
-        if fprev is None:
-            return a, [dv("f2", w, f1, lambda: tt(fout, ps(u)[:, 0:w], tm, Op.add), u)]
-        if fout is not None:
-            return a, [dv("f2", 2 * w, f1, lambda: tt(fout, fprev, tm, Op.add))]
-        return a, [dv("f2", 32, [f1[k]], lambda k=k: tt(T.ft[:, h + k, 0:16], T.ff[:, 1, 16 * (h + k):16 * (h + k + 1)],
-                                                       T.tm[:, rnd, 16 * (h + k):16 * (h + k + 1)], Op.add)) for k in range(n)]
-
-    def decide2(c, src, deps, fprev):
-        n, h = CHUNKS[c], H0[c]
-        w = 16 * n
-        o = 48 * h
-        u = unit("o")
-        to = pe("to", 1150, deps + [gpm, gnp, gni], lambda: (
-            [(ps(u)[:, 0:3 * w], T.pm[:], src(j, 0, 3), j == 3, False) for j in J] +
-            [(ps(u)[:, i * w:(i + 1) * w], T.nidf[:], fprev, False, False) for i in range(2)] +
-            [(ps(u)[:, 2 * w:3 * w], T.npm[:], src(j, 0, 1), False, j == 2) for j in J]), u)
-        a = count(u, 0, 64 * h + w, 3 * w, T.zv[:, o:o + 3 * w:16], T.th3[:, c, 0:3 * n], [to, mzv] + kt)
-
-        def z(k):
-            return T.zv[:, o + k * w:o + (k + 1) * w:16]
-        zu = dv("u", n, [a], lambda: tt(z(1), z(1), z(0), Op.is_gt))
-        zv = dv("v", n, [a], lambda: tt(z(2), z(2), z(0), Op.mult))
-        z4 = dv("bw", 3 * w // 2, [zu, zv], lambda: V.tensor_tensor_scan(T.wv[:, o:o + 3 * w], T.rm[:, 0:3 * w], T.zv[:, o:o + 3 * w],
-                                                                        0.0, Op.mult, Op.add))
-        z5 = dv("t3", 3 * w, [z4], lambda: tt(T.t3[:, o:o + 3 * w], ps(u)[:, 0:3 * w], T.wv[:, o:o + 3 * w], Op.mult), u)
-        z6 = dv("ta", 2 * w, [z5], lambda: tt(T.t2[:, 0, 16 * h:16 * (h + n)], T.t3[:, o:o + w], T.t3[:, o + w:o + 2 * w], Op.add))
-        z7 = dv("tb", 2 * w, [z5], lambda: tt(T.t2[:, 1, 16 * h:16 * (h + n)], T.t3[:, o + 2 * w:o + 3 * w], fprev, Op.add))
-        return [dv("tc", 32, [z6, z7], lambda k=k: tt(T.ft[:, k, 0:16], T.t2[:, 0, 16 * k:16 * k + 16], T.t2[:, 1, 16 * k:16 * k + 16],
-                                                     Op.add)) for k in range(h, h + n)] + [
-            dv("fl", n, [a], lambda: V.tensor_copy(T.ft[:, h:h + n, 17], z(0))),
-            dv("fl", n, [zu, zv], lambda: tt(T.ft[:, h:h + n, 18], z(1), z(2), Op.add))]
-
     fin = []
-    prev = []
 
     def chunk(c):
-        n, h, mode = CHUNKS[c], H0[c], MODES[c]
-        w, xa = 128 * n, 128 * h
-        cv = dv("cv", w, lp, lambda: V.tensor_copy(T.x0[:, xa:xa + w], T.p32[:, :, 32 * h:32 * (h + n)]))
+        cv = dv("cv", 256, lp, lambda: V.tensor_copy(T.xq[:, c, 0:256], T.p32[:, :, 32 * c:32 * c + 32]))
         ub = unit("o")
-        bc = pe("bc", 8 * max(64, 32 * n) + w, [ca, cbb, gs1, mfa, m1] + prev[-1:], lambda: [
-            (ps(ub)[:, 32 * n * j:32 * n * (j + 1)], T.sel[0:16, 128 * sl[j]:128 * sl[j] + 128],
-             T.fa[0:16, 32 * h:32 * (h + n)], True, True) for j in range(4)] +
-            [(ps(ub)[:, 256:256 + w], T.ones[0:1, 0:128], T.fa[0:1, 512:512 + w], True, False)] + [
-            (ps(ub)[:, 256 + 32 * n * j:256 + 32 * n * (j + 1)], T.sel[0:16, 128 * sl[j]:128 * sl[j] + 128],
-             T.fa[0:16, 256 + 32 * h:256 + 32 * (h + n)], False, j == 3) for j in range(4)], ub)
-        xx = dv("x", w, [bc, cv], lambda: tt(T.x1[:, xa:xa + w], ps(ub)[:, 0:w], T.x0[:, xa:xa + w], Op.mult), ub)
-        yy = dv("y", w, [xx], lambda: tt(T.y1[:, xa:xa + w], ps(ub)[:, 256:256 + w], T.x1[:, xa:xa + w], Op.subtract), ub)
-        prev.append(xx)
-        oa, sa = 64 * h, 128 * h
-        mk = masks(2 * w, lambda p, t: [(p[:, 0:w], st(3, t), T.x0[:, xa:xa + w], True, True),
-                                        (p[:, w:2 * w], st(3, t), T.x1[:, xa:xa + w], True, False),
-                                        (p[:, w:2 * w], st(3, t), T.y1[:, xa:xa + w], False, True)],
-                   3 * w, [yy, S[3]], T.b0, 768 * h, T.o0[:, oa:oa + 64 * n])
+        bc = pe("bc", 512, fa + [gs1, cv], lambda: [
+            [(ps(ub)[:, 256 * f + 64 * j:256 * f + 64 * j + 64], T.sel[0:24, 128 * sl[j]:128 * sl[j] + 128], T.fa[0:24, 4 * f + c, :])]
+            for f in range(2) for j in range(4)], ub)
+        e = dv("p1", 256, [bc], lambda: tt(T.m0[:, c, :], ps(ub)[:, 0:256], T.xq[:, c, 0:256], Op.mult), ub)
+        e = dv("p2", 256, [e], lambda: tt(T.xi[:, c, :], ps(ub)[:, 256:512], T.m0[:, c, :], Op.add), ub)
+        e = dv("p3", 256, [e], lambda: ts(T.xa[:, c, :], T.xi[:, c, :], 31, None, Op.bitwise_and))
+        p0 = dv("p4", 256, [e], lambda: V.tensor_copy(T.xq[:, c, 256:512], T.xa[:, c, :]))
+        mk0 = masks([(3, T.xq[:, c, :], 512)], [p0, S[3]], lambda s, n: T.b0[:, c, s:512:n], T.o0[:, c, :])
         cvs = []
         for hf in range(2):
             u = unit("s")
             sm = []
             for ev in range(2):
-                o1 = oa + 32 * n * ev + 16 * n * hf
-                ga = gather("g0", T.o0[:, o1:o1 + 16 * n], 16 * n, T.g0[:, 16 * o1:16 * o1 + 256 * n], [mk])
-                sm.append(pe("su", 128 * n, [ga, ks], lambda u=u, o1=o1, ev=ev: [
-                    (ps(u)[:, 32 * n * jj + 16 * n * ev + 16 * k:32 * n * jj + 16 * n * ev + 16 * k + 16],
-                     T.g0[:, 16 * o1 + 128 * (n * jj + k):16 * o1 + 128 * (n * jj + k + 1)], T.s16[:], True, True)
-                    for jj in range(2) for k in range(n)], u))
-            s1 = sa + 64 * n * hf
-            cvs.append(dv("sc", 64 * n, sm, lambda u=u, s1=s1: V.tensor_copy(T.s0[:, s1:s1 + 64 * n], ps(u)[:, 0:64 * n]), u))
-        sn = send("a0_%d" % c, lambda j: T.s0[:, sa + 32 * n * j:sa + 32 * n * (j + 1)], [cvs[0]], [cvs[1]], 20)
-        d0 = [arrive(sn, [0, 1, 2], "a0_%d" % c), cvs[1]]
+                o1 = 64 * ev + 32 * hf
+                ga = gather("g0", T.o0[:, c, o1:o1 + 32], 32, T.g0[:, c, 16 * o1:16 * o1 + 512], [mk0])
+                sm.append(pe("su", 256, [ga, ks], lambda u=u, o1=o1, ev=ev: [
+                    [(ps(u)[:, 64 * jj + 32 * ev + k:64 * jj + 32 * ev + 32:2],
+                      T.g0[:, c, 16 * o1 + 128 * (2 * jj + k):16 * o1 + 128 * (2 * jj + k + 1)], T.s16[:])]
+                    for jj in range(2) for k in range(2)], u))
+            cvs.append(dv("sc", 128, sm, lambda u=u, hf=hf: V.tensor_copy(T.s0[:, c, 128 * hf:128 * hf + 128], ps(u)[:, 0:128]), u))
+        sn = send("a0_%d" % c, lambda j: T.s0[:, c, 64 * j:64 * j + 64], [cvs[0]], [cvs[1]], 20)
+        dl = dv("dl", 128, [p0], lambda: tt(T.dl[:, c, :], T.xq[:, c, 448:512], T.xq[:, c, 192:256], Op.subtract))
 
-        def src0(j, a, e):
-            x, o = (T.s0, sa + 96 * n) if j == 3 else (T.l0, 96 * h + 32 * n * j)
-            return x[:, o + 16 * n * a:o + 16 * n * e]
-        pt = dv("pt", 16 * n, [cv], lambda: V.transpose(T.pc[:, 32 * h:32 * (h + n)], T.x0[:, xa + 96 * n:xa + 128 * n]))
-
-        def ff(i):
-            return T.ff[:, i, 16 * h:16 * (h + n)]
-        hs = slice(h, h + n)
-        a, f = decide1(c, 0, src0, d0, None, ff(0))
-        e4 = [dv("d4", 6, [a] + kd, lambda k=k: ts(T.ct[:, k, :], T.cd[:, k, :], flag(k, 0), None, Op.mult)) for k in range(h, h + n)]
-        e5 = dv("d5", 12 * n, e4 + kb, lambda: tt(T.cc[:, hs, :], T.ct[:, hs, :], T.cb[:, hs, :], Op.add))
-        src, d1 = owner_stage(c, 0, lambda k, ev: (T.cc[:, k, ev:ev + 1], T.cc[:, k, 3 + ev:4 + ev]), [e5, pt])
-        if mode == "t2":
-            done = decide2(c, src, d1 + f, ff(0))
-        else:
-            dl = dv("dl", 4 * n, [e5], lambda: tt(T.dm[:, 0, hs, :], T.cc[:, hs, 2:6:3], T.cc[:, hs, 1:6:3], Op.subtract))
-            a, f = decide1(c, 1, src, d1 + f, ff(0), ff(1))
-            e4 = [dv("d4", 2, [a, dl], lambda k=k: ts(T.dm[:, 1, k, :], T.dm[:, 0, k, :], flag(k, 1), None, Op.mult))
-                  for k in range(h, h + n)]
-            e6 = dv("d5", 4 * n, e4, lambda: tt(T.dm[:, 2, hs, :], T.dm[:, 1, hs, :], T.cc[:, hs, 1:6:3], Op.add))
-            sr2, d2 = owner_stage(c, 1, lambda k, ev: (T.dm[:, 2, k, 0:1], T.dm[:, 2, k, 1:2]), [e6])
-            a, done = decide1(c, 2, sr2, d2 + f, ff(1), None)
-        u = unit("o")
-        z7 = pe("tr", 512 * n, done + [gid], lambda: [
-            (ps(u)[0:19, 128 * k:128 * k + 128], T.ft[:, h + k, :], T.idf[:], True, True) for k in range(n)], u)
-        for k in range(n):
-            o, i = T.yy[0:19, :, 32 * (h + k):32 * (h + k + 1)], slice(128 * k, 128 * k + 128)
-            if P["e8"] and c < NCH - 1:
-                fin.append(act(128, [z7], o, lambda i=i: ps(u)[0:19, i], u=u))
-            else:
-                fin.append(dv("e8", 128, [z7], lambda o=o, i=i: V.tensor_copy(o, ps(u)[0:19, i]), u))
+        def src0(j, a, b):
+            return T.s0[:, c, 192 + a:192 + b] if j == 3 else T.l0[:, c, 64 * j + a:64 * j + b]
+        u0, up = unit("o"), unit("o")
+        to = pe("to", 512, [arrive(sn, [0, 1, 2], "a0_%d" % c), cvs[1], gpm, gnp], lambda: [
+            [(ps(u0)[:, 0:64], T.pm[:], src0(j, 0, 64)) for j in J] + [(ps(u0)[:, 32:64], T.npm[:], src0(j, 0, 32)) for j in J]], u0)
+        co = pe("co", 256, [to, gs2] + fa, lambda: [
+            [(ps(up)[:, 64 + 128 * f + 64 * k:128 + 128 * f + 64 * k], T.sel[0:24, 512 + 128 * k:640 + 128 * k], T.fa[0:24, 4 * f + c, :])]
+            for f in range(2) for k in range(2)], up)
+        tr = dv("tr", 64, [to], lambda: V.transpose(T.r0[:, c, 0:64], ps(u0)[:, 0:64]), u0)
+        ge = dv("ge", 32, [tr], lambda: ts(T.ge0[:, c, :], T.r0[:, c, 32:64], 0.0, None, Op.is_ge))
+        zp = pe("zp", 320, [ge, co, cm, gs1] + tp + kc, lambda: [
+            [(ps(up)[:, 0:64], T.sel[0:4, 0:128], T.fb[0:4, c, :])] +
+            [(ps(up)[:, 32 * k:32 * k + 32], T.cm[:, 128 + 128 * k:256 + 128 * k], T.ge0[:, c, :]) for k in range(2)] +
+            rnd(ps(up)[:, 0:64], 64)], up)
+        zf = pe("zf", 256, [ge, cm, tf0, gs8] + kc, lambda: [
+            [(ps(u0)[:, 64:96], T.s8[0:8, 0:128], T.tf0[0:8, 32 * c:32 * c + 32]), (ps(u0)[:, 64:96], T.cm[:, 0:128], T.ge0[:, c, :])] +
+            rnd(ps(u0)[:, 64:96], 32)], u0)
+        f1 = dv("f1", 32, [zf], lambda: tt(T.r0[:, c, 64:96], ps(u0)[:, 64:96], T.r0[:, c, 32:64], Op.mult), u0)
+        a0 = dv("a0", 32, [zf, mk, z0], lambda: ts(T.ze[:, c, 2:96:3], ps(u0)[:, 64:96], T.mk[:, 0:1], None, Op.mult), u0)
+        f2 = dv("f2", 64, [f1], lambda: tt(T.xx[:, c, 0:32], T.r0[:, c, 64:96], T.r0[:, c, 0:32], Op.add))
+        f3 = shift("f3", 32, [f2], T.zm[:, c, 2:96:3], lambda: T.xx[:, c, 0:32])
+        e = dv("q1", 64, [zp, dl], lambda: tt(T.cu[:, c, 0:64], ps(up)[:, 0:64], T.dl[:, c, :], Op.mult), up)
+        e = dv("q2", 128, [e], lambda: tt(T.cu[:, c, 64:128], T.cu[:, c, 0:64], T.xq[:, c, 192:256], Op.add))
+        q3 = [dv("q3", 64, [e], lambda k=k: tt(T.mi[:, c, 64 * k:64 * k + 64], ps(up)[:, 64 + 64 * k:128 + 64 * k], T.cu[:, c, 64:128],
+                                               Op.mult), up) for k in range(2)]
+        e = dv("q4", 128, q3, lambda: tt(T.yi[:, c, 0:128], ps(up)[:, 192:320], T.mi[:, c, 0:128], Op.add), up)
+        e = dv("q5", 64, [e], lambda: tt(T.mi[:, c, 128:192], ps(up)[:, 128:192], T.yi[:, c, 0:64], Op.mult), up)
+        e = dv("q6", 64, [e], lambda: tt(T.yi[:, c, 128:192], ps(up)[:, 256:320], T.mi[:, c, 128:192], Op.add), up)
+        e = dv("q7", 192, [e], lambda: ts(T.yb[:, c, :], T.yi[:, c, :], 31, None, Op.bitwise_and))
+        xt = dv("q8", 192, [e], lambda: V.tensor_copy(T.xt[:, c, :], T.yb[:, c, :]))
+        mo = [masks([(j, T.xt[:, c, :], 192) for j in (2 * h, 2 * h + 1)], [xt, S[2 * h], S[2 * h + 1]],
+                    lambda s, n, h=h: T.b1[:, c, 384 * h + s:384 * h + 384:n], T.om[:, c, 96 * h:96 * h + 96]) for h in range(2)]
+        sm_ = send("m_%d" % c, lambda j: T.om[:, c, 48 * j:48 * j + 48], [mo[0]], [mo[1]], 19)
+        cvs = []
+        for js in ([0, 1], [2], [3]):
+            u = unit("s")
+            sm = []
+            for j in js:
+                if j == 3:
+                    off, dep = T.om[:, c, 144:192], mo[1]
+                else:
+                    off, dep = T.ol[:, c, 48 * j:48 * j + 48], arrive(sm_, [j], "m%d_%d" % (j, c))
+                ga = gather("g1", off, 48, T.g1[:, c, 768 * j:768 * j + 768], [dep])
+                sm.append(pe("su", 384, [ga, ks], lambda u=u, j=j, a=96 * (j - js[0]): [
+                    [(ps(u)[:, a + 32 * ev + k:a + 32 * ev + 32:2],
+                      T.g1[:, c, 768 * j + 128 * (2 * ev + k):768 * j + 128 * (2 * ev + k + 1)], T.s16[:])]
+                    for ev in range(3) for k in range(2)], u))
+            w, a = 96 * len(js), 96 * js[0]
+            cvs.append(dv("sc", w, sm, lambda u=u, w=w, a=a: V.tensor_copy(T.s1[:, c, a:a + w], ps(u)[:, 0:w]), u))
+        sn1 = send("a1_%d" % c, lambda j: T.s1[:, c, 96 * j:96 * j + 96], [cvs[0]], [cvs[1]], 20)
+        u1 = unit("o")
+        to1 = pe("to", 384, [arrive(sn1, [0, 1, 2], "a1_%d" % c), cvs[2], gpm], lambda: [
+            [(ps(u1)[:, 0:96], T.pm[:], T.s1[:, c, 288:384] if j == 3 else T.l1[:, c, 96 * j:96 * j + 96]) for j in J]], u1)
+        tr1 = dv("tr", 96, [to1], lambda: V.transpose(T.xx[:, c, 32:128], ps(u1)[:, 0:96]), u1)
+        ga = dv("ge", 128, [tr1, f2], lambda: tt(T.ge1[:, c, 32:96], T.xx[:, c, 64:128], T.xx[:, c, 0:64], Op.is_ge))
+        gb = dv("ge", 64, [tr1, f2], lambda: tt(T.ge1[:, c, 0:32], T.xx[:, c, 32:64], T.xx[:, c, 0:32], Op.is_ge))
+        da = dv("df", 128, [ga], lambda: tt(T.zm[:, c, 0:192:3], T.xx[:, c, 64:128], T.xx[:, c, 0:64], Op.subtract))
+        db = dv("df", 64, [gb], lambda: tt(T.zm[:, c, 97:192:3], T.xx[:, c, 32:64], T.xx[:, c, 0:32], Op.subtract))
+        zq = pe("zq", 768, [ga, gb, cm, ncm, gs8] + tf1 + kc, lambda: [
+            [(ps(u1)[:, 128:320], T.s8[0:8, 0:128], T.tf1[0:8, c, :]),
+             (ps(u1)[:, 129:320:3], T.cm[:, 0:128], T.ge1[:, c, 32:96]),
+             (ps(u1)[:, 226:320:3], T.cm[:, 0:128], T.ge1[:, c, 0:32]),
+             (ps(u1)[:, 130:224:3], T.cm[:, 384:512], T.ge1[:, c, 0:32])] + rnd(ps(u1)[:, 128:320], 192)], u1)
+        for o, d, y, dep in ((T.om1, T.zm, T.yy, [da, db, f3] + zm), (T.oe1, T.ze, T.ye, [a0] + ze)):
+            e = dv("sn", 192, [zq] + dep, lambda o=o, d=d: V.tensor_tensor_scan(o[:, c, :], ps(u1)[:, 128:320], d[:, c, :], 0.0,
+                                                                               Op.mult, Op.add), u1)
+            fin.append(dv("fo", 64, [e], lambda o=o, y=y: tt(y[:, 32 * c:32 * c + 32], o[:, c, 2:96:3], o[:, c, 98:192:3], Op.add)))
 
     for c in range(NCH):
         cur[0] = c
         chunk(c)
-    dma("sp", fin, 90, T.yf[:], T.yy[0:16, :, :], "st", 32)
-    dma("act", fin, 9000, T.ya[:], T.yy[16:19, :, :], "st", 32)
+    for q in range(4):
+        dma("sp" if q % 2 else "act", fin[0::2], 9000, T.yf[:, 256 * q:256 * q + 256], T.yy[32 * q:32 * q + 32, :], "st", 128)
+        dma("act" if q % 2 else "sp", fin[1::2], 9001, T.ya[:, 256 * q:256 * q + 256], T.ye[32 * q:32 * q + 6, :], "st", 128)
     return ops, Q, sent
 
 
@@ -521,7 +424,7 @@ def lay_out(ops, P):
                     soon.append((o, y))
                     if o["eng"] == ["pe"]:
                         soon += [(x, y + o["cost"]["pe"] + P["lat"]) for x in o["unit"]["ops"] if len(x["deps"]) == 1 and x["deps"][0] is o]
-        for e in ("gp", "sp", "pe", "dve", "act"):
+        for e in ("gp", "sp", "pe", "act", "dve"):
             if free[e] > t + 1e-9:
                 continue
             best, bank = None, None

@@ -2,8 +2,9 @@ from concourse.bass import DstId, RemoteDMATransfer
 from concourse.mybir import AluOpType as Op, ActivationFunctionType as Fn
 
 NCH = 4
-PAR = {"cyc": 0.00095, "pe": 0.00048, "afix": 0.07, "lat": 0.15, "gat": 1.56, "hop": 2.0, "iss": 0.5, "pos": 4.0,
-       "tab": 8.5, "small": 2.0, "first": 3.0, "look": 0.2, "dg0": 0.0, "dg1": 0.0, "ab": -0.5, "skew": 2.0}
+PAR = {"cyc": 0.00088, "pe": 0.00044, "afix": 0.07, "lat": 0.11, "gat": 1.56, "hop": 1.8, "iss": 0.5, "pos": 4.2,
+       "tab": 7.6, "small": 2.0, "first": 2.0, "own": 0.6, "skew": 2.0, "sets": [(1.0, 0.0, 0.11, 0.0), (1.15, 0.7, 0.13, 0.3)],
+       "tidy": 0.2, "seed": 2, "moves": 45000, "slack": 0.3, "group": 25, "reach": 3}
 BIG = 1.5 * 2 ** 23
 LEFT = 3.0 * 2 ** 22 - 54
 
@@ -16,10 +17,10 @@ for _t, _l in (
                       "b1": [4, 768], "g1": [4, 3072], "xt": [4, 192], "dl": [4, 64], "cu": [4, 128], "ge0": [4, 32],
                       "ge1": [4, 96], "ze": [4, 192]}),
         ("float16", {"s0": [4, 256], "l0": [4, 192], "s1": [4, 384], "l1": [4, 288], "m0": [4, 256]}),
-        ("uint16", {"o0": [4, 128], "om": [4, 192], "ol": [4, 144]}),
+        ("uint16", {"o0": [16, 32], "om": [4, 192], "ol": [4, 144]}),
         ("int32", {"p32": [8, 128], "cs": [4], "cl": [4], "fi": [512], "fj": [640], "pi": [8], "xi": [4, 256], "xa": [4, 256],
                    "mi": [4, 192], "yi": [4, 192], "yb": [4, 192]}),
-        ("float32", {"cf": [8], "col": [144], "pf": [8], "mk": [4], "r0": [4, 96], "xx": [4, 128], "zm": [4, 192],
+        ("float32", {"cf": [8], "col": [144], "pf": [8], "mk": [4], "r0": [4, 128], "xx": [4, 128], "zm": [4, 192],
                      "om1": [4, 192], "oe1": [4, 192], "yy": [128], "ye": [128]})):
     for _n in _l:
         SCRATCH[_n] = ("sbuf", [128] + _l[_n], _t)
@@ -30,7 +31,7 @@ SEMAPHORES = ["pe", "dve", "act", "gp", "sent", "ac", "lc", "lp", "lt", "lf", "l
 for _c in range(NCH):
     SEMAPHORES += ["a0_%d" % _c, "a1_%d" % _c] + ["m%d_%d" % (_j, _c) for _j in range(3)]
 
-POOLS = {"w": [0, 1, 2], "s": [3, 4], "o": [5, 6, 7]}
+POOLS = {"w": [0, 1, 2], "s": [3, 4, 5], "o": [7, 6, 5]}
 FAR = {}
 
 
@@ -103,15 +104,17 @@ def build(g, T, topo, r, P):
             return V.tensor_scalar(out, in_(), scale, bias, Op.mult, Op.add)
         return add(name, ["dve", "act"], {"dve": max(64, n) * P["cyc"], "act": P["afix"] + n * P["cyc"]}, deps, prio, em, unit=u)
 
-    def pe(name, cyc, deps, fn, u, prio=R):
-        return add(name, "pe", 0.02 + cyc * P["pe"], deps, prio, lambda e: mms(fn()), unit=u)
+    def pe(name, cyc, deps, fn, u, prio=R, part=0):
+        o = add(name, "pe", cyc * P["pe"], deps, prio, lambda e: mms(fn(), part), unit=u)
+        o["free"] = part == 2
+        return o
 
     def gp(n, deps, prio, fn):
         return add("gp", "gp", 0.17 + 2 * n * P["cyc"], deps, prio, lambda e: fn())
 
     def dma(eng, deps, prio, out, in_, sem, tot, at=None):
         return add(sem, eng, 0.05, deps, prio, lambda e: Q[e].dma_start(out, in_).then_inc(T.sem[sem], 16), kind="d",
-                   sem=(sem, tot), lat=2.0, at=at)
+                   sem=(sem, tot), lat=at or 2.0)
 
     def ts(out, a, s1, s2, o0, o1=None):
         if o1 is None:
@@ -121,11 +124,11 @@ def build(g, T, topo, r, P):
     def tt(out, a, b, op):
         return V.tensor_tensor(out, a, b, op)
 
-    def mms(groups):
+    def mms(groups, part):
         last = None
         for grp in groups:
             for i, (o, l, rr) in enumerate(grp):
-                last = g.tensor.matmul(o, l, rr, i == 0, i == len(grp) - 1)
+                last = g.tensor.matmul(o, l, rr, i == 0 and part != 2, i == len(grp) - 1 and part != 1)
         return last
 
     sent = [0]
@@ -151,7 +154,7 @@ def build(g, T, topo, r, P):
             sent[0] += len(topo.engines(me, k))
             return g.remote_dma(dst, src(2), T.sem[sem], T.sem.sent, pid, rid, topo.mask(me, k))
         a = add("F", "gp", P["iss"] + (P["first"] if key == "c" else 0), dfar, prio, far, kind="r")
-        a["key"] = key
+        a["msg"] = key
         return a, add("N", "gp", P["iss"], dnear, prio + 0.01, near, kind="r")
 
     def incs(j):
@@ -159,8 +162,12 @@ def build(g, T, topo, r, P):
 
     def arrive(snd, js, sem, extra=0.0):
         lat = (2 * P["hop"] if min(js) < 2 else P["hop"]) + extra
-        return add("x", "x", 0.0, [snd[0] if min(js) < 2 else snd[1]] + ([snd[1]] if len(js) > 1 else []), 0, None, kind="x",
-                   sem=(sem, sum(incs(j) for j in js)), lat=lat)
+        far, near = [snd[0]] if min(js) < 2 else [], [snd[1]] if max(js) == 2 else []
+        if far and near:
+            near = [add("x", "x", 0.0, near, 0, None, kind="x", sem=None, lat=-P["hop"])]
+        o = add("x", "x", 0.0, far + near, 0, None, kind="x", sem=(sem, sum(incs(j) for j in js)), lat=lat)
+        o["hops"] = 2 if far else 1
+        return o
 
     def sel(out, in_, pat, op, base, cm):
         return lambda: g.affine_select(out, in_, pat, op, 0.0, base, cm)
@@ -173,7 +180,7 @@ def build(g, T, topo, r, P):
     lf = [dma("act", [], 0.5, o, i, "lf", 64, at=P["small"] + 0.3) for o, i in (
         (T.fi[0:16, 0:256], T.fac[0, :]), (T.fi[0:16, 256:512], T.inc[0, :]),
         (T.fi[16:24, 0:256], T.fac[1:3, own]), (T.fi[16:24, 256:512], T.inc[1:3, own]))]
-    ly = [dma("act", [], 0.6, o, i, "ly", 64, at=P["tab"]) for o, i in
+    ly = [dma("sp", [], 0.6, o, i, "ly", 64, at=P["small"] + 0.6) for o, i in
           [(T.fj[0:4, 384:640], T.th[0, own])] + [(T.fj[0:8, 128 * k:128 * k + 128], T.th[k, own]) for k in range(3)]]
 
     def c_(n, deps, prio, fn):
@@ -199,7 +206,6 @@ def build(g, T, topo, r, P):
     gs8 = gp(128, [m1], 6, sel(T.s8[0:8, 0:128], T.ones[0:8, 0:128], [[-2, 4], [0, 16], [-1, 2]], Op.is_equal, 0, 1))
     gsk = gp(256, [m1], 6, sel(T.s8[0:8, 128:384], T.ones[0:8, 0:256], [[-1, 2], [0, 32], [-2, 4]], Op.is_equal, 0, 1))
     gpm = gp(128, [m1], 6, sel(T.pm[:], T.ones[:, 0:128], [[-1, 4], [-4, 32]], Op.is_equal, 0, 1))
-    gnp = shift("c", 128, [gpm], T.npm[:], lambda: T.pm[:], -1.0)
     an = [c_(1, [ip], 2, lambda i=i, v=v: ts(T.pi[:, i:i + 1], T.pi[:, 0:1], v, None, Op.bitwise_and))
           for i, v in ((1, 28), (2, 3), (3, 15), (4, 30))]
     t0 = c_(1, an[0:1], 2, lambda: ts(T.pf[:, 0:1], T.pi[:, 1:2], 4.0, 12.0, Op.mult, Op.add))
@@ -244,7 +250,7 @@ def build(g, T, topo, r, P):
           for f in range(2) for k in range(2)]
 
     def thr(deps, out, in_, sgn):
-        return dv("th", 128, ly + deps, lambda: ts(out, in_, -sgn / 32, 0.5 + sgn / 64, Op.mult, Op.add))
+        return c_(128, ly + deps, 4.7, lambda: ts(out, in_, -sgn / 32, 0.5 + sgn / 64, Op.mult, Op.add))
     tp = [thr([], T.fb[0:4, :, 32 * k:32 * k + 32], T.fj[0:4, 384 + 128 * k:512 + 128 * k], 1) for k in range(2)]
     tf0 = thr([], T.tf0[0:8, :], T.fj[0:8, 0:128], 1)
     tf1 = [thr([z1], T.tf1[0:8, :, a:b:3], T.fj[0:8, 128 * k:128 * k + 128], s)
@@ -253,24 +259,22 @@ def build(g, T, topo, r, P):
     def rnd(o, w):
         return [(o, T.kc[0:1, 256:384], T.ones[0:1, 0:w]), (o, T.kc[0:1, 384:512], T.ones[0:1, 0:w])]
 
-    def masks(parts, deps, bits, out):
+    def masks(parts, deps, bits, out, tag):
         w = sum(p[2] for p in parts)
         u = unit("w")
 
-        def diff():
-            def x(k):
-                l, a = [], 0
-                for j, pos, n in parts:
-                    l.append((ps(u)[:, a:a + n], st(j, k), pos))
-                    a += n
-                return l
-            return [[(ps(u)[:, 0:w], T.kc[0:2, 0:128], T.ones[0:2, 0:w])] + x(2) + x(1) +
-                    [(ps(u)[:, 0:w], T.kc[0:1, 128:256], T.ones[0:1, 0:w])] + x(0)]
-        d = pe("md", 5 * w, deps + kc, diff, u)
-        b = shift("mb", w, [d], bits(0, 1), lambda: ps(u)[:, 0:w], 1.0, -LEFT, u)
-        m = pe("mm", 4 * max(64, w // 4), [b, ww], lambda: [[
+        def x(k):
+            l, a = [], 0
+            for j, pos, n in parts:
+                l.append((ps(u)[:, a:a + n], st(j, k), pos))
+                a += n
+            return l
+        d = pe("md" + tag, 3 * w, deps + kc, lambda: [[(ps(u)[:, 0:w], T.kc[0:2, 0:128], T.ones[0:2, 0:w])] + x(2) + x(1)], u, part=1)
+        d = pe("me" + tag, 2 * w, [d], lambda: [[(ps(u)[:, 0:w], T.kc[0:1, 128:256], T.ones[0:1, 0:w])] + x(0)], u, part=2)
+        b = shift("mb" + tag, w, [d], bits(0, 1), lambda: ps(u)[:, 0:w], 1.0, -LEFT, u)
+        m = pe("mm" + tag, 4 * max(64, w // 4), [b, ww], lambda: [[
             (ps(u)[:, 0:w // 4], T.ww[:, 12 - 4 * s:140 - 4 * s], bits(s, 4)) for s in range(4)]], u)
-        return dv("mc", w // 4, [m], lambda: V.tensor_copy(out, ps(u)[:, 0:w // 4]), u)
+        return dv("mc" + tag, w // 4, [m], lambda: V.tensor_copy(out, ps(u)[:, 0:w // 4]), u)
 
     def gather(name, off, k, out, deps):
         def em(e):
@@ -281,45 +285,51 @@ def build(g, T, topo, r, P):
         c = 16 * k * P["gat"] * P["cyc"]
         return add(name, ["act", "dve"], {"act": 0.07 + c, "dve": 0.05 + c}, deps + [lt], R, em)
 
+    def sums(n, offs, gb, sb, c):
+        cvs = []
+        for js in ([0, 1], [2], [3]):
+            u = unit("s")
+            tag = str(n - 2) + "ffno"[js[0]]
+            sm = []
+            for j in js:
+                off, dep = offs(j)
+                ga = gather("g" + tag, off, 16 * n, gb[:, c, 256 * n * j:256 * n * (j + 1)], dep)
+                sm.append(pe("su" + tag, 128 * n, [ga, ks], lambda u=u, j=j, a=32 * n * (j - js[0]): [
+                    [(ps(u)[:, a + 32 * ev + k:a + 32 * ev + 32:2],
+                      gb[:, c, 256 * n * j + 128 * (2 * ev + k):256 * n * j + 128 * (2 * ev + k + 1)], T.s16[:])]
+                    for ev in range(n) for k in range(2)], u))
+            w, a = 32 * n * len(js), 32 * n * js[0]
+            cvs.append(dv("sc" + tag, w, sm, lambda u=u, w=w, a=a: V.tensor_copy(sb[:, c, a:a + w], ps(u)[:, 0:w]), u))
+        return cvs
+
     J = (3, 0, 1, 2)
     fin = []
 
     def chunk(c):
         cv = dv("cv", 256, lp, lambda: V.tensor_copy(T.xq[:, c, 0:256], T.p32[:, :, 32 * c:32 * c + 32]))
         ub = unit("o")
-        bc = pe("bc", 512, fa + [gs1, cv], lambda: [
+        bc = pe("bc", 512, fa + [gs1] + ([cv] if c > 1 else []), lambda: [
             [(ps(ub)[:, 256 * f + 64 * j:256 * f + 64 * j + 64], T.sel[0:24, 128 * sl[j]:128 * sl[j] + 128], T.fa[0:24, 4 * f + c, :])]
             for f in range(2) for j in range(4)], ub)
-        e = dv("p1", 256, [bc], lambda: tt(T.m0[:, c, :], ps(ub)[:, 0:256], T.xq[:, c, 0:256], Op.mult), ub)
+        e = dv("p1", 256, [bc] + lp, lambda: tt(T.m0[:, c, :], ps(ub)[:, 0:256], T.p32[:, :, 32 * c:32 * c + 32], Op.mult), ub)
         e = dv("p2", 256, [e], lambda: tt(T.xi[:, c, :], ps(ub)[:, 256:512], T.m0[:, c, :], Op.add), ub)
         e = dv("p3", 256, [e], lambda: ts(T.xa[:, c, :], T.xi[:, c, :], 31, None, Op.bitwise_and))
         p0 = dv("p4", 256, [e], lambda: V.tensor_copy(T.xq[:, c, 256:512], T.xa[:, c, :]))
-        mk0 = masks([(3, T.xq[:, c, :], 512)], [p0, S[3]], lambda s, n: T.b0[:, c, s:512:n], T.o0[:, c, :])
-        cvs = []
-        for hf in range(2):
-            u = unit("s")
-            sm = []
-            for ev in range(2):
-                o1 = 64 * ev + 32 * hf
-                ga = gather("g0", T.o0[:, c, o1:o1 + 32], 32, T.g0[:, c, 16 * o1:16 * o1 + 512], [mk0])
-                sm.append(pe("su", 256, [ga, ks], lambda u=u, o1=o1, ev=ev: [
-                    [(ps(u)[:, 64 * jj + 32 * ev + k:64 * jj + 32 * ev + 32:2],
-                      T.g0[:, c, 16 * o1 + 128 * (2 * jj + k):16 * o1 + 128 * (2 * jj + k + 1)], T.s16[:])]
-                    for jj in range(2) for k in range(2)], u))
-            cvs.append(dv("sc", 128, sm, lambda u=u, hf=hf: V.tensor_copy(T.s0[:, c, 128 * hf:128 * hf + 128], ps(u)[:, 0:128]), u))
+        mk0 = [masks([(3, T.xq[:, c, 256 * ev:256 * ev + 256], 256)], [p0 if ev else cv, S[3]],
+                     lambda s, n, ev=ev: T.b0[:, c, 256 * ev + s:256 * ev + 256:n], T.o0[:, 4 * c:4 * c + 4, 16 * ev:16 * ev + 16], "0" + "sp"[ev])
+               for ev in range(2)]
+        cvs = sums(2, lambda j: (T.o0[:, 4 * c + j, :], mk0), T.g0, T.s0, c)
         sn = send("a0_%d" % c, lambda j: T.s0[:, c, 64 * j:64 * j + 64], [cvs[0]], [cvs[1]], 20)
-        dl = dv("dl", 128, [p0], lambda: tt(T.dl[:, c, :], T.xq[:, c, 448:512], T.xq[:, c, 192:256], Op.subtract))
-
-        def src0(j, a, b):
-            return T.s0[:, c, 192 + a:192 + b] if j == 3 else T.l0[:, c, 64 * j + a:64 * j + b]
+        dl = dv("dl", 128, [p0, cv], lambda: tt(T.dl[:, c, :], T.xq[:, c, 448:512], T.xq[:, c, 192:256], Op.subtract))
         u0, up = unit("o"), unit("o")
-        to = pe("to", 512, [arrive(sn, [0, 1, 2], "a0_%d" % c), cvs[1], gpm, gnp], lambda: [
-            [(ps(u0)[:, 0:64], T.pm[:], src0(j, 0, 64)) for j in J] + [(ps(u0)[:, 32:64], T.npm[:], src0(j, 0, 32)) for j in J]], u0)
+        to = pe("to", 256, [arrive(sn, [0, 1, 2], "a0_%d" % c), cvs[2], gpm], lambda: [
+            [(ps(u0)[:, 0:64], T.pm[:], T.s0[:, c, 192:256] if j == 3 else T.l0[:, c, 64 * j:64 * j + 64]) for j in J]], u0)
         co = pe("co", 256, [to, gs2] + fa, lambda: [
             [(ps(up)[:, 64 + 128 * f + 64 * k:128 + 128 * f + 64 * k], T.sel[0:24, 512 + 128 * k:640 + 128 * k], T.fa[0:24, 4 * f + c, :])]
             for f in range(2) for k in range(2)], up)
         tr = dv("tr", 64, [to], lambda: V.transpose(T.r0[:, c, 0:64], ps(u0)[:, 0:64]), u0)
-        ge = dv("ge", 32, [tr], lambda: ts(T.ge0[:, c, :], T.r0[:, c, 32:64], 0.0, None, Op.is_ge))
+        ge = dv("ge", 64, [tr], lambda: tt(T.ge0[:, c, :], T.r0[:, c, 32:64], T.r0[:, c, 0:32], Op.is_ge))
+        d0 = dv("d0", 64, [ge], lambda: tt(T.r0[:, c, 96:128], T.r0[:, c, 32:64], T.r0[:, c, 0:32], Op.subtract))
         zp = pe("zp", 320, [ge, co, cm, gs1] + tp + kc, lambda: [
             [(ps(up)[:, 0:64], T.sel[0:4, 0:128], T.fb[0:4, c, :])] +
             [(ps(up)[:, 32 * k:32 * k + 32], T.cm[:, 128 + 128 * k:256 + 128 * k], T.ge0[:, c, :]) for k in range(2)] +
@@ -327,7 +337,7 @@ def build(g, T, topo, r, P):
         zf = pe("zf", 256, [ge, cm, tf0, gs8] + kc, lambda: [
             [(ps(u0)[:, 64:96], T.s8[0:8, 0:128], T.tf0[0:8, 32 * c:32 * c + 32]), (ps(u0)[:, 64:96], T.cm[:, 0:128], T.ge0[:, c, :])] +
             rnd(ps(u0)[:, 64:96], 32)], u0)
-        f1 = dv("f1", 32, [zf], lambda: tt(T.r0[:, c, 64:96], ps(u0)[:, 64:96], T.r0[:, c, 32:64], Op.mult), u0)
+        f1 = dv("f1", 32, [zf, d0], lambda: tt(T.r0[:, c, 64:96], ps(u0)[:, 64:96], T.r0[:, c, 96:128], Op.mult), u0)
         a0 = dv("a0", 32, [zf, mk, z0], lambda: ts(T.ze[:, c, 2:96:3], ps(u0)[:, 64:96], T.mk[:, 0:1], None, Op.mult), u0)
         f2 = dv("f2", 64, [f1], lambda: tt(T.xx[:, c, 0:32], T.r0[:, c, 64:96], T.r0[:, c, 0:32], Op.add))
         f3 = shift("f3", 32, [f2], T.zm[:, c, 2:96:3], lambda: T.xx[:, c, 0:32])
@@ -341,24 +351,11 @@ def build(g, T, topo, r, P):
         e = dv("q7", 192, [e], lambda: ts(T.yb[:, c, :], T.yi[:, c, :], 31, None, Op.bitwise_and))
         xt = dv("q8", 192, [e], lambda: V.tensor_copy(T.xt[:, c, :], T.yb[:, c, :]))
         mo = [masks([(j, T.xt[:, c, :], 192) for j in (2 * h, 2 * h + 1)], [xt, S[2 * h], S[2 * h + 1]],
-                    lambda s, n, h=h: T.b1[:, c, 384 * h + s:384 * h + 384:n], T.om[:, c, 96 * h:96 * h + 96]) for h in range(2)]
+                    lambda s, n, h=h: T.b1[:, c, 384 * h + s:384 * h + 384:n], T.om[:, c, 96 * h:96 * h + 96], "1" + "fn"[h])
+              for h in range(2)]
         sm_ = send("m_%d" % c, lambda j: T.om[:, c, 48 * j:48 * j + 48], [mo[0]], [mo[1]], 19)
-        cvs = []
-        for js in ([0, 1], [2], [3]):
-            u = unit("s")
-            sm = []
-            for j in js:
-                if j == 3:
-                    off, dep = T.om[:, c, 144:192], mo[1]
-                else:
-                    off, dep = T.ol[:, c, 48 * j:48 * j + 48], arrive(sm_, [j], "m%d_%d" % (j, c))
-                ga = gather("g1", off, 48, T.g1[:, c, 768 * j:768 * j + 768], [dep])
-                sm.append(pe("su", 384, [ga, ks], lambda u=u, j=j, a=96 * (j - js[0]): [
-                    [(ps(u)[:, a + 32 * ev + k:a + 32 * ev + 32:2],
-                      T.g1[:, c, 768 * j + 128 * (2 * ev + k):768 * j + 128 * (2 * ev + k + 1)], T.s16[:])]
-                    for ev in range(3) for k in range(2)], u))
-            w, a = 96 * len(js), 96 * js[0]
-            cvs.append(dv("sc", w, sm, lambda u=u, w=w, a=a: V.tensor_copy(T.s1[:, c, a:a + w], ps(u)[:, 0:w]), u))
+        cvs = sums(3, lambda j: (T.om[:, c, 144:192], [mo[1]]) if j == 3 else
+                   (T.ol[:, c, 48 * j:48 * j + 48], [arrive(sm_, [j], "m%d_%d" % (j, c))]), T.g1, T.s1, c)
         sn1 = send("a1_%d" % c, lambda j: T.s1[:, c, 96 * j:96 * j + 96], [cvs[0]], [cvs[1]], 20)
         u1 = unit("o")
         to1 = pe("to", 384, [arrive(sn1, [0, 1, 2], "a1_%d" % c), cvs[2], gpm], lambda: [
@@ -388,84 +385,220 @@ def build(g, T, topo, r, P):
 
 
 def lay_out(ops, P):
-    free = {e: 0.0 for e in ("pe", "dve", "act", "gp", "sp")}
+    free = {e: 0.0 for e in ("gp", "sp", "pe", "act", "dve")}
     order = {e: [] for e in free}
     holder = [None] * 8
-    left = list(ops)
     for o in ops:
-        o["end"], o["bdeps"], o["up"] = None, [], 0.0
+        o["end"], o["up"], o["outs"], o["left"], o["at"] = None, 0.0, [], len(o["deps"]), 0.0
     for o in reversed(ops):
         o["up"] += min(o["cost"].values()) + o["lat"] + P["lat"]
         for d in o["deps"]:
             d["up"] = max(d["up"], o["up"])
-        if o["p"] is None:
-            v = 1000.0 - o["up"] + P["skew"] * o["c"]
-            ga = o["name"] in ("g0", "g1")
-            o["prio"] = {e: v + (P["d" + o["name"]] if ga and e == "dve" else P["ab"] if e == "act" and not ga else 0.0)
-                         for e in o["eng"]}
-        else:
-            o["prio"] = {e: o["p"] for e in o["eng"]}
-    t = 0.0
+            d["outs"].append(o)
+        o["key"] = o["p"] if o["p"] is not None else 1000.0 + P["skew"] * o["c"] - o["up"]
+    pend = [o for o in ops if not o["deps"]]
     marks = []
-    while left:
+
+    def done(o, t):
+        o["end"] = t
+        marks.append(t + P["lat"])
+        for x in o["outs"]:
+            x["at"] = max(x["at"], t + (0.0 if x.get("free") else P["lat"]))
+            x["left"] -= 1
+            if x["left"] == 0:
+                if x["kind"] == "x":
+                    x["on"] = "x"
+                    done(x, x["at"] + x["lat"])
+                else:
+                    pend.append(x)
+
+    def bank(o, t):
+        u = o["unit"]
+        if u is None or u["bank"] is not None:
+            return -1
+        for k in POOLS[u["pool"]]:
+            if holder[k] is None or all(x["end"] is not None and x["end"] + P["lat"] <= t + 1e-9 for x in holder[k]["ops"]):
+                return k
+        return None
+    t = 0.0
+    while pend:
         did = False
-        for o in [o for o in left if o["kind"] == "x" and all(d["end"] is not None for d in o["deps"])]:
-            o["end"] = max(d["end"] for d in o["deps"]) + o["lat"]
-            o["on"] = "x"
-            marks.append(o["end"] + P["lat"])
-            left.remove(o)
-        ready, soon = [], []
-        for o in left:
-            if o["kind"] != "x" and all(d["end"] is not None for d in o["deps"]):
-                y = max([d["end"] + P["lat"] for d in o["deps"]] + [0.0])
-                if y <= t + 1e-9:
-                    ready.append(o)
-                elif o["kind"] == "c":
-                    soon.append((o, y))
-                    if o["eng"] == ["pe"]:
-                        soon += [(x, y + o["cost"]["pe"] + P["lat"]) for x in o["unit"]["ops"] if len(x["deps"]) == 1 and x["deps"][0] is o]
-        for e in ("gp", "sp", "pe", "act", "dve"):
+        pend.sort(key=lambda o: o["key"])
+        for e in free:
             if free[e] > t + 1e-9:
                 continue
-            best, bank = None, None
-            for o in ready:
-                if o["end"] is not None or e not in o["eng"] or (best is not None and o["prio"][e] >= best["prio"][e]):
-                    continue
-                b = None
-                u = o["unit"]
-                if u is not None and u["bank"] is None:
-                    for k in POOLS[u["pool"]]:
-                        hu = holder[k]
-                        if hu is None or all(x["end"] is not None and x["end"] + P["lat"] <= t + 1e-9 for x in hu["ops"]):
-                            b = k
-                            break
-                    if b is None:
-                        continue
-                best, bank = o, b
-            if best is None:
+            for o in pend:
+                if e in o["eng"] and o["at"] <= t + 1e-9 and bank(o, t) is not None and not (
+                        e == "dve" and len(o["eng"]) > 1 and free["act"] < t + o["cost"][e] * P["own"]):
+                    break
+            else:
                 continue
-            o = best
-            if e in ("dve", "act") and any(e in x["eng"] and x["prio"][e] < o["prio"][e] and y < t + P["look"] * o["cost"][e]
-                                           and (len(x["eng"]) == 1 or e == "act") for x, y in soon):
-                continue
-            if bank is not None:
-                if holder[bank] is not None:
-                    o["bdeps"] = list(holder[bank]["ops"])
-                holder[bank] = o["unit"]
-                o["unit"]["bank"] = bank
-            o["on"] = e
-            o["start"] = t
+            k = bank(o, t)
+            if k >= 0:
+                holder[k], o["unit"]["bank"] = o["unit"], k
+            o["on"], o["start"] = e, t
             free[e] = t + o["cost"][e]
-            o["end"] = free[e] + o["lat"]
-            if o["at"] is not None:
-                o["end"] = max(o["at"], free[e] + 1.5)
+            marks.append(free[e])
             order[e].append(o)
-            marks.extend([free[e], o["end"] + P["lat"]])
-            left.remove(o)
+            pend.remove(o)
+            done(o, free[e] + o["lat"])
             did = True
         if not did:
-            t = min([y for y in marks if y > t + 1e-9] + [t + 1.0])
-    FAR["order"] = [o["key"] for o in order["gp"] if "key" in o]
+            marks[:] = [y for y in marks if y > t + 1e-9]
+            t = min(marks + [t + 1.0])
+    return order
+
+
+def polish(ops, order, P):
+    n = len(ops)
+    sets = P["sets"]
+    deps = [[d["n"] for d in o["deps"]] for o in ops]
+    outs0 = [[d["n"] for d in o["outs"]] for o in ops]
+    free = [bool(o.get("free")) for o in ops]
+    units = [o["unit"] for o in ops if o["unit"] is not None and o["unit"]["ops"][0] is o]
+    uops = [[x["n"] for x in u["ops"]] for u in units]
+    heads = [[x["n"] for x in u["ops"] if not any(d["unit"] is u for d in x["deps"])] for u in units]
+    tails = [[x["n"] for x in u["ops"] if not any(d["unit"] is u for d in x["outs"])] for u in units]
+    uof = {x: i for i in range(len(units)) for x in uops[i]}
+    seq = {e: [o["n"] for o in order[e]] for e in order}
+    on = [o["on"] for o in ops]
+    bank = {k: [i for i in sorted(range(len(units)), key=lambda i: ops[heads[i][0]]["start"]) if units[i]["bank"] == k]
+            for k in range(8)}
+    cost = [[{e: c * (s[0] if o["kind"] == "c" else 1.0) + (s[3] if o["kind"] == "r" else 0.0) for e, c in o["cost"].items()}
+             for o in ops] for s in sets]
+    lat = [[o["lat"] + s[1] * o.get("hops", 0) for o in ops] for s in sets]
+
+    def evaluate():
+        qp, qn, extra, after = [-1] * n, [-1] * n, [()] * n, [()] * n
+        cnt = [len(d) for d in deps]
+        for s in seq.values():
+            for i in range(1, len(s)):
+                qp[s[i]], qn[s[i - 1]] = s[i - 1], s[i]
+                cnt[s[i]] += 1
+        for b in bank.values():
+            for i in range(1, len(b)):
+                for h in heads[b[i]]:
+                    extra[h] = tails[b[i - 1]]
+                    cnt[h] += len(extra[h])
+                for h in tails[b[i - 1]]:
+                    after[h] = heads[b[i]]
+        topo = [i for i in range(n) if cnt[i] == 0]
+        for i in topo:
+            for x in outs0[i]:
+                cnt[x] -= 1
+                if cnt[x] == 0:
+                    topo.append(x)
+            for x in after[i]:
+                cnt[x] -= 1
+                if cnt[x] == 0:
+                    topo.append(x)
+            x = qn[i]
+            if x >= 0:
+                cnt[x] -= 1
+                if cnt[x] == 0:
+                    topo.append(x)
+        if len(topo) < n:
+            return None
+        tot, crit, st0 = 0.0, [], None
+        for s in range(len(sets)):
+            w, cs, ls = sets[s][2], cost[s], lat[s]
+            st, fr, en, why = [0.0] * n, [0.0] * n, [0.0] * n, [-1] * n
+            for i in topo:
+                t, y = -w, -1
+                for d in deps[i]:
+                    if en[d] > t:
+                        t, y = en[d], d
+                for d in extra[i]:
+                    if en[d] > t:
+                        t, y = en[d], d
+                if not free[i]:
+                    t += w
+                q = qp[i]
+                if q >= 0 and fr[q] > t:
+                    t, y = fr[q], q
+                st[i], why[i] = t, y
+                fr[i] = t = t + cs[i][on[i]]
+                en[i] = t + ls[i]
+            top = max(en)
+            i = en.index(top)
+            tot += top + P["tidy"] * sum(en) / n
+            while i >= 0:
+                crit.append((i, why[i]))
+                i = why[i]
+            st0 = st0 or st
+        return tot, crit, st0, qp, extra
+    fixed = set([o["n"] for o in ops if o["kind"] == "d"] + [o["n"] for o in ops if o["kind"] == "r"][:2])
+    seed = [P["seed"]]
+
+    def rnd(k):
+        seed[0] = (seed[0] * 1103515245 + 12345) % 2147483648
+        return (seed[0] >> 8) % k
+    cur = best = evaluate()
+    keep = (seq, on, bank)
+    for it in range(P["moves"]):
+        i, y = cur[1][rnd(len(cur[1]))]
+        if rnd(4) == 0:
+            i = rnd(n)
+            y = cur[3][i]
+        e = on[i]
+        if e == "x" or i in fixed or y in fixed:
+            continue
+        old = (seq, on, bank)
+        kind = rnd(10)
+        if rnd(100) < P["group"]:
+            d = 0.15 * (1 + rnd(4) * rnd(6))
+            i, d, nxt = (i, -d, deps) if rnd(2) or y < 0 else (y, d, outs0)
+            key, grp = list(cur[2]), [i]
+            for x in grp:
+                key[x] += d
+                grp += [z for z in nxt[x] if z not in grp and z not in fixed and abs(cur[2][z] - cur[2][i]) < abs(d) + P["reach"]]
+            seq = {f: sorted(s, key=lambda v: key[v]) for f, s in seq.items()}
+            bank = {b: sorted(s, key=lambda v: key[heads[v][0]]) for b, s in bank.items()}
+        elif len(ops[i]["eng"]) > 1 and kind < 3:
+            f = [x for x in ops[i]["eng"] if x != e][0]
+            t = cur[2][i] - 0.3 * rnd(4)
+            j = len([x for x in seq[f] if cur[2][x] < t])
+            seq, on = dict(seq), list(on)
+            seq[e], seq[f], on[i] = [x for x in seq[e] if x != i], seq[f][:j] + [i] + seq[f][j:], f
+        elif y >= 0 and y in cur[4][i] and kind < 8:
+            u, k, t = uof[i], rnd(8), cur[2][i] - 0.5 * rnd(3)
+            bank = {b: [v for v in bank[b] if v != u] for b in bank}
+            bank[k].insert(len([v for v in bank[k] if cur[2][heads[v][0]] < t]), u)
+        elif y >= 0 and y == cur[3][i]:
+            seq = dict(seq)
+            s = seq[e] = list(seq[e])
+            j = s.index(i)
+            if kind < 7:
+                s.insert(max(0, j - 1 - rnd(3) * rnd(3)), s.pop(j))
+            else:
+                s.insert(j + rnd(4), s.pop(j - 1))
+        else:
+            continue
+        new = evaluate()
+        if new is not None and new[0] <= cur[0] + P["slack"] * (1.0 - it / P["moves"]) * rnd(100) / 100.0:
+            cur = new
+            if cur[0] < best[0]:
+                best, keep = cur, (seq, on, bank)
+        else:
+            seq, on, bank = old
+    FAR["end"] = best[0] / len(sets)
+    return {"seq": keep[0], "on": keep[1], "bank": keep[2], "start": best[2], "heads": heads, "tails": tails}
+
+
+def plan_for(ops, P):
+    if "plan" not in FAR:
+        FAR["plan"] = polish(ops, lay_out(ops, P), P)
+    plan = FAR["plan"]
+    units = [o["unit"] for o in ops if o["unit"] is not None and o["unit"]["ops"][0] is o]
+    for o in ops:
+        o["on"], o["start"], o["bdeps"] = plan["on"][o["n"]], plan["start"][o["n"]], []
+    for k, b in plan["bank"].items():
+        for i, u in enumerate(b):
+            units[u]["bank"] = k
+            for h in plan["heads"][u]:
+                ops[h]["bdeps"] = [ops[x] for x in plan["tails"][b[i - 1]]] if i else []
+    order = FAR["o"] = {e: [ops[i] for i in s] for e, s in plan["seq"].items()}
+    FAR["order"] = [o["msg"] for o in order["gp"] if "msg" in o]
     return order
 
 
@@ -476,13 +609,12 @@ def emit_all(g, T, Q, order, sent):
             if o["kind"] == "c":
                 k += 1
                 o["sem"] = (e, k)
-    allo = sorted([o for e in order for o in order[e]], key=lambda o: (o["start"], o["n"]))
     seen = {e: {} for e in order}
     top = {}
-    for o in allo:
+    for o in [o for e in order for o in order[e]]:
         e = o["on"]
         need = {}
-        for d in o["deps"] + [d for d in o["bdeps"] if d["on"] != e]:
+        for d in ([] if o.get("free") else o["deps"]) + o["bdeps"]:
             s, v = d["sem"]
             need[s] = max(need.get(s, 0), v)
         for s in need:
@@ -503,14 +635,14 @@ def rank_program(g, core, T, topo):
     r = T.rank_of(core)
     if r is not None:
         ops, Q, sent = build(g, T, topo, r, PAR)
-        emit_all(g, T, Q, lay_out(ops, PAR), sent)
+        emit_all(g, T, Q, plan_for(ops, PAR), sent)
         return
     cores, slots, relay = wiring(T, topo)
     for (s, d), k in relay.items():
         if k != core:
             continue
         if "order" not in FAR:
-            lay_out(build(g, T, topo, s, PAR)[0], PAR)
+            plan_for(build(g, T, topo, s, PAR)[0], PAR)
         msg = messages(T, slots[d].index(s))
         got = len(topo.engines(cores[s], core)) // 2
         rid, pid = topo.addr(cores[d], core)

@@ -2,24 +2,29 @@ from concourse.bass import DstId, RemoteDMATransfer
 from concourse.mybir import AluOpType as Op, ActivationFunctionType as Fn
 
 NCH = 4
-PAR = {"cyc": 0.00088, "pe": 0.00044, "afix": 0.07, "lat": 0.11, "gat": 1.56, "hop": 1.8, "iss": 0.5, "pos": 4.2,
-       "tab": 7.6, "small": 2.0, "first": 2.0, "own": 0.6, "skew": 2.0, "sets": [(1.0, 0.0, 0.11, 0.0), (1.15, 0.7, 0.13, 0.3)],
-       "tidy": 0.2, "seed": 2, "moves": 45000, "slack": 0.3, "group": 25, "reach": 3}
+H = 1
+C = NCH // H
+W = 64 * C
+PAR = {"cyc": 0.00088, "pe": 0.00046, "afix": 0.07, "lat": 0.18, "gat": 1.56, "hop": 1.9, "iss": 0.65, "pos": [4.2, 0],
+       "tab": 7.4, "late": 9.0, "turn": 4.0, "small": 2.0, "first": 2.8, "cand": 5.0, "own": 0.6, "skew": 1.4,
+       "sets": [(0.95, 0.0, 0.18, 0.0, 0.95, 1.0, 0.8), (1.05, 1.1, 0.2, 0.45, 1.0, 1.2, 0.6), (1.18, 0.1, 0.22, 0.1, 1.3, 1.05, 0.5),
+                (1.42, 0.3, 0.27, 0.2, 1.88, 1.1, 0.7)],
+       "tidy": 0.15, "seed": 5, "moves": 45000, "slack": 0.2, "group": 15, "reach": 3, "look": 0.4, "tries": 2000, "heat": 0.7,
+       "off": {}, "split": [], "apart": [], "lq": "sp"}
 BIG = 1.5 * 2 ** 23
-LEFT = 3.0 * 2 ** 22 - 54
+LEFT = 3.0 * 2 ** 22 - 56
 
 SCRATCH = {}
 for _t, _l in (
-        ("bfloat16", {"tb": [4096], "fa": [8, 64], "ones": [768], "zz": [528], "wk": [96], "qq": [96], "ns": [64], "eq": [128],
-                      "ss": [1536], "ww": [144], "sel": [768], "fb": [4, 64], "s8": [384], "s16": [16], "pm": [128], "npm": [128],
-                      "cm": [512], "kc": [512],
-                      "al": [384], "tf0": [128], "tf1": [4, 192], "xq": [4, 512], "b0": [4, 512], "g0": [4, 2048],
-                      "b1": [4, 768], "g1": [4, 3072], "xt": [4, 192], "dl": [4, 64], "cu": [4, 128], "ge0": [4, 32],
-                      "ge1": [4, 96], "ze": [4, 192]}),
-        ("float16", {"s0": [4, 256], "l0": [4, 192], "s1": [4, 384], "l1": [4, 288], "m0": [4, 256]}),
+        ("bfloat16", {"tb": [4096], "fa": [4 * C, 64], "ones": [768], "zz": [528], "wk": [96], "qq": [96], "ns": [64], "eq": [128],
+                      "ss": [1536], "ww": [144], "sel": [1024], "fb": [C, 128], "s8": [768], "s16": [16], "pm": [128],
+                      "cm": [512], "kc": [512], "pat": [512], "fd": [64], "fc": [512], "al": [384], "tf0": [32], "tf1": [192],
+                      "xq": [4, 256], "xr": [4, 512], "b0": [4, 512], "g0": [4, 2048], "b1": [4, 768], "g1": [4, 3072],
+                      "xt": [4, 384], "dl": [4, 128], "cu": [4, 128], "ge0": [4, 32], "ge1": [4, 96], "ze": [4, 192]}),
+        ("float16", {"s0": [4, 256], "l0": [4, 192], "s1": [4, 384], "l1": [4, 288], "m0": [4, 256], "xi": [4, 512],
+                     "mi": [4, 192], "yi": [4, 384]}),
         ("uint16", {"o0": [16, 32], "om": [4, 192], "ol": [4, 144]}),
-        ("int32", {"p32": [8, 128], "cs": [4], "cl": [4], "fi": [512], "fj": [640], "pi": [8], "xi": [4, 256], "xa": [4, 256],
-                   "mi": [4, 192], "yi": [4, 192], "yb": [4, 192]}),
+        ("int32", {"p32": [8 * H, 32 * C], "cs": [4], "cl": [4], "fi": [1024], "fj": [512], "fk": [128], "pi": [8]}),
         ("float32", {"cf": [8], "col": [144], "pf": [8], "mk": [4], "r0": [4, 128], "xx": [4, 128], "zm": [4, 192],
                      "om1": [4, 192], "oe1": [4, 192], "yy": [128], "ye": [128]})):
     for _n in _l:
@@ -27,7 +32,7 @@ for _t, _l in (
 for _i in range(8):
     SCRATCH["ps%d" % _i] = ("psum", [128, 512], "float32")
 
-SEMAPHORES = ["pe", "dve", "act", "gp", "sent", "ac", "lc", "lp", "lt", "lf", "ly", "st"]
+SEMAPHORES = ["pe", "dve", "act", "gp", "sent", "ac", "lc", "lp0", "lp1", "lt", "lf", "ly", "lr", "st"]
 for _c in range(NCH):
     SEMAPHORES += ["a0_%d" % _c, "a1_%d" % _c] + ["m%d_%d" % (_j, _c) for _j in range(3)]
 
@@ -73,7 +78,7 @@ def build(g, T, topo, r, P):
     me = cores[r]
     sl = slots[r]
     ops = []
-    cur = [0]
+    cur = [0, "c"]
     Q = {"pe": g.tensor, "dve": g.vector, "act": g.scalar, "gp": g, "sp": g.sync}
     V = g.vector
     R = None
@@ -82,7 +87,8 @@ def build(g, T, topo, r, P):
         if not isinstance(eng, list):
             eng, cost = [eng], {eng: cost}
         o = {"name": name, "eng": eng, "cost": cost, "deps": list(deps), "p": prio, "emit": emit, "unit": unit, "kind": kind,
-             "sem": sem, "lat": lat, "at": at, "n": len(ops), "c": cur[0]}
+             "sem": sem, "lat": lat, "at": at, "n": len(ops), "c": cur[0],
+             "grp": (name[0] + name[-2:] if name[0] in "gm" and len(name) > 2 else "g" + name[-2:] if len(name) > 3 else cur[1], cur[0])}
         if unit is not None:
             unit["ops"].append(o)
         ops.append(o)
@@ -106,7 +112,7 @@ def build(g, T, topo, r, P):
 
     def pe(name, cyc, deps, fn, u, prio=R, part=0):
         o = add(name, "pe", cyc * P["pe"], deps, prio, lambda e: mms(fn(), part), unit=u)
-        o["free"] = part == 2
+        o["free"] = [d for d in deps if d["unit"] is u and d["eng"] == ["pe"] and part > 1]
         return o
 
     def gp(n, deps, prio, fn):
@@ -128,7 +134,7 @@ def build(g, T, topo, r, P):
         last = None
         for grp in groups:
             for i, (o, l, rr) in enumerate(grp):
-                last = g.tensor.matmul(o, l, rr, i == 0 and part != 2, i == len(grp) - 1 and part != 1)
+                last = g.tensor.matmul(o, l, rr, i == 0 and part < 2, i == len(grp) - 1 and part % 2 == 0)
         return last
 
     sent = [0]
@@ -174,14 +180,17 @@ def build(g, T, topo, r, P):
 
     own = slice(1024 * r, 1024 * r + 1024)
     lc = dma("sp", [], 0, T.cs[0:96, 0:1], T.cand[:], "lc", 16, at=P["small"])
-    lp = [dma("sp", [], 1, T.p32[:, 2 * j:2 * j + 2, :], T.pos0[:, 1024 * sl[j]:1024 * sl[j] + 1024], "lp", 64, at=P["pos"])
-          for j in range(4)]
+    lp = [[dma("sp", [], 1 + 2 * h, T.p32[:, 8 * h + 2 * j:8 * h + 2 * j + 2, :],
+               T.pos0[:, 1024 * sl[j] + 4 * W * h:1024 * sl[j] + 4 * W * (h + 1)], "lp%d" % h, 64, at=P["pos"][h])
+           for j in range(4)] for h in range(H)]
     lt = dma("sp", [], 2, T.tb[:], T.tab[:], "lt", 16, at=P["tab"])
-    lf = [dma("act", [], 0.5, o, i, "lf", 64, at=P["small"] + 0.3) for o, i in (
-        (T.fi[0:16, 0:256], T.fac[0, :]), (T.fi[0:16, 256:512], T.inc[0, :]),
-        (T.fi[16:24, 0:256], T.fac[1:3, own]), (T.fi[16:24, 256:512], T.inc[1:3, own]))]
-    ly = [dma("sp", [], 0.6, o, i, "ly", 64, at=P["small"] + 0.6) for o, i in
-          [(T.fj[0:4, 384:640], T.th[0, own])] + [(T.fj[0:8, 128 * k:128 * k + 128], T.th[k, own]) for k in range(3)]]
+    lf = [dma("sp", [], 0.5, o, i, "lf", 32, at=P["small"]) for o, i in (
+        (T.fi[0:16 * H, 0:W], T.fac[0, :]), (T.fi[0:16 * H, W:2 * W], T.inc[0, :]))]
+    ly = [dma(P["lq"], [], -1 if P["lq"] == "act" else 3.5, o, i, "ly", 160, at=P["late"]) for o, i in
+          [(T.fi[0:8 * H, 2 * W:3 * W], T.fac[1:3, own]), (T.fi[0:8 * H, 3 * W:4 * W], T.inc[1:3, own]),
+           (T.fj[0:4 * H, 256:256 + W], T.th[0, own])] +
+          [(T.fj[0:32, 32 * k:32 * k + 32], T.th[k, own]) for k in range(3)] +
+          [(T.fj[0:32, 96 + 32 * k:128 + 32 * k], (T.fac, T.inc)[k % 2][1 + k // 2, own]) for k in range(4)]]
 
     def c_(n, deps, prio, fn):
         return dv("c", n, deps, fn, prio=prio)
@@ -190,21 +199,30 @@ def build(g, T, topo, r, P):
         return c_(n, deps, prio, lambda: V.memset(ap, val))
     mc = fill(T.cs[96:128, :], 1, 0, 0)
     m1 = fill(T.ones[:], 384, 1.0, 0.1)
+
+    def fil2(ap, p, n, val, prio, deps=(), w=0.5):
+        def em(e):
+            if e == "act":
+                return g.scalar.activation(ap, T.ones[0:p, 0:n], Fn.Identity, scale=val)
+            return V.memset(ap, val) if isinstance(val, float) else ts(ap, T.ones[0:p, 0:n], val, None, Op.mult)
+        return add("c", ["dve", "act"], {"dve": max(64, n * w) * P["cyc"], "act": P["afix"] + n * P["cyc"]}, [m1] + list(deps), prio, em)
     wk = [fill(T.wk[0:96, 32 * k:32 * k + 32], 1, 2.0 ** k / 32, 0.2) for k in range(3)]
-    mz = fill(T.zz[:], 264, 0.0, 1)
-    al = [fill(T.al[0:1, 128 * k:128 * k + 128], 64, 2.0 ** k / 32 * (1 / 128 - (0.5 if k == 1 else 0.0)), 1) for k in range(3)]
-    k0 = fill(T.kc[0:2, 0:128], 64, 8.0, 1.5)
-    kc = [fill(T.kc[0:1, 0:128], 64, 2.0 ** 25, 1.5, [k0])] + [
-        fill(T.kc[0:1, 128 * i:128 * i + 128], 64, v, 1.5) for i, v in ((1, -5.0 * 2 ** 22), (2, BIG), (3, -BIG))] + [m1]
+    mz = fil2(T.zz[:], 128, 528, 0.0, 1)
+    al = [fil2(T.al[0:1, 128 * k:128 * k + 128], 1, 128, 2.0 ** k / 32 * ((0.5 if k == 1 else 0.0) - 1 / 128), 1) for k in range(3)]
+    k0 = fil2(T.kc[0:2, 0:128], 2, 128, 8.0, 1.5)
+    kc = [fil2(T.kc[0:1, 0:128], 1, 128, 2.0 ** 25, 1.5, [k0])] + [
+        fil2(T.kc[0:1, 128 * i:128 * i + 128], 1, 128, v, 1.5) for i, v in ((1, -5.0 * 2 ** 22), (2, BIG), (3, -BIG))] + [m1]
+    pat = [fil2(T.pat[:, i:512:2], 128, 256, -1.0 * i, 1.6) for i in range(2)]
     icol = gp(144, [], 0, lambda: g.iota(T.col[:], [[1, 144]], 0, 0, allow_small_or_imprecise_dtypes=True))
     ip = gp(1, [], 0.1, lambda: g.iota(T.pi[:, 0:1], [[0, 1]], 0, 1))
     gn1 = gp(56, [m1], 1, sel(T.ns[0:96, 0:56], T.ones[0:96, 0:56], [[-12, 56]], Op.is_ge, 288, 1))
     gq = gp(96, wk, 1.1, sel(T.qq[0:96, :], T.wk[0:96, :], [[-1, 3], [-3, 4], [-12, 8]], Op.is_equal, 0, 1))
     gns = gp(56, [gn1], 1.2, sel(T.ns[0:96, 0:56], T.ns[0:96, 0:56], [[12, 56]], Op.is_ge, -277, -1))
-    gs1 = gp(512, [m1], 1.3, sel(T.sel[0:24, 0:512], T.ones[0:24, 0:512], [[-4, 4], [0, 32], [-1, 4]], Op.is_equal, 0, 1))
-    gs2 = gp(256, [m1], 6, sel(T.sel[0:24, 512:768], T.ones[0:24, 0:256], [[-4, 2], [0, 32], [-1, 4]], Op.is_equal, -16, 1))
-    gs8 = gp(128, [m1], 6, sel(T.s8[0:8, 0:128], T.ones[0:8, 0:128], [[-2, 4], [0, 16], [-1, 2]], Op.is_equal, 0, 1))
-    gsk = gp(256, [m1], 6, sel(T.s8[0:8, 128:384], T.ones[0:8, 0:256], [[-1, 2], [0, 32], [-2, 4]], Op.is_equal, 0, 1))
+    gs1 = [gp(512, [m1], 1.3 + 4 * h, sel(T.sel[0:32, 512 * h:512 * h + 512], T.ones[0:32, 0:512], [[-4 * H, 4], [0, 32], [-1, 4]],
+                                          Op.is_equal, -4 * h, 1)) for h in range(H)]
+    gs8 = [gp(128, [m1], 6, sel(T.s8[0:32, 384 - 128 * c:512 - 128 * c], T.ones[0:32, 0:128], [[-2 * C, 4], [0, 16], [-C, 2]],
+                                Op.is_equal, -8 * C * (c // C) - c % C, 1)) for c in range(NCH)]
+    gsk = gp(256, [m1], 6, sel(T.s8[0:32, 512:768], T.ones[0:32, 0:256], [[-C, 2], [0, 32], [-2 * C, 4]], Op.is_equal, 0, 1))
     gpm = gp(128, [m1], 6, sel(T.pm[:], T.ones[:, 0:128], [[-1, 4], [-4, 32]], Op.is_equal, 0, 1))
     an = [c_(1, [ip], 2, lambda i=i, v=v: ts(T.pi[:, i:i + 1], T.pi[:, 0:1], v, None, Op.bitwise_and))
           for i, v in ((1, 28), (2, 3), (3, 15), (4, 30))]
@@ -215,21 +233,20 @@ def build(g, T, topo, r, P):
     ww = c_(144, [icol, t1] + wq, 3, lambda: ts(T.ww[:], T.col[:], T.pf[:, 1:2], T.pf[:, 4:5], Op.is_equal, Op.mult))
     ks = c_(16, [icol, t2], 4, lambda: ts(T.s16[:], T.col[:, 0:16], T.pf[:, 2:3], None, Op.is_equal))
     mk = c_(3, [icol, t2], 4, lambda: ts(T.mk[:, 0:3], T.col[:, 0:6:2], T.pf[:, 3:4], None, Op.is_equal))
-    z0 = fill(T.ze[:], 384, 0.0, 4.5)
-    ze = [c_(128, [z0, mk, m1], 4.6, lambda: ts(T.ze[:, :, 0:192:3], T.ones[:, 0:256], T.mk[:, 2:3], None, Op.mult)),
-          c_(64, [z0, mk, m1], 4.6, lambda: ts(T.ze[:, :, 97:192:3], T.ones[:, 0:128], T.mk[:, 1:2], None, Op.mult))]
-    zm = [fill(T.zm[:, :, 1:96:3], 128, 0.0, 4.6), fill(T.zm[:, :, 98:192:3], 128, 0.0, 4.6)]
-    z1 = fill(T.tf1[0:8, :, :], 384, 0.0, 4.6)
+    ze = [fil2(T.ze[:, :, 0:192:3], 128, 256, T.mk[:, 2:3], 4.6, [mk]), fil2(T.ze[:, :, 97:192:3], 128, 128, T.mk[:, 1:2], 4.6, [mk])]
+    zm = [fil2(z[:, :, a:b:3], 128, 128, 0.0, 4.6, w=1.0) for z in (T.zm, T.ze) for a, b in ((1, 96), (98, 192))]
+    z1 = fil2(T.tf1[0:32, 0:192:3], 32, 64, 0.0, 4.6)
     u = unit("w")
-    m = pe("cm", 384, [gs8, gsk], lambda u=u: [[(ps(u)[:, 0:384], T.s8[0:8, 0:128], T.s8[0:8, 0:384])]], u)
+    m = pe("cm", 384, [gs8[0], gsk], lambda u=u: [[(ps(u)[:, 0:384], T.s8[0:32, 384:512], T.s8[0:32, 384:768])]], u)
     cm = shift("c", 384, [m], T.cm[:, 0:384], lambda u=u: ps(u)[:, 0:384], 1 / 32, u=u)
     ncm = shift("c", 128, [cm], T.cm[:, 384:512], lambda: T.cm[:, 0:128], -1.0)
 
     sc = send("c", lambda j: T.cs[:, 0:1], [lc, mc], [lc, mc], 3)
-    ac = arrive(sc, [0, 1, 2], "ac", P["first"])
+    ac = arrive(sc, [0, 1, 2], "ac", P["cand"])
     cfo = c_(1, [lc], 1.5, lambda: V.tensor_copy(T.cf[0:96, 4:5], T.cs[0:96, 0:1]))
     cfr = c_(3, [ac], R, lambda: V.tensor_copy(T.cf[0:96, 0:3], T.cl[0:96, 0:3]))
     S = []
+    cur[1] = "s"
     for j in range(4):
         pr = 1.6 if j == 3 else R
         b, i = 132 * j, j + j // 3
@@ -245,21 +262,35 @@ def build(g, T, topo, r, P):
     def st(j, k):
         return T.ss[:, 384 * j + 128 * k:384 * j + 128 * k + 128]
 
-    fa = [c_(128, lf, 4, lambda f=f, k=k: V.tensor_copy(T.fa[0:24, 4 * f:4 * f + 4, 32 * k:32 * k + 32],
-                                                        T.fi[0:24, 256 * f + 128 * k:256 * f + 128 * k + 128]))
-          for f in range(2) for k in range(2)]
+    cur[1] = "t"
+    fa = [[c_(W // 2, ly if s else lf, R if s else 1.4, lambda s=s, f=f, k=k: ts(
+        T.fa[0:(16 - 8 * s) * H, C * (2 * s + f):C * (2 * s + f + 1), 32 * k:32 * k + 32],
+        T.fi[0:(16 - 8 * s) * H, W * (4 * s + 2 * f + k) // 2:W * (4 * s + 2 * f + k + 1) // 2], 16.5 * f, None, Op.add))
+        for f in range(2) for k in range(2)] for s in range(2)]
 
-    def thr(deps, out, in_, sgn):
-        return c_(128, ly + deps, 4.7, lambda: ts(out, in_, -sgn / 32, 0.5 + sgn / 64, Op.mult, Op.add))
-    tp = [thr([], T.fb[0:4, :, 32 * k:32 * k + 32], T.fj[0:4, 384 + 128 * k:512 + 128 * k], 1) for k in range(2)]
-    tf0 = thr([], T.tf0[0:8, :], T.fj[0:8, 0:128], 1)
-    tf1 = [thr([z1], T.tf1[0:8, :, a:b:3], T.fj[0:8, 128 * k:128 * k + 128], s)
-           for a, b, k, s in ((1, 96, 2, 1), (97, 192, 2, 1), (2, 96, 1, -1), (98, 192, 1, 1))]
+    def thr(n, out, in_, sgn):
+        return c_(n, ly, R, lambda: ts(out, in_, -sgn / 32, 0.5 + sgn / 64, Op.mult, Op.add))
+    tp = [thr(W // 2, T.fb[0:4 * H, :, 64 * k + 1:64 * k + 64:2], T.fj[0:4 * H, 256 + W * k // 2:256 + W * (k + 1) // 2], 1)
+          for k in range(2)] + [fil2(T.fb[0:4 * H, :, 0:128:2], 4 * H, W, 0.0, 4.6)]
+    tf0 = thr(32, T.tf0[0:32, :], T.fj[0:32, 0:32], 1)
+    tf1 = [z1] + [thr(32, T.tf1[0:32, a:b:3], T.fj[0:32, 32 * k:32 * k + 32], s)
+                  for a, b, k, s in ((1, 96, 2, 1), (97, 192, 2, 1), (2, 96, 1, -1), (98, 192, 1, 1))]
+    h = [c_(64, ly, R, lambda i=i: tt(T.fk[0:32, 32 * i:32 * i + 32], T.fj[0:32, 96 + 32 * i:128 + 32 * i], T.fj[0:32, 160:192], Op.mult))
+         for i in range(2)]
+    h[1] = c_(64, h[1:], R, lambda: tt(T.fk[0:32, 32:64], T.fk[0:32, 32:64], T.fj[0:32, 192:224], Op.add))
+    h = c_(64, h, R, lambda: ts(T.fk[0:32, 64:128], T.fk[0:32, 0:64], 31, None, Op.bitwise_and))
+    h = [c_(32, [h], R, lambda i=i: ts(T.fd[0:32, 32 * i:32 * i + 32], T.fk[0:32, 64 + 32 * i:96 + 32 * i], 16.5 * i, None, Op.add))
+         for i in range(2)]
+    fc = [dma("sp", h, 4, T.fc[0:4 * H, W * i:W * i + W], T.fd[0:32, 32 * i:32 * i + 32], "lr", 32, at=P["turn"]) for i in range(2)]
+
+    def wrap(tag, x, out, n, deps):
+        e = dv(tag + "y", n // 2, deps + pat, lambda: ts(x(1), x(0), 2.0 ** 28, 2.0 ** 28 - 16, Op.add, Op.subtract))
+        return dv(tag + "z", n, [e], lambda: V.tensor_tensor_scan(out, T.pat[:, 0:2 * n], x(None), 0.0, Op.mult, Op.subtract))
 
     def rnd(o, w):
         return [(o, T.kc[0:1, 256:384], T.ones[0:1, 0:w]), (o, T.kc[0:1, 384:512], T.ones[0:1, 0:w])]
 
-    def masks(parts, deps, bits, out, tag):
+    def masks(parts, early, deps, bits, out, tag):
         w = sum(p[2] for p in parts)
         u = unit("w")
 
@@ -269,7 +300,8 @@ def build(g, T, topo, r, P):
                 l.append((ps(u)[:, a:a + n], st(j, k), pos))
                 a += n
             return l
-        d = pe("md" + tag, 3 * w, deps + kc, lambda: [[(ps(u)[:, 0:w], T.kc[0:2, 0:128], T.ones[0:2, 0:w])] + x(2) + x(1)], u, part=1)
+        d = pe("mi" + tag, w, early + kc, lambda: [[(ps(u)[:, 0:w], T.kc[0:2, 0:128], T.ones[0:2, 0:w])]], u, part=1)
+        d = pe("md" + tag, 2 * w, deps + [d], lambda: [x(2) + x(1)], u, part=3)
         d = pe("me" + tag, 2 * w, [d], lambda: [[(ps(u)[:, 0:w], T.kc[0:1, 128:256], T.ones[0:1, 0:w])] + x(0)], u, part=2)
         b = shift("mb" + tag, w, [d], bits(0, 1), lambda: ps(u)[:, 0:w], 1.0, -LEFT, u)
         m = pe("mm" + tag, 4 * max(64, w // 4), [b, ww], lambda: [[
@@ -306,57 +338,67 @@ def build(g, T, topo, r, P):
     fin = []
 
     def chunk(c):
-        cv = dv("cv", 256, lp, lambda: V.tensor_copy(T.xq[:, c, 0:256], T.p32[:, :, 32 * c:32 * c + 32]))
+        cur[1] = "p"
+        hh, cc = c // C, c % C
+        pos = T.p32[:, 8 * hh:8 * hh + 8, 32 * cc:32 * cc + 32]
+
+        def row(n, i):
+            return T.sel[0:n, 512 * hh + 128 * i:512 * hh + 128 * i + 128]
+        cv = dv("cv", 256, lp[hh], lambda: ts(T.xq[:, c, :], pos, -31.5, None, Op.add))
         ub = unit("o")
-        bc = pe("bc", 512, fa + [gs1] + ([cv] if c > 1 else []), lambda: [
-            [(ps(ub)[:, 256 * f + 64 * j:256 * f + 64 * j + 64], T.sel[0:24, 128 * sl[j]:128 * sl[j] + 128], T.fa[0:24, 4 * f + c, :])]
+        bc = pe("bc", 512, fa[0] + [gs1[hh]] + ([cv] if c > 1 else []), lambda: [
+            [(ps(ub)[:, 256 * f + 64 * j:256 * f + 64 * j + 64], row(16 * H, sl[j]), T.fa[0:16 * H, C * f + cc, :])]
             for f in range(2) for j in range(4)], ub)
-        e = dv("p1", 256, [bc] + lp, lambda: tt(T.m0[:, c, :], ps(ub)[:, 0:256], T.p32[:, :, 32 * c:32 * c + 32], Op.mult), ub)
-        e = dv("p2", 256, [e], lambda: tt(T.xi[:, c, :], ps(ub)[:, 256:512], T.m0[:, c, :], Op.add), ub)
-        e = dv("p3", 256, [e], lambda: ts(T.xa[:, c, :], T.xi[:, c, :], 31, None, Op.bitwise_and))
-        p0 = dv("p4", 256, [e], lambda: V.tensor_copy(T.xq[:, c, 256:512], T.xa[:, c, :]))
-        mk0 = [masks([(3, T.xq[:, c, 256 * ev:256 * ev + 256], 256)], [p0 if ev else cv, S[3]],
+        e = dv("p1", 256, [bc] + lp[hh], lambda: tt(T.m0[:, c, :], ps(ub)[:, 0:256], pos, Op.mult), ub)
+        e = dv("p2", 256, [e], lambda: tt(T.xi[:, c, 0:512:2], ps(ub)[:, 256:512], T.m0[:, c, :], Op.add), ub)
+        p0 = wrap("p", lambda i: T.xi[:, c, :] if i is None else T.xi[:, c, i:512:2], T.xr[:, c, :], 256, [e])
+        mk0 = [masks([(3, T.xr[:, c, 1:512:2] if ev else T.xq[:, c, :], 256)], [e if ev else cv], [p0 if ev else cv, S[3]],
                      lambda s, n, ev=ev: T.b0[:, c, 256 * ev + s:256 * ev + 256:n], T.o0[:, 4 * c:4 * c + 4, 16 * ev:16 * ev + 16], "0" + "sp"[ev])
                for ev in range(2)]
         cvs = sums(2, lambda j: (T.o0[:, 4 * c + j, :], mk0), T.g0, T.s0, c)
         sn = send("a0_%d" % c, lambda j: T.s0[:, c, 64 * j:64 * j + 64], [cvs[0]], [cvs[1]], 20)
-        dl = dv("dl", 128, [p0, cv], lambda: tt(T.dl[:, c, :], T.xq[:, c, 448:512], T.xq[:, c, 192:256], Op.subtract))
+        dl = [dv("dl", 128, [p0, cv], lambda: tt(T.dl[:, c, 0:128:2], T.xr[:, c, 385:512:2], T.xq[:, c, 192:256], Op.subtract)),
+              shift("dp", 64, [cv], T.dl[:, c, 1:128:2], lambda: T.xq[:, c, 192:256], 1.0, 31.5)]
+        cur[1] = "d"
         u0, up = unit("o"), unit("o")
         to = pe("to", 256, [arrive(sn, [0, 1, 2], "a0_%d" % c), cvs[2], gpm], lambda: [
             [(ps(u0)[:, 0:64], T.pm[:], T.s0[:, c, 192:256] if j == 3 else T.l0[:, c, 64 * j:64 * j + 64]) for j in J]], u0)
-        co = pe("co", 256, [to, gs2] + fa, lambda: [
-            [(ps(up)[:, 64 + 128 * f + 64 * k:128 + 128 * f + 64 * k], T.sel[0:24, 512 + 128 * k:640 + 128 * k], T.fa[0:24, 4 * f + c, :])]
-            for f in range(2) for k in range(2)], up)
+        co = pe("co", 512, [cvs[2], gs1[hh]] + fa[1] + fc, lambda: [
+            [(ps(up)[:, 128 + 192 * f + 64 * k:192 + 192 * f + 64 * k], row(8 * H, k), T.fa[0:8 * H, C * (2 + f) + cc, :])]
+            for f in range(2) for k in range(2)] + [
+            [(ps(up)[:, 256 + 192 * f + 32 * k:288 + 192 * f + 32 * k], row(4 * H, 0),
+              T.fc[0:4 * H, W * (2 * f + k) // 2 + 32 * cc:W * (2 * f + k) // 2 + 32 * cc + 32])] for f in range(2) for k in range(2)], up)
         tr = dv("tr", 64, [to], lambda: V.transpose(T.r0[:, c, 0:64], ps(u0)[:, 0:64]), u0)
         ge = dv("ge", 64, [tr], lambda: tt(T.ge0[:, c, :], T.r0[:, c, 32:64], T.r0[:, c, 0:32], Op.is_ge))
         d0 = dv("d0", 64, [ge], lambda: tt(T.r0[:, c, 96:128], T.r0[:, c, 32:64], T.r0[:, c, 0:32], Op.subtract))
-        zp = pe("zp", 320, [ge, co, cm, gs1] + tp + kc, lambda: [
-            [(ps(up)[:, 0:64], T.sel[0:4, 0:128], T.fb[0:4, c, :])] +
-            [(ps(up)[:, 32 * k:32 * k + 32], T.cm[:, 128 + 128 * k:256 + 128 * k], T.ge0[:, c, :]) for k in range(2)] +
-            rnd(ps(up)[:, 0:64], 64)], up)
-        zf = pe("zf", 256, [ge, cm, tf0, gs8] + kc, lambda: [
-            [(ps(u0)[:, 64:96], T.s8[0:8, 0:128], T.tf0[0:8, 32 * c:32 * c + 32]), (ps(u0)[:, 64:96], T.cm[:, 0:128], T.ge0[:, c, :])] +
+        zp = pe("zi", 128, [co] + tp, lambda: [[(ps(up)[:, 0:128], row(4 * H, 0), T.fb[0:4 * H, cc, :])]], up, part=1)
+        zp = pe("zp", 256, [ge, zp, cm] + kc, lambda: [
+            [(ps(up)[:, 64 * k + 1:64 * k + 64:2], T.cm[:, 128 + 128 * k:256 + 128 * k], T.ge0[:, c, :]) for k in range(2)] +
+            rnd(ps(up)[:, 1:128:2], 64)], up, part=4)
+        cur[1] = "z"
+        s8 = T.s8[0:32, 384 - 128 * c:512 - 128 * c]
+        zf = pe("zf", 256, [ge, cm, tf0, gs8[c]] + kc, lambda: [
+            [(ps(u0)[:, 64:96], s8, T.tf0[0:32, :]), (ps(u0)[:, 64:96], T.cm[:, 0:128], T.ge0[:, c, :])] +
             rnd(ps(u0)[:, 64:96], 32)], u0)
         f1 = dv("f1", 32, [zf, d0], lambda: tt(T.r0[:, c, 64:96], ps(u0)[:, 64:96], T.r0[:, c, 96:128], Op.mult), u0)
-        a0 = dv("a0", 32, [zf, mk, z0], lambda: ts(T.ze[:, c, 2:96:3], ps(u0)[:, 64:96], T.mk[:, 0:1], None, Op.mult), u0)
+        a0 = shift("a0", 32, [f1, mk], T.ze[:, c, 2:96:3], lambda: ps(u0)[:, 64:96], T.mk[:, 0:1], u=u0)
         f2 = dv("f2", 64, [f1], lambda: tt(T.xx[:, c, 0:32], T.r0[:, c, 64:96], T.r0[:, c, 0:32], Op.add))
         f3 = shift("f3", 32, [f2], T.zm[:, c, 2:96:3], lambda: T.xx[:, c, 0:32])
-        e = dv("q1", 64, [zp, dl], lambda: tt(T.cu[:, c, 0:64], ps(up)[:, 0:64], T.dl[:, c, :], Op.mult), up)
-        e = dv("q2", 128, [e], lambda: tt(T.cu[:, c, 64:128], T.cu[:, c, 0:64], T.xq[:, c, 192:256], Op.add))
-        q3 = [dv("q3", 64, [e], lambda k=k: tt(T.mi[:, c, 64 * k:64 * k + 64], ps(up)[:, 64 + 64 * k:128 + 64 * k], T.cu[:, c, 64:128],
-                                               Op.mult), up) for k in range(2)]
-        e = dv("q4", 128, q3, lambda: tt(T.yi[:, c, 0:128], ps(up)[:, 192:320], T.mi[:, c, 0:128], Op.add), up)
-        e = dv("q5", 64, [e], lambda: tt(T.mi[:, c, 128:192], ps(up)[:, 128:192], T.yi[:, c, 0:64], Op.mult), up)
-        e = dv("q6", 64, [e], lambda: tt(T.yi[:, c, 128:192], ps(up)[:, 256:320], T.mi[:, c, 128:192], Op.add), up)
-        e = dv("q7", 192, [e], lambda: ts(T.yb[:, c, :], T.yi[:, c, :], 31, None, Op.bitwise_and))
-        xt = dv("q8", 192, [e], lambda: V.tensor_copy(T.xt[:, c, :], T.yb[:, c, :]))
-        mo = [masks([(j, T.xt[:, c, :], 192) for j in (2 * h, 2 * h + 1)], [xt, S[2 * h], S[2 * h + 1]],
-                    lambda s, n, h=h: T.b1[:, c, 384 * h + s:384 * h + 384:n], T.om[:, c, 96 * h:96 * h + 96], "1" + "fn"[h])
-              for h in range(2)]
-        sm_ = send("m_%d" % c, lambda j: T.om[:, c, 48 * j:48 * j + 48], [mo[0]], [mo[1]], 19)
-        cvs = sums(3, lambda j: (T.om[:, c, 144:192], [mo[1]]) if j == 3 else
+        cur[1] = "d"
+        e = dv("q1", 128, [zp] + dl, lambda: V.tensor_tensor_scan(T.cu[:, c, :], ps(up)[:, 0:128], T.dl[:, c, :], 0.0, Op.mult, Op.add), up)
+        q3 = [dv("q3", 64, [e], lambda k=k: tt(T.mi[:, c, 64 * k:64 * k + 64], ps(up)[:, 128 + 64 * k:192 + 64 * k], T.cu[:, c, 1:128:2],
+                                               Op.mult), up) for k in range(3)]
+        e = dv("q4", 192, q3, lambda: tt(T.yi[:, c, 0:384:2], ps(up)[:, 320:512], T.mi[:, c, :], Op.add), up)
+        xt = wrap("q", lambda i: T.yi[:, c, :] if i is None else T.yi[:, c, i:384:2], T.xt[:, c, :], 192, [e])
+        mo = [masks([(j, T.xt[:, c, 1:384:2], 192) for j in js], [e], [xt] + [S[j] for j in js],
+                    lambda s, n, js=js: T.b1[:, c, 192 * js[0] + s:192 * js[-1] + 192:n], T.om[:, c, 48 * js[0]:48 * js[-1] + 48],
+                    "1" + "ffno"[js[0]]) for js in ([[0], [1]] if c in P["apart"] else [[0, 1]]) + ([[2], [3]] if c in P["split"] else [[2, 3]])]
+        nf = 2 if c in P["apart"] else 1
+        sm_ = send("m_%d" % c, lambda j: T.om[:, c, 48 * j:48 * j + 48], mo[0:nf], [mo[nf]], 19)
+        cvs = sums(3, lambda j: (T.om[:, c, 144:192], [mo[-1]]) if j == 3 else
                    (T.ol[:, c, 48 * j:48 * j + 48], [arrive(sm_, [j], "m%d_%d" % (j, c))]), T.g1, T.s1, c)
         sn1 = send("a1_%d" % c, lambda j: T.s1[:, c, 96 * j:96 * j + 96], [cvs[0]], [cvs[1]], 20)
+        cur[1] = "e"
         u1 = unit("o")
         to1 = pe("to", 384, [arrive(sn1, [0, 1, 2], "a1_%d" % c), cvs[2], gpm], lambda: [
             [(ps(u1)[:, 0:96], T.pm[:], T.s1[:, c, 288:384] if j == 3 else T.l1[:, c, 96 * j:96 * j + 96]) for j in J]], u1)
@@ -365,12 +407,12 @@ def build(g, T, topo, r, P):
         gb = dv("ge", 64, [tr1, f2], lambda: tt(T.ge1[:, c, 0:32], T.xx[:, c, 32:64], T.xx[:, c, 0:32], Op.is_ge))
         da = dv("df", 128, [ga], lambda: tt(T.zm[:, c, 0:192:3], T.xx[:, c, 64:128], T.xx[:, c, 0:64], Op.subtract))
         db = dv("df", 64, [gb], lambda: tt(T.zm[:, c, 97:192:3], T.xx[:, c, 32:64], T.xx[:, c, 0:32], Op.subtract))
-        zq = pe("zq", 768, [ga, gb, cm, ncm, gs8] + tf1 + kc, lambda: [
-            [(ps(u1)[:, 128:320], T.s8[0:8, 0:128], T.tf1[0:8, c, :]),
-             (ps(u1)[:, 129:320:3], T.cm[:, 0:128], T.ge1[:, c, 32:96]),
-             (ps(u1)[:, 226:320:3], T.cm[:, 0:128], T.ge1[:, c, 0:32]),
-             (ps(u1)[:, 130:224:3], T.cm[:, 384:512], T.ge1[:, c, 0:32])] + rnd(ps(u1)[:, 128:320], 192)], u1)
-        for o, d, y, dep in ((T.om1, T.zm, T.yy, [da, db, f3] + zm), (T.oe1, T.ze, T.ye, [a0] + ze)):
+        zq = pe("zj", 192, [tr1, gs8[c]] + tf1, lambda: [[(ps(u1)[:, 128:320], s8, T.tf1[0:32, :])]], u1, part=1)
+        zq = pe("zq", 448, [ga, gb, zq, cm, ncm] + kc, lambda: [
+            [(ps(u1)[:, 129:320:3], T.cm[:, 0:128], T.ge1[:, c, 32:96])] + rnd(ps(u1)[:, 129:320:3], 64) +
+            [(ps(u1)[:, 226:320:3], T.cm[:, 0:128], T.ge1[:, c, 0:32]),
+             (ps(u1)[:, 130:224:3], T.cm[:, 384:512], T.ge1[:, c, 0:32])] + rnd(ps(u1)[:, 130:320:3], 64)], u1, part=4)
+        for o, d, y, dep in ((T.om1, T.zm, T.yy, [da, db, f3] + zm), (T.oe1, T.ze, T.ye, [a0] + ze + zm)):
             e = dv("sn", 192, [zq] + dep, lambda o=o, d=d: V.tensor_tensor_scan(o[:, c, :], ps(u1)[:, 128:320], d[:, c, :], 0.0,
                                                                                Op.mult, Op.add), u1)
             fin.append(dv("fo", 64, [e], lambda o=o, y=y: tt(y[:, 32 * c:32 * c + 32], o[:, c, 2:96:3], o[:, c, 98:192:3], Op.add)))
@@ -378,24 +420,58 @@ def build(g, T, topo, r, P):
     for c in range(NCH):
         cur[0] = c
         chunk(c)
-    for q in range(4):
-        dma("sp" if q % 2 else "act", fin[0::2], 9000, T.yf[:, 256 * q:256 * q + 256], T.yy[32 * q:32 * q + 32, :], "st", 128)
-        dma("act" if q % 2 else "sp", fin[1::2], 9001, T.ya[:, 256 * q:256 * q + 256], T.ye[32 * q:32 * q + 6, :], "st", 128)
+    for h in range(H):
+        for i, (y, b, n) in enumerate(((T.yf, T.yy, 32), (T.ya, T.ye, 6))):
+            for q in range(4):
+                dma("act" if h == H - 1 and q % 2 else "sp", fin[2 * C * h + i:2 * C * (h + 1):2], 9000 + 2 * h + i,
+                    y[:, W * (4 * h + q):W * (4 * h + q + 1)], b[32 * q:32 * q + n, 32 * C * h:32 * C * (h + 1)], "st", 128 * H)
     return ops, Q, sent
 
 
-def lay_out(ops, P):
-    free = {e: 0.0 for e in ("gp", "sp", "pe", "act", "dve")}
-    order = {e: [] for e in free}
-    holder = [None] * 8
+def draws(seed):
+    s = [seed]
+
+    def rnd(k):
+        s[0] = (s[0] * 1103515245 + 12345) % 2147483648
+        return (s[0] >> 8) % k
+    return rnd
+
+
+def rough(ops, P):
     for o in ops:
-        o["end"], o["up"], o["outs"], o["left"], o["at"] = None, 0.0, [], len(o["deps"]), 0.0
+        o["up"], o["outs"] = 0.0, []
     for o in reversed(ops):
         o["up"] += min(o["cost"].values()) + o["lat"] + P["lat"]
         for d in o["deps"]:
             d["up"] = max(d["up"], o["up"])
             d["outs"].append(o)
-        o["key"] = o["p"] if o["p"] is not None else 1000.0 + P["skew"] * o["c"] - o["up"]
+    stages = sorted(set(o["grp"] for o in ops if o["p"] is None))
+    rnd = draws(P["seed"])
+    off = keep = {(k, c): v for k in P["off"] for c, v in enumerate(P["off"][k])}
+    cur = best = lay_out(ops, P, off)[1]
+    for it in range(P["tries"]):
+        new = dict(off)
+        for i in range(1 + rnd(2)):
+            k = stages[rnd(len(stages))]
+            new[k] = new.get(k, 0.0) + (rnd(2) - 0.5) * (0.5, 1, 2, 4, 8)[rnd(5)]
+        t = lay_out(ops, P, new)[1]
+        if t <= cur + P["heat"] * (1.0 - it / P["tries"]) * rnd(100) / 100.0:
+            cur, off = t, new
+            if t < best:
+                best, keep = t, new
+    FAR["rough"] = (best, keep)
+    return lay_out(ops, P, keep)[0]
+
+
+def lay_out(ops, P, off):
+    free = {e: 0.0 for e in ("gp", "sp", "pe", "act", "dve")}
+    order = {e: [] for e in free}
+    holder = [None] * 8
+    for o in ops:
+        o["end"], o["left"], o["at"] = None, len(o["deps"]), 0.0
+        o["key"] = o["p"] if o["p"] is not None else 1000.0 + P["skew"] * o["c"] - o["up"] + off.get(o["grp"], 0.0)
+        if o["unit"] is not None:
+            o["unit"]["bank"] = None
     pend = [o for o in ops if not o["deps"]]
     marks = []
 
@@ -403,7 +479,7 @@ def lay_out(ops, P):
         o["end"] = t
         marks.append(t + P["lat"])
         for x in o["outs"]:
-            x["at"] = max(x["at"], t + (0.0 if x.get("free") else P["lat"]))
+            x["at"] = max(x["at"], t + (0.0 if any(d is o for d in x.get("free", ())) else P["lat"]))
             x["left"] -= 1
             if x["left"] == 0:
                 if x["kind"] == "x":
@@ -433,6 +509,10 @@ def lay_out(ops, P):
                     break
             else:
                 continue
+            far = t + P["look"] * o["cost"][e]
+            if o["cost"][e] > 0.3 and e != "pe" and any(t + 1e-9 < x["at"] < far and e in x["eng"] and x["key"] < o["key"] and
+                                                        (len(x["eng"]) == 1 or e == "act") for x in pend):
+                continue
             k = bank(o, t)
             if k >= 0:
                 holder[k], o["unit"]["bank"] = o["unit"], k
@@ -445,8 +525,10 @@ def lay_out(ops, P):
             did = True
         if not did:
             marks[:] = [y for y in marks if y > t + 1e-9]
-            t = min(marks + [t + 1.0])
-    return order
+            if not marks:
+                return None, 1e9
+            t = min(marks)
+    return order, max(o["end"] for o in ops) + P["tidy"] * sum(o["end"] for o in ops) / len(ops)
 
 
 def polish(ops, order, P):
@@ -454,7 +536,7 @@ def polish(ops, order, P):
     sets = P["sets"]
     deps = [[d["n"] for d in o["deps"]] for o in ops]
     outs0 = [[d["n"] for d in o["outs"]] for o in ops]
-    free = [bool(o.get("free")) for o in ops]
+    wait = [[d["n"] for d in o["deps"] if not any(d is x for x in o.get("free", ()))] for o in ops]
     units = [o["unit"] for o in ops if o["unit"] is not None and o["unit"]["ops"][0] is o]
     uops = [[x["n"] for x in u["ops"]] for u in units]
     heads = [[x["n"] for x in u["ops"] if not any(d["unit"] is u for d in x["deps"])] for u in units]
@@ -464,9 +546,11 @@ def polish(ops, order, P):
     on = [o["on"] for o in ops]
     bank = {k: [i for i in sorted(range(len(units)), key=lambda i: ops[heads[i][0]]["start"]) if units[i]["bank"] == k]
             for k in range(8)}
-    cost = [[{e: c * (s[0] if o["kind"] == "c" else 1.0) + (s[3] if o["kind"] == "r" else 0.0) for e, c in o["cost"].items()}
+    cost = [[{e: c * (s[4] if o["name"][:2] in ("g0", "g1") else s[0] if o["kind"] == "c" else 1.0) +
+              (s[3] if o["kind"] == "r" else 0.0) for e, c in o["cost"].items()}
              for o in ops] for s in sets]
-    lat = [[o["lat"] + s[1] * o.get("hops", 0) for o in ops] for s in sets]
+    lat = [[o["lat"] * (s[5] if o["kind"] == "d" or o["sem"] and o["sem"][0] == "ac" else 1.0) + s[1] * o.get("hops", 0) for o in ops]
+           for s in sets]
 
     def evaluate():
         qp, qn, extra, after = [-1] * n, [-1] * n, [()] * n, [()] * n
@@ -505,14 +589,13 @@ def polish(ops, order, P):
             st, fr, en, why = [0.0] * n, [0.0] * n, [0.0] * n, [-1] * n
             for i in topo:
                 t, y = -w, -1
-                for d in deps[i]:
+                for d in wait[i]:
                     if en[d] > t:
                         t, y = en[d], d
                 for d in extra[i]:
                     if en[d] > t:
                         t, y = en[d], d
-                if not free[i]:
-                    t += w
+                t += w
                 q = qp[i]
                 if q >= 0 and fr[q] > t:
                     t, y = fr[q], q
@@ -521,18 +604,15 @@ def polish(ops, order, P):
                 en[i] = t + ls[i]
             top = max(en)
             i = en.index(top)
-            tot += top + P["tidy"] * sum(en) / n
+            tot += (top + P["tidy"] * sum(en) / n) * sets[s][6]
             while i >= 0:
                 crit.append((i, why[i]))
                 i = why[i]
             st0 = st0 or st
         return tot, crit, st0, qp, extra
     fixed = set([o["n"] for o in ops if o["kind"] == "d"] + [o["n"] for o in ops if o["kind"] == "r"][:2])
-    seed = [P["seed"]]
-
-    def rnd(k):
-        seed[0] = (seed[0] * 1103515245 + 12345) % 2147483648
-        return (seed[0] >> 8) % k
+    lead = [i for i in seq["act"] if ops[i]["kind"] == "d" and not deps[i]]
+    rnd = draws(P["seed"])
     cur = best = evaluate()
     keep = (seq, on, bank)
     for it in range(P["moves"]):
@@ -574,6 +654,9 @@ def polish(ops, order, P):
                 s.insert(j + rnd(4), s.pop(j - 1))
         else:
             continue
+        if seq["act"][:len(lead)] != lead:
+            seq, on, bank = old
+            continue
         new = evaluate()
         if new is not None and new[0] <= cur[0] + P["slack"] * (1.0 - it / P["moves"]) * rnd(100) / 100.0:
             cur = new
@@ -587,7 +670,7 @@ def polish(ops, order, P):
 
 def plan_for(ops, P):
     if "plan" not in FAR:
-        FAR["plan"] = polish(ops, lay_out(ops, P), P)
+        FAR["plan"] = polish(ops, rough(ops, P), P)
     plan = FAR["plan"]
     units = [o["unit"] for o in ops if o["unit"] is not None and o["unit"]["ops"][0] is o]
     for o in ops:
@@ -614,7 +697,7 @@ def emit_all(g, T, Q, order, sent):
     for o in [o for e in order for o in order[e]]:
         e = o["on"]
         need = {}
-        for d in ([] if o.get("free") else o["deps"]) + o["bdeps"]:
+        for d in [d for d in o["deps"] if not any(d is x for x in o.get("free", ()))] + o["bdeps"]:
             s, v = d["sem"]
             need[s] = max(need.get(s, 0), v)
         for s in need:

from concourse.bass import DstId, RemoteDMATransfer
from concourse.mybir import AluOpType as Op, ActivationFunctionType as Fn

NCH = 4
H = 1
C = NCH // H
W = 64 * C
PAR = {"cyc": 0.00088, "pe": 0.00046, "afix": 0.07, "lat": 0.18, "gat": 1.56, "hop": 1.9, "iss": 0.65, "pos": [4.2, 0],
       "tab": 7.4, "late": 9.0, "turn": 4.0, "small": 2.0, "first": 2.8, "cand": 5.0, "own": 0.6, "skew": 1.4,
       "sets": [(0.95, 0.0, 0.18, 0.0, 0.95, 1.0, 0.8), (1.05, 1.1, 0.2, 0.45, 1.0, 1.2, 0.6), (1.18, 0.1, 0.22, 0.1, 1.3, 1.05, 0.5),
                (1.42, 0.3, 0.27, 0.2, 1.88, 1.1, 0.7)],
       "tidy": 0.15, "seed": 5, "moves": 45000, "slack": 0.2, "group": 15, "reach": 3, "look": 0.4, "tries": 2000, "heat": 0.7,
       "off": {}, "split": [], "apart": [], "lq": "sp"}
BIG = 1.5 * 2 ** 23
LEFT = 3.0 * 2 ** 22 - 56

SCRATCH = {}
for _t, _l in (
        ("bfloat16", {"tb": [4096], "fa": [4 * C, 64], "ones": [768], "zz": [528], "wk": [96], "qq": [96], "ns": [64], "eq": [128],
                      "ss": [1536], "ww": [144], "sel": [1024], "fb": [C, 128], "s8": [768], "s16": [16], "pm": [128],
                      "cm": [512], "kc": [512], "pat": [512], "fd": [64], "fc": [512], "al": [384], "tf0": [32], "tf1": [192],
                      "xq": [4, 256], "xr": [4, 512], "b0": [4, 512], "g0": [4, 2048], "b1": [4, 768], "g1": [4, 3072],
                      "xt": [4, 384], "dl": [4, 128], "cu": [4, 128], "ge0": [4, 32], "ge1": [4, 96], "ze": [4, 192]}),
        ("float16", {"s0": [4, 256], "l0": [4, 192], "s1": [4, 384], "l1": [4, 288], "m0": [4, 256], "xi": [4, 512],
                     "mi": [4, 192], "yi": [4, 384]}),
        ("uint16", {"o0": [16, 32], "om": [4, 192], "ol": [4, 144]}),
        ("int32", {"p32": [8 * H, 32 * C], "cs": [4], "cl": [4], "fi": [1024], "fj": [512], "fk": [128], "pi": [8]}),
        ("float32", {"cf": [8], "col": [144], "pf": [8], "mk": [4], "r0": [4, 128], "xx": [4, 128], "zm": [4, 192],
                     "om1": [4, 192], "oe1": [4, 192], "yy": [128], "ye": [128]})):
    for _n in _l:
        SCRATCH[_n] = ("sbuf", [128] + _l[_n], _t)
for _i in range(8):
    SCRATCH["ps%d" % _i] = ("psum", [128, 512], "float32")

SEMAPHORES = ["pe", "dve", "act", "gp", "sent", "ac", "lc", "lp0", "lp1", "lt", "lf", "ly", "lr", "st"]
for _c in range(NCH):
    SEMAPHORES += ["a0_%d" % _c, "a1_%d" % _c] + ["m%d_%d" % (_j, _c) for _j in range(3)]

POOLS = {"w": [0, 1, 2], "s": [3, 4, 5], "o": [7, 6, 5]}
FAR = {}


def wiring(T, topo):
    cores = list(T.cores)
    n = len(cores)
    slots, relay = [], {}
    for r in range(n):
        far = [d for d in range(n) if d != r and not topo.may_write(cores[r], cores[d])]
        near = [d for d in range(n) if d != r and d not in far]
        slots.append(far + near + [r])
        used = []
        for d in far:
            c = [k for k in topo.cores_of(cores[r]) if k not in cores and k not in used and topo.may_write(k, cores[d])]
            c.sort(key=lambda k: topo.die(k) != topo.die(cores[r]))
            used.append(c[0])
            relay[(r, d)] = c[0]
    return cores, slots, relay


def messages(T, j):
    m = {"c": ("ac", T.cl[:, j:j + 1])}
    for c in range(NCH):
        m["a0_%d" % c] = ("a0_%d" % c, T.l0[:, c, 64 * j:64 * j + 64])
        m["m_%d" % c] = ("m%d_%d" % (j, c), T.ol[:, c, 48 * j:48 * j + 48])
        m["a1_%d" % c] = ("a1_%d" % c, T.l1[:, c, 96 * j:96 * j + 96])
    return m


def bits_of(lst):
    m = 0
    for e in lst:
        m |= 1 << e
    return m


def build(g, T, topo, r, P):
    cores, slots, relay = wiring(T, topo)
    me = cores[r]
    sl = slots[r]
    ops = []
    cur = [0, "c"]
    Q = {"pe": g.tensor, "dve": g.vector, "act": g.scalar, "gp": g, "sp": g.sync}
    V = g.vector
    R = None

    def add(name, eng, cost, deps, prio, emit, unit=None, kind="c", sem=None, lat=0.0, at=None):
        if not isinstance(eng, list):
            eng, cost = [eng], {eng: cost}
        o = {"name": name, "eng": eng, "cost": cost, "deps": list(deps), "p": prio, "emit": emit, "unit": unit, "kind": kind,
             "sem": sem, "lat": lat, "at": at, "n": len(ops), "c": cur[0],
             "grp": (name[0] + name[-2:] if name[0] in "gm" and len(name) > 2 else "g" + name[-2:] if len(name) > 3 else cur[1], cur[0])}
        if unit is not None:
            unit["ops"].append(o)
        ops.append(o)
        return o

    def unit(pool):
        return {"pool": pool, "ops": [], "bank": None}

    def ps(u):
        return T["ps%d" % u["bank"]]

    def dv(name, n, deps, fn, u=None, prio=R):
        return add(name, "dve", max(64, n) * P["cyc"], deps, prio, lambda e: fn(), unit=u)

    def shift(name, n, deps, out, in_, scale=1.0, bias=0.0, u=None, prio=R):
        def em(e):
            if e == "act":
                return g.scalar.activation(out, in_(), Fn.Identity, bias=bias, scale=scale)
            return V.tensor_scalar(out, in_(), scale, bias, Op.mult, Op.add)
        return add(name, ["dve", "act"], {"dve": max(64, n) * P["cyc"], "act": P["afix"] + n * P["cyc"]}, deps, prio, em, unit=u)

    def pe(name, cyc, deps, fn, u, prio=R, part=0):
        o = add(name, "pe", cyc * P["pe"], deps, prio, lambda e: mms(fn(), part), unit=u)
        o["free"] = [d for d in deps if d["unit"] is u and d["eng"] == ["pe"] and part > 1]
        return o

    def gp(n, deps, prio, fn):
        return add("gp", "gp", 0.17 + 2 * n * P["cyc"], deps, prio, lambda e: fn())

    def dma(eng, deps, prio, out, in_, sem, tot, at=None):
        return add(sem, eng, 0.05, deps, prio, lambda e: Q[e].dma_start(out, in_).then_inc(T.sem[sem], 16), kind="d",
                   sem=(sem, tot), lat=at or 2.0)

    def ts(out, a, s1, s2, o0, o1=None):
        if o1 is None:
            return V.tensor_scalar(out, a, s1, None, o0)
        return V.tensor_scalar(out, a, s1, s2, o0, o1)

    def tt(out, a, b, op):
        return V.tensor_tensor(out, a, b, op)

    def mms(groups, part):
        last = None
        for grp in groups:
            for i, (o, l, rr) in enumerate(grp):
                last = g.tensor.matmul(o, l, rr, i == 0 and part < 2, i == len(grp) - 1 and part % 2 == 0)
        return last

    sent = [0]

    def send(key, src, dfar, dnear, prio):
        def far(e):
            tr = []
            for j in (0, 1):
                k = relay[(r, sl[j])]
                sem, dst = messages(T, slots[sl[j]].index(r))[key]
                en = topo.engines(me, k)
                h = len(en) // 2
                rid, pid = topo.addr(k, me)
                tr.append(RemoteDMATransfer(dst_ids=[DstId(rid=rid, pnc=pid)], dma_engine_mask=bits_of(en[j * h:(j + 1) * h]),
                                            remote_sem=T.sem[sem], src=src(j), dst=dst))
                sent[0] += h
            return g.remote_dma_fused(tr, local_sem=T.sem.sent)

        def near(e):
            k = cores[sl[2]]
            sem, dst = messages(T, slots[sl[2]].index(r))[key]
            rid, pid = topo.addr(k, me)
            sent[0] += len(topo.engines(me, k))
            return g.remote_dma(dst, src(2), T.sem[sem], T.sem.sent, pid, rid, topo.mask(me, k))
        a = add("F", "gp", P["iss"] + (P["first"] if key == "c" else 0), dfar, prio, far, kind="r")
        a["msg"] = key
        return a, add("N", "gp", P["iss"], dnear, prio + 0.01, near, kind="r")

    def incs(j):
        return len(topo.engines(cores[sl[j]] if j == 2 else relay[(sl[j], r)], me))

    def arrive(snd, js, sem, extra=0.0):
        lat = (2 * P["hop"] if min(js) < 2 else P["hop"]) + extra
        far, near = [snd[0]] if min(js) < 2 else [], [snd[1]] if max(js) == 2 else []
        if far and near:
            near = [add("x", "x", 0.0, near, 0, None, kind="x", sem=None, lat=-P["hop"])]
        o = add("x", "x", 0.0, far + near, 0, None, kind="x", sem=(sem, sum(incs(j) for j in js)), lat=lat)
        o["hops"] = 2 if far else 1
        return o

    def sel(out, in_, pat, op, base, cm):
        return lambda: g.affine_select(out, in_, pat, op, 0.0, base, cm)

    own = slice(1024 * r, 1024 * r + 1024)
    lc = dma("sp", [], 0, T.cs[0:96, 0:1], T.cand[:], "lc", 16, at=P["small"])
    lp = [[dma("sp", [], 1 + 2 * h, T.p32[:, 8 * h + 2 * j:8 * h + 2 * j + 2, :],
               T.pos0[:, 1024 * sl[j] + 4 * W * h:1024 * sl[j] + 4 * W * (h + 1)], "lp%d" % h, 64, at=P["pos"][h])
           for j in range(4)] for h in range(H)]
    lt = dma("sp", [], 2, T.tb[:], T.tab[:], "lt", 16, at=P["tab"])
    lf = [dma("sp", [], 0.5, o, i, "lf", 32, at=P["small"]) for o, i in (
        (T.fi[0:16 * H, 0:W], T.fac[0, :]), (T.fi[0:16 * H, W:2 * W], T.inc[0, :]))]
    ly = [dma(P["lq"], [], -1 if P["lq"] == "act" else 3.5, o, i, "ly", 160, at=P["late"]) for o, i in
          [(T.fi[0:8 * H, 2 * W:3 * W], T.fac[1:3, own]), (T.fi[0:8 * H, 3 * W:4 * W], T.inc[1:3, own]),
           (T.fj[0:4 * H, 256:256 + W], T.th[0, own])] +
          [(T.fj[0:32, 32 * k:32 * k + 32], T.th[k, own]) for k in range(3)] +
          [(T.fj[0:32, 96 + 32 * k:128 + 32 * k], (T.fac, T.inc)[k % 2][1 + k // 2, own]) for k in range(4)]]

    def c_(n, deps, prio, fn):
        return dv("c", n, deps, fn, prio=prio)

    def fill(ap, n, val, prio, deps=()):
        return c_(n, deps, prio, lambda: V.memset(ap, val))
    mc = fill(T.cs[96:128, :], 1, 0, 0)
    m1 = fill(T.ones[:], 384, 1.0, 0.1)

    def fil2(ap, p, n, val, prio, deps=(), w=0.5):
        def em(e):
            if e == "act":
                return g.scalar.activation(ap, T.ones[0:p, 0:n], Fn.Identity, scale=val)
            return V.memset(ap, val) if isinstance(val, float) else ts(ap, T.ones[0:p, 0:n], val, None, Op.mult)
        return add("c", ["dve", "act"], {"dve": max(64, n * w) * P["cyc"], "act": P["afix"] + n * P["cyc"]}, [m1] + list(deps), prio, em)
    wk = [fill(T.wk[0:96, 32 * k:32 * k + 32], 1, 2.0 ** k / 32, 0.2) for k in range(3)]
    mz = fil2(T.zz[:], 128, 528, 0.0, 1)
    al = [fil2(T.al[0:1, 128 * k:128 * k + 128], 1, 128, 2.0 ** k / 32 * ((0.5 if k == 1 else 0.0) - 1 / 128), 1) for k in range(3)]
    k0 = fil2(T.kc[0:2, 0:128], 2, 128, 8.0, 1.5)
    kc = [fil2(T.kc[0:1, 0:128], 1, 128, 2.0 ** 25, 1.5, [k0])] + [
        fil2(T.kc[0:1, 128 * i:128 * i + 128], 1, 128, v, 1.5) for i, v in ((1, -5.0 * 2 ** 22), (2, BIG), (3, -BIG))] + [m1]
    pat = [fil2(T.pat[:, i:512:2], 128, 256, -1.0 * i, 1.6) for i in range(2)]
    icol = gp(144, [], 0, lambda: g.iota(T.col[:], [[1, 144]], 0, 0, allow_small_or_imprecise_dtypes=True))
    ip = gp(1, [], 0.1, lambda: g.iota(T.pi[:, 0:1], [[0, 1]], 0, 1))
    gn1 = gp(56, [m1], 1, sel(T.ns[0:96, 0:56], T.ones[0:96, 0:56], [[-12, 56]], Op.is_ge, 288, 1))
    gq = gp(96, wk, 1.1, sel(T.qq[0:96, :], T.wk[0:96, :], [[-1, 3], [-3, 4], [-12, 8]], Op.is_equal, 0, 1))
    gns = gp(56, [gn1], 1.2, sel(T.ns[0:96, 0:56], T.ns[0:96, 0:56], [[12, 56]], Op.is_ge, -277, -1))
    gs1 = [gp(512, [m1], 1.3 + 4 * h, sel(T.sel[0:32, 512 * h:512 * h + 512], T.ones[0:32, 0:512], [[-4 * H, 4], [0, 32], [-1, 4]],
                                          Op.is_equal, -4 * h, 1)) for h in range(H)]
    gs8 = [gp(128, [m1], 6, sel(T.s8[0:32, 384 - 128 * c:512 - 128 * c], T.ones[0:32, 0:128], [[-2 * C, 4], [0, 16], [-C, 2]],
                                Op.is_equal, -8 * C * (c // C) - c % C, 1)) for c in range(NCH)]
    gsk = gp(256, [m1], 6, sel(T.s8[0:32, 512:768], T.ones[0:32, 0:256], [[-C, 2], [0, 32], [-2 * C, 4]], Op.is_equal, 0, 1))
    gpm = gp(128, [m1], 6, sel(T.pm[:], T.ones[:, 0:128], [[-1, 4], [-4, 32]], Op.is_equal, 0, 1))
    an = [c_(1, [ip], 2, lambda i=i, v=v: ts(T.pi[:, i:i + 1], T.pi[:, 0:1], v, None, Op.bitwise_and))
          for i, v in ((1, 28), (2, 3), (3, 15), (4, 30))]
    t0 = c_(1, an[0:1], 2, lambda: ts(T.pf[:, 0:1], T.pi[:, 1:2], 4.0, 12.0, Op.mult, Op.add))
    t1 = c_(1, [t0, an[1]], 2, lambda: tt(T.pf[:, 1:2], T.pf[:, 0:1], T.pi[:, 2:3], Op.add))
    t2 = c_(2, an[2:4], 2, lambda: V.tensor_copy(T.pf[:, 2:4], T.pi[:, 3:5]))
    wq = [fill(T.pf[32 * q:32 * q + 32, 4:5], 1, 8.0 ** q, 2) for q in range(4)]
    ww = c_(144, [icol, t1] + wq, 3, lambda: ts(T.ww[:], T.col[:], T.pf[:, 1:2], T.pf[:, 4:5], Op.is_equal, Op.mult))
    ks = c_(16, [icol, t2], 4, lambda: ts(T.s16[:], T.col[:, 0:16], T.pf[:, 2:3], None, Op.is_equal))
    mk = c_(3, [icol, t2], 4, lambda: ts(T.mk[:, 0:3], T.col[:, 0:6:2], T.pf[:, 3:4], None, Op.is_equal))
    ze = [fil2(T.ze[:, :, 0:192:3], 128, 256, T.mk[:, 2:3], 4.6, [mk]), fil2(T.ze[:, :, 97:192:3], 128, 128, T.mk[:, 1:2], 4.6, [mk])]
    zm = [fil2(z[:, :, a:b:3], 128, 128, 0.0, 4.6, w=1.0) for z in (T.zm, T.ze) for a, b in ((1, 96), (98, 192))]
    z1 = fil2(T.tf1[0:32, 0:192:3], 32, 64, 0.0, 4.6)
    u = unit("w")
    m = pe("cm", 384, [gs8[0], gsk], lambda u=u: [[(ps(u)[:, 0:384], T.s8[0:32, 384:512], T.s8[0:32, 384:768])]], u)
    cm = shift("c", 384, [m], T.cm[:, 0:384], lambda u=u: ps(u)[:, 0:384], 1 / 32, u=u)
    ncm = shift("c", 128, [cm], T.cm[:, 384:512], lambda: T.cm[:, 0:128], -1.0)

    sc = send("c", lambda j: T.cs[:, 0:1], [lc, mc], [lc, mc], 3)
    ac = arrive(sc, [0, 1, 2], "ac", P["cand"])
    cfo = c_(1, [lc], 1.5, lambda: V.tensor_copy(T.cf[0:96, 4:5], T.cs[0:96, 0:1]))
    cfr = c_(3, [ac], R, lambda: V.tensor_copy(T.cf[0:96, 0:3], T.cl[0:96, 0:3]))
    S = []
    cur[1] = "s"
    for j in range(4):
        pr = 1.6 if j == 3 else R
        b, i = 132 * j, j + j // 3
        e = c_(32, [cfo if j == 3 else cfr, icol], pr,
               lambda j=j, i=i: ts(T.eq[0:96, 32 * j:32 * j + 32], T.col[0:96, 0:32], T.cf[0:96, i:i + 1], None, Op.is_equal))
        e = c_(64, [e, gns, mz], pr, lambda j=j, b=b: tt(T.zz[0:96, b + 3:b + 131:4], T.ns[0:96, 24 - 8 * sl[j]:56 - 8 * sl[j]],
                                                        T.eq[0:96, 32 * j:32 * j + 32], Op.subtract))
        u = unit("w")
        m = pe("sm", 768, [e, gq, m1] + al, lambda u=u, b=b: [[(ps(u)[:, 0:384], T.ones[0:1, 0:128], T.al[0:1, :])] + [
            (ps(u)[:, a:384:4], T.zz[0:96, b + 3 - a:b + 131 - a], T.qq[0:96, :]) for a in range(4)]], u, pr)
        S.append(shift("sc", 384, [m], T.ss[:, 384 * j:384 * j + 384], lambda u=u: ps(u)[:, 0:384], u=u, prio=pr))

    def st(j, k):
        return T.ss[:, 384 * j + 128 * k:384 * j + 128 * k + 128]

    cur[1] = "t"
    fa = [[c_(W // 2, ly if s else lf, R if s else 1.4, lambda s=s, f=f, k=k: ts(
        T.fa[0:(16 - 8 * s) * H, C * (2 * s + f):C * (2 * s + f + 1), 32 * k:32 * k + 32],
        T.fi[0:(16 - 8 * s) * H, W * (4 * s + 2 * f + k) // 2:W * (4 * s + 2 * f + k + 1) // 2], 16.5 * f, None, Op.add))
        for f in range(2) for k in range(2)] for s in range(2)]

    def thr(n, out, in_, sgn):
        return c_(n, ly, R, lambda: ts(out, in_, -sgn / 32, 0.5 + sgn / 64, Op.mult, Op.add))
    tp = [thr(W // 2, T.fb[0:4 * H, :, 64 * k + 1:64 * k + 64:2], T.fj[0:4 * H, 256 + W * k // 2:256 + W * (k + 1) // 2], 1)
          for k in range(2)] + [fil2(T.fb[0:4 * H, :, 0:128:2], 4 * H, W, 0.0, 4.6)]
    tf0 = thr(32, T.tf0[0:32, :], T.fj[0:32, 0:32], 1)
    tf1 = [z1] + [thr(32, T.tf1[0:32, a:b:3], T.fj[0:32, 32 * k:32 * k + 32], s)
                  for a, b, k, s in ((1, 96, 2, 1), (97, 192, 2, 1), (2, 96, 1, -1), (98, 192, 1, 1))]
    h = [c_(64, ly, R, lambda i=i: tt(T.fk[0:32, 32 * i:32 * i + 32], T.fj[0:32, 96 + 32 * i:128 + 32 * i], T.fj[0:32, 160:192], Op.mult))
         for i in range(2)]
    h[1] = c_(64, h[1:], R, lambda: tt(T.fk[0:32, 32:64], T.fk[0:32, 32:64], T.fj[0:32, 192:224], Op.add))
    h = c_(64, h, R, lambda: ts(T.fk[0:32, 64:128], T.fk[0:32, 0:64], 31, None, Op.bitwise_and))
    h = [c_(32, [h], R, lambda i=i: ts(T.fd[0:32, 32 * i:32 * i + 32], T.fk[0:32, 64 + 32 * i:96 + 32 * i], 16.5 * i, None, Op.add))
         for i in range(2)]
    fc = [dma("sp", h, 4, T.fc[0:4 * H, W * i:W * i + W], T.fd[0:32, 32 * i:32 * i + 32], "lr", 32, at=P["turn"]) for i in range(2)]

    def wrap(tag, x, out, n, deps):
        e = dv(tag + "y", n // 2, deps + pat, lambda: ts(x(1), x(0), 2.0 ** 28, 2.0 ** 28 - 16, Op.add, Op.subtract))
        return dv(tag + "z", n, [e], lambda: V.tensor_tensor_scan(out, T.pat[:, 0:2 * n], x(None), 0.0, Op.mult, Op.subtract))

    def rnd(o, w):
        return [(o, T.kc[0:1, 256:384], T.ones[0:1, 0:w]), (o, T.kc[0:1, 384:512], T.ones[0:1, 0:w])]

    def masks(parts, early, deps, bits, out, tag):
        w = sum(p[2] for p in parts)
        u = unit("w")

        def x(k):
            l, a = [], 0
            for j, pos, n in parts:
                l.append((ps(u)[:, a:a + n], st(j, k), pos))
                a += n
            return l
        d = pe("mi" + tag, w, early + kc, lambda: [[(ps(u)[:, 0:w], T.kc[0:2, 0:128], T.ones[0:2, 0:w])]], u, part=1)
        d = pe("md" + tag, 2 * w, deps + [d], lambda: [x(2) + x(1)], u, part=3)
        d = pe("me" + tag, 2 * w, [d], lambda: [[(ps(u)[:, 0:w], T.kc[0:1, 128:256], T.ones[0:1, 0:w])] + x(0)], u, part=2)
        b = shift("mb" + tag, w, [d], bits(0, 1), lambda: ps(u)[:, 0:w], 1.0, -LEFT, u)
        m = pe("mm" + tag, 4 * max(64, w // 4), [b, ww], lambda: [[
            (ps(u)[:, 0:w // 4], T.ww[:, 12 - 4 * s:140 - 4 * s], bits(s, 4)) for s in range(4)]], u)
        return dv("mc" + tag, w // 4, [m], lambda: V.tensor_copy(out, ps(u)[:, 0:w // 4]), u)

    def gather(name, off, k, out, deps):
        def em(e):
            src = T.tb[:, 0:4096].indirect(off)
            if e == "act":
                return g.scalar.activation(out, src, Fn.Copy)
            return V.tensor_copy(out, src)
        c = 16 * k * P["gat"] * P["cyc"]
        return add(name, ["act", "dve"], {"act": 0.07 + c, "dve": 0.05 + c}, deps + [lt], R, em)

    def sums(n, offs, gb, sb, c):
        cvs = []
        for js in ([0, 1], [2], [3]):
            u = unit("s")
            tag = str(n - 2) + "ffno"[js[0]]
            sm = []
            for j in js:
                off, dep = offs(j)
                ga = gather("g" + tag, off, 16 * n, gb[:, c, 256 * n * j:256 * n * (j + 1)], dep)
                sm.append(pe("su" + tag, 128 * n, [ga, ks], lambda u=u, j=j, a=32 * n * (j - js[0]): [
                    [(ps(u)[:, a + 32 * ev + k:a + 32 * ev + 32:2],
                      gb[:, c, 256 * n * j + 128 * (2 * ev + k):256 * n * j + 128 * (2 * ev + k + 1)], T.s16[:])]
                    for ev in range(n) for k in range(2)], u))
            w, a = 32 * n * len(js), 32 * n * js[0]
            cvs.append(dv("sc" + tag, w, sm, lambda u=u, w=w, a=a: V.tensor_copy(sb[:, c, a:a + w], ps(u)[:, 0:w]), u))
        return cvs

    J = (3, 0, 1, 2)
    fin = []

    def chunk(c):
        cur[1] = "p"
        hh, cc = c // C, c % C
        pos = T.p32[:, 8 * hh:8 * hh + 8, 32 * cc:32 * cc + 32]

        def row(n, i):
            return T.sel[0:n, 512 * hh + 128 * i:512 * hh + 128 * i + 128]
        cv = dv("cv", 256, lp[hh], lambda: ts(T.xq[:, c, :], pos, -31.5, None, Op.add))
        ub = unit("o")
        bc = pe("bc", 512, fa[0] + [gs1[hh]] + ([cv] if c > 1 else []), lambda: [
            [(ps(ub)[:, 256 * f + 64 * j:256 * f + 64 * j + 64], row(16 * H, sl[j]), T.fa[0:16 * H, C * f + cc, :])]
            for f in range(2) for j in range(4)], ub)
        e = dv("p1", 256, [bc] + lp[hh], lambda: tt(T.m0[:, c, :], ps(ub)[:, 0:256], pos, Op.mult), ub)
        e = dv("p2", 256, [e], lambda: tt(T.xi[:, c, 0:512:2], ps(ub)[:, 256:512], T.m0[:, c, :], Op.add), ub)
        p0 = wrap("p", lambda i: T.xi[:, c, :] if i is None else T.xi[:, c, i:512:2], T.xr[:, c, :], 256, [e])
        mk0 = [masks([(3, T.xr[:, c, 1:512:2] if ev else T.xq[:, c, :], 256)], [e if ev else cv], [p0 if ev else cv, S[3]],
                     lambda s, n, ev=ev: T.b0[:, c, 256 * ev + s:256 * ev + 256:n], T.o0[:, 4 * c:4 * c + 4, 16 * ev:16 * ev + 16], "0" + "sp"[ev])
               for ev in range(2)]
        cvs = sums(2, lambda j: (T.o0[:, 4 * c + j, :], mk0), T.g0, T.s0, c)
        sn = send("a0_%d" % c, lambda j: T.s0[:, c, 64 * j:64 * j + 64], [cvs[0]], [cvs[1]], 20)
        dl = [dv("dl", 128, [p0, cv], lambda: tt(T.dl[:, c, 0:128:2], T.xr[:, c, 385:512:2], T.xq[:, c, 192:256], Op.subtract)),
              shift("dp", 64, [cv], T.dl[:, c, 1:128:2], lambda: T.xq[:, c, 192:256], 1.0, 31.5)]
        cur[1] = "d"
        u0, up = unit("o"), unit("o")
        to = pe("to", 256, [arrive(sn, [0, 1, 2], "a0_%d" % c), cvs[2], gpm], lambda: [
            [(ps(u0)[:, 0:64], T.pm[:], T.s0[:, c, 192:256] if j == 3 else T.l0[:, c, 64 * j:64 * j + 64]) for j in J]], u0)
        co = pe("co", 512, [cvs[2], gs1[hh]] + fa[1] + fc, lambda: [
            [(ps(up)[:, 128 + 192 * f + 64 * k:192 + 192 * f + 64 * k], row(8 * H, k), T.fa[0:8 * H, C * (2 + f) + cc, :])]
            for f in range(2) for k in range(2)] + [
            [(ps(up)[:, 256 + 192 * f + 32 * k:288 + 192 * f + 32 * k], row(4 * H, 0),
              T.fc[0:4 * H, W * (2 * f + k) // 2 + 32 * cc:W * (2 * f + k) // 2 + 32 * cc + 32])] for f in range(2) for k in range(2)], up)
        tr = dv("tr", 64, [to], lambda: V.transpose(T.r0[:, c, 0:64], ps(u0)[:, 0:64]), u0)
        ge = dv("ge", 64, [tr], lambda: tt(T.ge0[:, c, :], T.r0[:, c, 32:64], T.r0[:, c, 0:32], Op.is_ge))
        d0 = dv("d0", 64, [ge], lambda: tt(T.r0[:, c, 96:128], T.r0[:, c, 32:64], T.r0[:, c, 0:32], Op.subtract))
        zp = pe("zi", 128, [co] + tp, lambda: [[(ps(up)[:, 0:128], row(4 * H, 0), T.fb[0:4 * H, cc, :])]], up, part=1)
        zp = pe("zp", 256, [ge, zp, cm] + kc, lambda: [
            [(ps(up)[:, 64 * k + 1:64 * k + 64:2], T.cm[:, 128 + 128 * k:256 + 128 * k], T.ge0[:, c, :]) for k in range(2)] +
            rnd(ps(up)[:, 1:128:2], 64)], up, part=4)
        cur[1] = "z"
        s8 = T.s8[0:32, 384 - 128 * c:512 - 128 * c]
        zf = pe("zf", 256, [ge, cm, tf0, gs8[c]] + kc, lambda: [
            [(ps(u0)[:, 64:96], s8, T.tf0[0:32, :]), (ps(u0)[:, 64:96], T.cm[:, 0:128], T.ge0[:, c, :])] +
            rnd(ps(u0)[:, 64:96], 32)], u0)
        f1 = dv("f1", 32, [zf, d0], lambda: tt(T.r0[:, c, 64:96], ps(u0)[:, 64:96], T.r0[:, c, 96:128], Op.mult), u0)
        a0 = shift("a0", 32, [f1, mk], T.ze[:, c, 2:96:3], lambda: ps(u0)[:, 64:96], T.mk[:, 0:1], u=u0)
        f2 = dv("f2", 64, [f1], lambda: tt(T.xx[:, c, 0:32], T.r0[:, c, 64:96], T.r0[:, c, 0:32], Op.add))
        f3 = shift("f3", 32, [f2], T.zm[:, c, 2:96:3], lambda: T.xx[:, c, 0:32])
        cur[1] = "d"
        e = dv("q1", 128, [zp] + dl, lambda: V.tensor_tensor_scan(T.cu[:, c, :], ps(up)[:, 0:128], T.dl[:, c, :], 0.0, Op.mult, Op.add), up)
        q3 = [dv("q3", 64, [e], lambda k=k: tt(T.mi[:, c, 64 * k:64 * k + 64], ps(up)[:, 128 + 64 * k:192 + 64 * k], T.cu[:, c, 1:128:2],
                                               Op.mult), up) for k in range(3)]
        e = dv("q4", 192, q3, lambda: tt(T.yi[:, c, 0:384:2], ps(up)[:, 320:512], T.mi[:, c, :], Op.add), up)
        xt = wrap("q", lambda i: T.yi[:, c, :] if i is None else T.yi[:, c, i:384:2], T.xt[:, c, :], 192, [e])
        mo = [masks([(j, T.xt[:, c, 1:384:2], 192) for j in js], [e], [xt] + [S[j] for j in js],
                    lambda s, n, js=js: T.b1[:, c, 192 * js[0] + s:192 * js[-1] + 192:n], T.om[:, c, 48 * js[0]:48 * js[-1] + 48],
                    "1" + "ffno"[js[0]]) for js in ([[0], [1]] if c in P["apart"] else [[0, 1]]) + ([[2], [3]] if c in P["split"] else [[2, 3]])]
        nf = 2 if c in P["apart"] else 1
        sm_ = send("m_%d" % c, lambda j: T.om[:, c, 48 * j:48 * j + 48], mo[0:nf], [mo[nf]], 19)
        cvs = sums(3, lambda j: (T.om[:, c, 144:192], [mo[-1]]) if j == 3 else
                   (T.ol[:, c, 48 * j:48 * j + 48], [arrive(sm_, [j], "m%d_%d" % (j, c))]), T.g1, T.s1, c)
        sn1 = send("a1_%d" % c, lambda j: T.s1[:, c, 96 * j:96 * j + 96], [cvs[0]], [cvs[1]], 20)
        cur[1] = "e"
        u1 = unit("o")
        to1 = pe("to", 384, [arrive(sn1, [0, 1, 2], "a1_%d" % c), cvs[2], gpm], lambda: [
            [(ps(u1)[:, 0:96], T.pm[:], T.s1[:, c, 288:384] if j == 3 else T.l1[:, c, 96 * j:96 * j + 96]) for j in J]], u1)
        tr1 = dv("tr", 96, [to1], lambda: V.transpose(T.xx[:, c, 32:128], ps(u1)[:, 0:96]), u1)
        ga = dv("ge", 128, [tr1, f2], lambda: tt(T.ge1[:, c, 32:96], T.xx[:, c, 64:128], T.xx[:, c, 0:64], Op.is_ge))
        gb = dv("ge", 64, [tr1, f2], lambda: tt(T.ge1[:, c, 0:32], T.xx[:, c, 32:64], T.xx[:, c, 0:32], Op.is_ge))
        da = dv("df", 128, [ga], lambda: tt(T.zm[:, c, 0:192:3], T.xx[:, c, 64:128], T.xx[:, c, 0:64], Op.subtract))
        db = dv("df", 64, [gb], lambda: tt(T.zm[:, c, 97:192:3], T.xx[:, c, 32:64], T.xx[:, c, 0:32], Op.subtract))
        zq = pe("zj", 192, [tr1, gs8[c]] + tf1, lambda: [[(ps(u1)[:, 128:320], s8, T.tf1[0:32, :])]], u1, part=1)
        zq = pe("zq", 448, [ga, gb, zq, cm, ncm] + kc, lambda: [
            [(ps(u1)[:, 129:320:3], T.cm[:, 0:128], T.ge1[:, c, 32:96])] + rnd(ps(u1)[:, 129:320:3], 64) +
            [(ps(u1)[:, 226:320:3], T.cm[:, 0:128], T.ge1[:, c, 0:32]),
             (ps(u1)[:, 130:224:3], T.cm[:, 384:512], T.ge1[:, c, 0:32])] + rnd(ps(u1)[:, 130:320:3], 64)], u1, part=4)
        for o, d, y, dep in ((T.om1, T.zm, T.yy, [da, db, f3] + zm), (T.oe1, T.ze, T.ye, [a0] + ze + zm)):
            e = dv("sn", 192, [zq] + dep, lambda o=o, d=d: V.tensor_tensor_scan(o[:, c, :], ps(u1)[:, 128:320], d[:, c, :], 0.0,
                                                                               Op.mult, Op.add), u1)
            fin.append(dv("fo", 64, [e], lambda o=o, y=y: tt(y[:, 32 * c:32 * c + 32], o[:, c, 2:96:3], o[:, c, 98:192:3], Op.add)))

    for c in range(NCH):
        cur[0] = c
        chunk(c)
    for h in range(H):
        for i, (y, b, n) in enumerate(((T.yf, T.yy, 32), (T.ya, T.ye, 6))):
            for q in range(4):
                dma("act" if h == H - 1 and q % 2 else "sp", fin[2 * C * h + i:2 * C * (h + 1):2], 9000 + 2 * h + i,
                    y[:, W * (4 * h + q):W * (4 * h + q + 1)], b[32 * q:32 * q + n, 32 * C * h:32 * C * (h + 1)], "st", 128 * H)
    return ops, Q, sent


def draws(seed):
    s = [seed]

    def rnd(k):
        s[0] = (s[0] * 1103515245 + 12345) % 2147483648
        return (s[0] >> 8) % k
    return rnd


def rough(ops, P):
    for o in ops:
        o["up"], o["outs"] = 0.0, []
    for o in reversed(ops):
        o["up"] += min(o["cost"].values()) + o["lat"] + P["lat"]
        for d in o["deps"]:
            d["up"] = max(d["up"], o["up"])
            d["outs"].append(o)
    stages = sorted(set(o["grp"] for o in ops if o["p"] is None))
    rnd = draws(P["seed"])
    off = keep = {(k, c): v for k in P["off"] for c, v in enumerate(P["off"][k])}
    cur = best = lay_out(ops, P, off)[1]
    for it in range(P["tries"]):
        new = dict(off)
        for i in range(1 + rnd(2)):
            k = stages[rnd(len(stages))]
            new[k] = new.get(k, 0.0) + (rnd(2) - 0.5) * (0.5, 1, 2, 4, 8)[rnd(5)]
        t = lay_out(ops, P, new)[1]
        if t <= cur + P["heat"] * (1.0 - it / P["tries"]) * rnd(100) / 100.0:
            cur, off = t, new
            if t < best:
                best, keep = t, new
    FAR["rough"] = (best, keep)
    return lay_out(ops, P, keep)[0]


def lay_out(ops, P, off):
    free = {e: 0.0 for e in ("gp", "sp", "pe", "act", "dve")}
    order = {e: [] for e in free}
    holder = [None] * 8
    for o in ops:
        o["end"], o["left"], o["at"] = None, len(o["deps"]), 0.0
        o["key"] = o["p"] if o["p"] is not None else 1000.0 + P["skew"] * o["c"] - o["up"] + off.get(o["grp"], 0.0)
        if o["unit"] is not None:
            o["unit"]["bank"] = None
    pend = [o for o in ops if not o["deps"]]
    marks = []

    def done(o, t):
        o["end"] = t
        marks.append(t + P["lat"])
        for x in o["outs"]:
            x["at"] = max(x["at"], t + (0.0 if any(d is o for d in x.get("free", ())) else P["lat"]))
            x["left"] -= 1
            if x["left"] == 0:
                if x["kind"] == "x":
                    x["on"] = "x"
                    done(x, x["at"] + x["lat"])
                else:
                    pend.append(x)

    def bank(o, t):
        u = o["unit"]
        if u is None or u["bank"] is not None:
            return -1
        for k in POOLS[u["pool"]]:
            if holder[k] is None or all(x["end"] is not None and x["end"] + P["lat"] <= t + 1e-9 for x in holder[k]["ops"]):
                return k
        return None
    t = 0.0
    while pend:
        did = False
        pend.sort(key=lambda o: o["key"])
        for e in free:
            if free[e] > t + 1e-9:
                continue
            for o in pend:
                if e in o["eng"] and o["at"] <= t + 1e-9 and bank(o, t) is not None and not (
                        e == "dve" and len(o["eng"]) > 1 and free["act"] < t + o["cost"][e] * P["own"]):
                    break
            else:
                continue
            far = t + P["look"] * o["cost"][e]
            if o["cost"][e] > 0.3 and e != "pe" and any(t + 1e-9 < x["at"] < far and e in x["eng"] and x["key"] < o["key"] and
                                                        (len(x["eng"]) == 1 or e == "act") for x in pend):
                continue
            k = bank(o, t)
            if k >= 0:
                holder[k], o["unit"]["bank"] = o["unit"], k
            o["on"], o["start"] = e, t
            free[e] = t + o["cost"][e]
            marks.append(free[e])
            order[e].append(o)
            pend.remove(o)
            done(o, free[e] + o["lat"])
            did = True
        if not did:
            marks[:] = [y for y in marks if y > t + 1e-9]
            if not marks:
                return None, 1e9
            t = min(marks)
    return order, max(o["end"] for o in ops) + P["tidy"] * sum(o["end"] for o in ops) / len(ops)


def polish(ops, order, P):
    n = len(ops)
    sets = P["sets"]
    deps = [[d["n"] for d in o["deps"]] for o in ops]
    outs0 = [[d["n"] for d in o["outs"]] for o in ops]
    wait = [[d["n"] for d in o["deps"] if not any(d is x for x in o.get("free", ()))] for o in ops]
    units = [o["unit"] for o in ops if o["unit"] is not None and o["unit"]["ops"][0] is o]
    uops = [[x["n"] for x in u["ops"]] for u in units]
    heads = [[x["n"] for x in u["ops"] if not any(d["unit"] is u for d in x["deps"])] for u in units]
    tails = [[x["n"] for x in u["ops"] if not any(d["unit"] is u for d in x["outs"])] for u in units]
    uof = {x: i for i in range(len(units)) for x in uops[i]}
    seq = {e: [o["n"] for o in order[e]] for e in order}
    on = [o["on"] for o in ops]
    bank = {k: [i for i in sorted(range(len(units)), key=lambda i: ops[heads[i][0]]["start"]) if units[i]["bank"] == k]
            for k in range(8)}
    cost = [[{e: c * (s[4] if o["name"][:2] in ("g0", "g1") else s[0] if o["kind"] == "c" else 1.0) +
              (s[3] if o["kind"] == "r" else 0.0) for e, c in o["cost"].items()}
             for o in ops] for s in sets]
    lat = [[o["lat"] * (s[5] if o["kind"] == "d" or o["sem"] and o["sem"][0] == "ac" else 1.0) + s[1] * o.get("hops", 0) for o in ops]
           for s in sets]

    def evaluate():
        qp, qn, extra, after = [-1] * n, [-1] * n, [()] * n, [()] * n
        cnt = [len(d) for d in deps]
        for s in seq.values():
            for i in range(1, len(s)):
                qp[s[i]], qn[s[i - 1]] = s[i - 1], s[i]
                cnt[s[i]] += 1
        for b in bank.values():
            for i in range(1, len(b)):
                for h in heads[b[i]]:
                    extra[h] = tails[b[i - 1]]
                    cnt[h] += len(extra[h])
                for h in tails[b[i - 1]]:
                    after[h] = heads[b[i]]
        topo = [i for i in range(n) if cnt[i] == 0]
        for i in topo:
            for x in outs0[i]:
                cnt[x] -= 1
                if cnt[x] == 0:
                    topo.append(x)
            for x in after[i]:
                cnt[x] -= 1
                if cnt[x] == 0:
                    topo.append(x)
            x = qn[i]
            if x >= 0:
                cnt[x] -= 1
                if cnt[x] == 0:
                    topo.append(x)
        if len(topo) < n:
            return None
        tot, crit, st0 = 0.0, [], None
        for s in range(len(sets)):
            w, cs, ls = sets[s][2], cost[s], lat[s]
            st, fr, en, why = [0.0] * n, [0.0] * n, [0.0] * n, [-1] * n
            for i in topo:
                t, y = -w, -1
                for d in wait[i]:
                    if en[d] > t:
                        t, y = en[d], d
                for d in extra[i]:
                    if en[d] > t:
                        t, y = en[d], d
                t += w
                q = qp[i]
                if q >= 0 and fr[q] > t:
                    t, y = fr[q], q
                st[i], why[i] = t, y
                fr[i] = t = t + cs[i][on[i]]
                en[i] = t + ls[i]
            top = max(en)
            i = en.index(top)
            tot += (top + P["tidy"] * sum(en) / n) * sets[s][6]
            while i >= 0:
                crit.append((i, why[i]))
                i = why[i]
            st0 = st0 or st
        return tot, crit, st0, qp, extra
    fixed = set([o["n"] for o in ops if o["kind"] == "d"] + [o["n"] for o in ops if o["kind"] == "r"][:2])
    lead = [i for i in seq["act"] if ops[i]["kind"] == "d" and not deps[i]]
    rnd = draws(P["seed"])
    cur = best = evaluate()
    keep = (seq, on, bank)
    for it in range(P["moves"]):
        i, y = cur[1][rnd(len(cur[1]))]
        if rnd(4) == 0:
            i = rnd(n)
            y = cur[3][i]
        e = on[i]
        if e == "x" or i in fixed or y in fixed:
            continue
        old = (seq, on, bank)
        kind = rnd(10)
        if rnd(100) < P["group"]:
            d = 0.15 * (1 + rnd(4) * rnd(6))
            i, d, nxt = (i, -d, deps) if rnd(2) or y < 0 else (y, d, outs0)
            key, grp = list(cur[2]), [i]
            for x in grp:
                key[x] += d
                grp += [z for z in nxt[x] if z not in grp and z not in fixed and abs(cur[2][z] - cur[2][i]) < abs(d) + P["reach"]]
            seq = {f: sorted(s, key=lambda v: key[v]) for f, s in seq.items()}
            bank = {b: sorted(s, key=lambda v: key[heads[v][0]]) for b, s in bank.items()}
        elif len(ops[i]["eng"]) > 1 and kind < 3:
            f = [x for x in ops[i]["eng"] if x != e][0]
            t = cur[2][i] - 0.3 * rnd(4)
            j = len([x for x in seq[f] if cur[2][x] < t])
            seq, on = dict(seq), list(on)
            seq[e], seq[f], on[i] = [x for x in seq[e] if x != i], seq[f][:j] + [i] + seq[f][j:], f
        elif y >= 0 and y in cur[4][i] and kind < 8:
            u, k, t = uof[i], rnd(8), cur[2][i] - 0.5 * rnd(3)
            bank = {b: [v for v in bank[b] if v != u] for b in bank}
            bank[k].insert(len([v for v in bank[k] if cur[2][heads[v][0]] < t]), u)
        elif y >= 0 and y == cur[3][i]:
            seq = dict(seq)
            s = seq[e] = list(seq[e])
            j = s.index(i)
            if kind < 7:
                s.insert(max(0, j - 1 - rnd(3) * rnd(3)), s.pop(j))
            else:
                s.insert(j + rnd(4), s.pop(j - 1))
        else:
            continue
        if seq["act"][:len(lead)] != lead:
            seq, on, bank = old
            continue
        new = evaluate()
        if new is not None and new[0] <= cur[0] + P["slack"] * (1.0 - it / P["moves"]) * rnd(100) / 100.0:
            cur = new
            if cur[0] < best[0]:
                best, keep = cur, (seq, on, bank)
        else:
            seq, on, bank = old
    FAR["end"] = best[0] / len(sets)
    return {"seq": keep[0], "on": keep[1], "bank": keep[2], "start": best[2], "heads": heads, "tails": tails}


def plan_for(ops, P):
    if "plan" not in FAR:
        FAR["plan"] = polish(ops, rough(ops, P), P)
    plan = FAR["plan"]
    units = [o["unit"] for o in ops if o["unit"] is not None and o["unit"]["ops"][0] is o]
    for o in ops:
        o["on"], o["start"], o["bdeps"] = plan["on"][o["n"]], plan["start"][o["n"]], []
    for k, b in plan["bank"].items():
        for i, u in enumerate(b):
            units[u]["bank"] = k
            for h in plan["heads"][u]:
                ops[h]["bdeps"] = [ops[x] for x in plan["tails"][b[i - 1]]] if i else []
    order = FAR["o"] = {e: [ops[i] for i in s] for e, s in plan["seq"].items()}
    FAR["order"] = [o["msg"] for o in order["gp"] if "msg" in o]
    return order


def emit_all(g, T, Q, order, sent):
    for e in order:
        k = 0
        for o in order[e]:
            if o["kind"] == "c":
                k += 1
                o["sem"] = (e, k)
    seen = {e: {} for e in order}
    top = {}
    for o in [o for e in order for o in order[e]]:
        e = o["on"]
        need = {}
        for d in [d for d in o["deps"] if not any(d is x for x in o.get("free", ()))] + o["bdeps"]:
            s, v = d["sem"]
            need[s] = max(need.get(s, 0), v)
        for s in need:
            if seen[e].get(s, 0) < need[s]:
                Q[e].wait_ge(T.sem[s], need[s])
                seen[e][s] = need[s]
        ins = o["emit"](e)
        if o["kind"] == "c":
            ins.then_inc(T.sem[e], 1)
        if o["sem"] is not None:
            top[o["sem"][0]] = max(top.get(o["sem"][0], 0), o["sem"][1])
    top["sent"] = sent[0]
    for s in top:
        g.wait_ge(T.sem[s], top[s])


def rank_program(g, core, T, topo):
    r = T.rank_of(core)
    if r is not None:
        ops, Q, sent = build(g, T, topo, r, PAR)
        emit_all(g, T, Q, plan_for(ops, PAR), sent)
        return
    cores, slots, relay = wiring(T, topo)
    for (s, d), k in relay.items():
        if k != core:
            continue
        if "order" not in FAR:
            plan_for(build(g, T, topo, s, PAR)[0], PAR)
        msg = messages(T, slots[d].index(s))
        got = len(topo.engines(cores[s], core)) // 2
        rid, pid = topo.addr(cores[d], core)
        tot = 0
        for key in FAR["order"]:
            sem, ap = msg[key]
            g.wait_ge(T.sem[sem], got)
            g.remote_dma(ap, ap, T.sem[sem], T.sem.sent, pid, rid, topo.mask(core, cores[d]))
            tot += len(topo.engines(core, cores[d]))
        g.wait_ge(T.sem.sent, tot)
